import numpy as np, ml_dtypes
CORES = [25,29,65,69,153,157,193,197]
N = 8
BF = ml_dtypes.bfloat16
W, U, SH, B, T, DEL, LIM = 2560, 320, 3, 256, 8, 3, 16
def parts(rng):
    return (rng.integers(0, 64, (N, 8, 16, W)), rng.integers(0, W, (N, 8, 16, U)), rng.integers(0, W, (N, 8, 16, B)), rng.integers(0, W, (N, 8, B)), rng.integers(0, 64, (N, 8, 16, B)))
def pack(x, canal, trail, cut, z):
    return {"x": x.reshape(N, 128, W).astype(np.float32).astype(BF), "canal": np.ascontiguousarray(canal.reshape(N, 128, U)).astype(np.int32), "trail": np.ascontiguousarray(trail.reshape(N, 128, B)).astype(np.int32),
            "cut": np.ascontiguousarray(cut).astype(np.int32), "z": z.reshape(N, 128, B).astype(np.float32).astype(BF)}
def setup_inputs(rng):
    return pack(*parts(rng))
def setup_inputs_spread(rng):
    def low(*shape): return np.minimum((W * rng.random(shape) ** 3).astype(np.int64), W - 1)
    def size(n): return np.minimum((64.0 ** rng.random((N, 8, 1, n)) * rng.random((N, 8, 16, n))).astype(np.int64), 63)
    return pack(size(W), low(N, 8, 16, U), low(N, 8, 16, B), low(N, 8, B), size(B))
def tips(rng, *shape):
    q = rng.random(shape)
    return np.where(q < 0.36, 0, np.where(q < 0.72, W - 1, rng.integers(0, W, shape)))
def setup_inputs_ends(rng):
    k = rng.random((N, 8, 1, W)); x = np.where(k < 0.2, 0, np.where(k < 0.4, 63, 63 * rng.integers(0, 2, (N, 8, 16, W))))
    one = (np.arange(16).reshape(1, 1, 16, 1) == rng.integers(0, 16, (N, 8, 1, W))) & (rng.random((N, 8, 1, W)) < 0.15)
    x = np.where(one, np.where(x == 63, 62, 1), x)
    for q in (1, N - 1): x[q] = np.where(rng.random((8, 1, W)) < 0.3, 32 + LIM + rng.integers(0, 3, (8, 1, W)), x[q])
    k = rng.random((N, 8, 1, B)); z = np.where(k < 0.3, 0, np.where(k < 0.45, 63, 63 * rng.integers(0, 2, (N, 8, 16, B))))
    for q in (0, 1, N - 1): z[q] = np.repeat(63 * rng.integers(0, 2, (8, 1, B)), 16, axis=1)
    z[:, :, :, B - 1] = 0
    canal, trail, cut = tips(rng, N, 8, 16, U), tips(rng, N, 8, 16, B), tips(rng, N, 8, B); cut[:, :, B - 1] = W - 1
    for r in range(N):
        for g in range(8):
            a = 2 * int(rng.integers(W // 8, W // 4)); b = a - 1; rows = rng.permutation(15)[:2]
            x[r, g, :, 0] = 0 if r in (0, 1, N - 1) else 63 * ((r + g) % 2)
            x[r, g, :, W - 1] = 63; x[r, g, :, a] = 63; x[r, g, :, b] = 63; x[r, g, int(rng.integers(0, 16)), b] = 62
            canal[r, g, :, U - 1] = W - 1; canal[r, g, rows[0], U - 1] = a; canal[r, g, rows[1], U - 1] = b
    w = 16 - DEL
    for q in (1, N - 1): trail[q, :, w] = np.where(z[q, :, 0] == 0, W - 1, 0)
    trail[1, 0, w, 0] = W - 1 - trail[1, 0, w, 0]
    trail[0, :, w] = np.where(z[0, :, 0] == 0, 0, W - 1)
    for q in range(2, N - 1):
        trail[q, 7, w] = np.where((trail[q, 7, w] >> SH) == U - 1, 0, trail[q, 7, w]); trail[q, 7, w, B - 1] = W - 1
    return pack(x, canal, trail, cut, z)
def setup_inputs_corners(rng):
    x, canal, trail, cut, z = parts(rng); s = int(rng.integers(0, 8)); H = 1 << SH
    for r in range(N):
        for g in range(8):
            kind = (r + g + s) % 8
            if kind == 0: cut[r, g] = (0, W - 1, int(rng.integers(0, W)))[r % 3]
            if kind == 1:
                u = rng.integers(0, U, (16, 1)); u[16 - DEL] = U - 1; u[17 - DEL if DEL > 1 else 0] = 0
                trail[r, g] = (u << SH) + rng.integers(0, H, (16, B))
            if kind == 2: trail[r, g] = (np.argsort(rng.random((16, U)), axis=1)[:, :B] << SH) + rng.integers(0, H, (16, B))
            if kind == 3:
                canal[r, g] = (np.arange(U)[None, :] << SH) + rng.integers(0, H, (16, U))
                cut[r, g] = rng.permutation(W)[:B]; trail[r, g] = cut[r, g][None, :]
            if kind == 4: x[r, g] = 30 + rng.integers(0, 4, (16, W)); z[r, g] = 30 + rng.integers(0, 4, (16, B))
            if kind == 5: x[r, g] = rng.integers(0, 4, (16, W)); z[r, g] = rng.integers(60, 64, (16, B))
            if kind == 6:
                at = np.argsort(rng.random((16, W)), axis=0); n = rng.integers(8, 10, (1, W)); sg = 2 * rng.integers(0, 2, (16, W)) - 1
                x[r, g] = 24 + sg * np.where(at < n, LIM + 1, LIM); z[r, g] = 24
            if kind == 7:
                x[r, g] = rng.integers(60, 64, (16, 4))[:, rng.integers(0, 4, W)]
                canal[r, g] = -np.sort(-canal[r, g], axis=0); canal[r, g, :, ::5] = canal[r, g, :1, ::5]
    return pack(x, canal, trail, cut, z)
def setup_inputs_full(rng):
    x, canal, trail, cut, z = parts(rng); w = 16 - DEL; w1 = (17 - DEL) % 16; H = 1 << SH; q = B // 4
    for r in range(N):
        for g in range(8):
            v = rng.integers(0, 64, W); y = np.full(B, 16); l = canal[r, g]; h = trail[r, g]
            if r == 0:
                h[w] = (rng.permutation(U)[:B] << SH) + rng.integers(0, H, B); v[h[w]] = rng.integers(40, 59, B)
            elif r == 1:
                o = rng.permutation(W - H); best = o[:B]; low = o[B:]
                v = rng.integers(0, 21, W); v[best] = rng.integers(25, 33, B)
                u = rng.permutation(U)[:B]; cut[r, g] = (u << SH) + rng.integers(0, H, B)
                l[:] = low[rng.integers(0, len(low), (16, U))]; l[rng.integers(0, 16, B), u] = best
                h[:] = rng.integers(0, W - H, (16, B))
                h[w, :B - 1] = (rng.permutation(U - 1)[:B - 1] << SH) + rng.integers(0, H, B - 1); h[w, B - 1] = W - 1
            elif r == 2:
                a = np.flatnonzero((v >= 16) & (v <= 32)); h[w] = a[rng.integers(0, len(a), B)]; h[w1] = a[rng.integers(0, len(a), B)]
                if g in (0, 3, 7):
                    far = np.flatnonzero(v >= 40); i = 0 if g == 0 else B - 1 if g == 7 else int(rng.integers(0, B))
                    h[w, i] = far[int(rng.integers(0, len(far)))]
            else:
                v = rng.integers(0, 63, W); v[0] = 63; v[W - 1] = 63
                y = rng.integers(0, 64, B); i = rng.permutation(B); u = rng.permutation(U - 1)[:2 * q]
                y[i[:q]] = 63; y[i[q:2 * q]] = 0; cut[r, g, i[:2 * q]] = (u << SH) + rng.integers(0, H, 2 * q)
                l[:, u[:q]] = W - 1; l[:, u[q:]] = rng.integers(1, W - 1, (16, q))
                l[rng.integers(0, 2, q), u[q:]] = 0; l[rng.integers(13, 16, q), u[q:]] = W - 1
            x[r, g] = v; z[r, g] = y
            if r > 2: x[r, g, int(rng.integers(0, 16)), 0] = 62
    return pack(x, canal, trail, cut, z)
def setup_inputs_meet(rng):
    x, canal, trail, cut, z = parts(rng)
    for r in range(N):
        for g in range(8):
            s = rng.permutation(W)[:64]; s[0] = W - 1
            canal[r, g] = s[rng.integers(0, 64, (16, U))]; trail[r, g] = s[rng.integers(0, 64, (16, B))]; cut[r, g] = s[rng.integers(0, 64, B)]
    return pack(x, canal, trail, cut, z)
def check_inputs(d):
    bad = []
    for k, hi in (("x", 63), ("canal", W - 1), ("trail", W - 1), ("cut", W - 1), ("z", 63)):
        a = np.asarray(d[k]).astype(np.float64)
        if not (np.min(a) >= 0 and np.max(a) <= hi): bad.append("range of " + k)
        if not np.all(a == np.floor(a)): bad.append("whole numbers in " + k)
    return bad
def reference(x, canal, trail, cut, z):
    X = x.astype(np.float32).astype(np.int64).reshape(N, 8, 16, W); C = canal.astype(np.int64).reshape(N, 8, 16, U); G = trail.astype(np.int64).reshape(N, 8, 16, B)
    V = cut.astype(np.int64).reshape(N, 8, B); Z = z.astype(np.float32).astype(np.int64).reshape(N, 8, 16, B); skips = np.zeros(N, np.int64)
    for t in range(T):
        lim = LIM + (skips & 3); skips = np.zeros(N, np.int64); come = np.zeros_like(Z); row = (t + 16 - DEL) % 16
        for r in range(N):
            for g in range(8):
                a, l, h, q = X[r, g], C[r, g], G[r, g], Z[r, g]
                k = l[:, V[r, g] >> SH]
                score = np.add.reduce(np.maximum(a[:, k] - q[:, None, :], 0), axis=0)
                c = np.min(np.where(score == np.max(score, axis=0), k, W), axis=0)
                cut_off = np.sum(np.abs(a[:, h] - q[:, None, :]) > lim[r], axis=0) >= 9
                w = h[row] + 0; skip = cut_off[row]; xw = a[:, w]; xc = a[:, c]
                first = np.zeros(B, bool); first[np.unique(w >> SH, return_index=True)[1]] = True
                new = np.where(skip, np.minimum(xw + 4, 63), (xw + q) >> 1)
                a[:, w[first]] = new[:, first]
                m = first & ~skip; u = w[m] >> SH
                l[:, u] = np.where(cut_off[:, m], l[:, u], h[:, m])
                h[:] = np.where(cut_off, k, h); h[t] = c
                a[:, c] = xc >> 1
                V[r, g] = c; skips[r] += np.sum(skip)
                come[(r + 1 + t % (N - 1)) % N, g] = (q + xc) >> 1
        Z = come
    return {"yx": X.reshape(N, 128, W).astype(np.float32).astype(BF), "yl": C.reshape(N, 128, U).astype(np.float32), "yg": G.reshape(N, 128, B).astype(np.float32)}

@@ -1,0 +1,675 @@
+import math
+from concourse.mybir import AluOpType as OP, ActivationFunctionType as AF
+
+NC, NU, B, STEPS, CEN = 2560, 320, 256, 8, 1280
+BIG = 4096.0
+LN = math.log(1.75)
+BY_ACT = (0, 1, 2)
+ORDER = "AABBBABA"
+NET = 7.0
+PEC = 0.0006
+SMALL = 0.3
+GAT, SCA, CY = 1.5, 3.0, 0.001
+BK = {"zn": "b0", "dup": "b1", "skip": "b6"}
+
+BUFS = {
+    "bfloat16": "xs 2816 xraw 2560 zraw 256 zland 1792 zn 1792 relay 1792 zr 2048 D 4096 AB 4096 SG 4096 E 4096 R 4096 SM 256 NM 256 SW 256 "
+                "NW 256 PB 256 XM 256 XW 256 xc 256 xh 256 EQ 240 G12 512 LOH 576 Fs 160 Pf 256 skb 16 W 144 Ib 128 Ihalf 128 Ineg 128 "
+                "Im1 128 BD 128 one 128 four 256 TRI 240 T12 640 R2 160 xo 2560",
+    "float16": "can16 320 tr16 256 cut16 256 GV 1024 KN 512 TRK 1024 c16 16 Ih 128 Imh 128 Y 144 X 512 Xs 512 PS 256 ZW 144 trO 256 uh 16 hh 16 vh 16",
+    "float32": "can 576 BS 512 VN 256 kS 128 k1 128 k2 64 k3 32 km 16 kd 16 cF 16 dd 16 wuF 64 ssj 16 sc 1 lc 2 M2 32 M3 32 M4 32 ioF 320 "
+               "pc 24 tF 320 tG 320 tH 320 DUMP 32 iL 16 THR 16 swa 2 swt 2 outF 320 outG 256",
+    "int32": "canI 320 trI 256 cutI 256 kr 16 cdI 16 scI 1 sdI 1 ioI 320 pI 1 qI 4 tI 320 tI2 320",
+    "uint16": "GL 512 KL 256 cl 16 vuL 96 cdl 32 hl 16 wcl 32",
+}
+SCRATCH = {"b%d" % i: ("psum", [128, 512], "float32") for i in range(8)}
+for _dt, _s in BUFS.items():
+    _l = _s.split()
+    for _i in range(0, len(_l), 2):
+        SCRATCH[_l[_i]] = ("sbuf", [128, int(_l[_i + 1])], _dt)
+SEMAPHORES = ["sv", "sa", "sp", "sg", "zl"] + ["z%d" % t for t in range(7)] + ["r%d" % t for t in range(7)] + ["d%d" % i for i in range(9)]
+
+
+def col(i):
+    return ("pc", i, i + 1, 1)
+
+
+def c(name, lo, hi, st=1):
+    return (name, lo, hi, st)
+
+
+def ap(T, a):
+    t = T[a[0]]
+    if len(a) == 5:
+        return t[0:a[4], a[1]:a[2]:a[3]] if a[3] > 1 else t[0:a[4], a[1]:a[2]]
+    return t[:, a[1]:a[2]:a[3]] if a[3] > 1 else t[:, a[1]:a[2]]
+
+
+def width(a):
+    return (a[2] - a[1] + a[3] - 1) // a[3]
+
+
+def half(a):
+    return SCRATCH[a[0]][2] in ("bfloat16", "float16", "uint16")
+
+
+def add(p, q, fn, reads, writes, cost, dsem=None, tag=""):
+    i = len(p["ops"])
+    deps = {}
+    for lst, wr in ((reads, False), (writes, True)):
+        for a in lst:
+            name, lo, hi, st = a[:4]
+            psum = SCRATCH[name][0] == "psum"
+            keep = []
+            for e in p["acc"].setdefault(name, []):
+                j, l2, h2, s2, w2 = e
+                qj = p["ops"][j]["q"] if j < i else q
+                apart = h2 <= lo or hi <= l2 or (st == s2 and (lo - l2) % st)
+                conf = j < i and ((not apart and (wr or w2)) or (psum and qj != q))
+                if conf:
+                    deps[j] = deps.get(j, False) or qj != q or q != "p"
+                if not (conf and wr and lo <= l2 and h2 <= hi and st in (1, s2) and (not psum or qj == q)):
+                    keep.append(e)
+            keep.append((i, lo, hi, st, wr))
+            p["acc"][name] = keep
+    p["ops"].append({"q": q, "fn": fn, "deps": deps, "cost": cost, "ext": None, "dsem": dsem, "tag": tag})
+    return i
+
+
+def ts(p, out, in0, s1, op0, s2=None, op1=None, tag=""):
+    def fn(g, T):
+        a1 = ap(T, s1) if isinstance(s1, tuple) else s1
+        a2 = ap(T, s2) if isinstance(s2, tuple) else s2
+        if op1 is None:
+            return g.vector.tensor_scalar(ap(T, out), ap(T, in0), a1, None, op0)
+        return g.vector.tensor_scalar(ap(T, out), ap(T, in0), a1, a2, op0, op1)
+    f = 0.5 if half(out) and half(in0) else 1.0
+    return add(p, "v", fn, [in0] + [s for s in (s1, s2) if isinstance(s, tuple)], [out], 0.01 + max(64, width(out) * f) * CY, tag=tag)
+
+
+def tt(p, out, in0, in1, op, tag=""):
+    f = 1 if SCRATCH[in0[0]][0] == "psum" or SCRATCH[in1[0]][0] == "psum" else 2
+    return add(p, "v", lambda g, T: g.vector.tensor_tensor(ap(T, out), ap(T, in0), ap(T, in1), op), [in0, in1], [out], 0.01 + max(64, width(out) * f) * CY, tag=tag)
+
+
+def cp(p, out, in0, tag=""):
+    f = 0.5 if half(out) and half(in0) else 1.0
+    return add(p, "v", lambda g, T: g.vector.tensor_copy(ap(T, out), ap(T, in0)), [in0], [out], 0.01 + max(64, width(out) * f) * CY, tag=tag)
+
+
+def memset(p, out, val):
+    return add(p, "v", lambda g, T: g.vector.memset(ap(T, out), val), [], [out], 0.01 + max(64, width(out)) * CY)
+
+
+def gtt(p, out, win, offs, in1, op, tag=""):
+    return add(p, "v", lambda g, T: g.vector.tensor_tensor(ap(T, out), ap(T, win).indirect(ap(T, offs)), ap(T, in1), op), [win, offs, in1], [out], 0.05 + width(out) * GAT * CY, tag=tag)
+
+
+def gcp(p, out, win, offs, tag=""):
+    return add(p, "v", lambda g, T: g.vector.tensor_copy(ap(T, out), ap(T, win).indirect(ap(T, offs))), [win, offs], [out], 0.05 + width(out) * GAT * CY, tag=tag)
+
+
+def scat(p, win, offs, in0, tag=""):
+    return add(p, "v", lambda g, T: g.vector.tensor_copy(ap(T, win).indirect(ap(T, offs)), ap(T, in0)), [offs, in0], [win], 0.05 + width(in0) * SCA * CY, tag=tag)
+
+
+def vtr(p, out, in0, tag=""):
+    return add(p, "v", lambda g, T: g.vector.transpose(ap(T, out), ap(T, in0)), [in0], [out], 0.01 + 64 * CY, tag=tag)
+
+
+def act(p, out, in0, func, bias=None, scale=None, accum=None, offs=None, tag=""):
+    def fn(g, T):
+        kw = {}
+        if bias is not None:
+            kw["bias"] = ap(T, bias) if isinstance(bias, tuple) else bias
+        if scale is not None:
+            kw["scale"] = ap(T, scale) if isinstance(scale, tuple) else scale
+        if accum is not None:
+            kw["accum_out"] = ap(T, accum)
+        src = ap(T, in0) if offs is None else ap(T, in0).indirect(ap(T, offs))
+        return g.scalar.activation(ap(T, out), src, func, **kw)
+    return add(p, "a", fn, [in0] + [s for s in (bias, scale, offs) if isinstance(s, tuple)], [out] + ([accum] if accum else []), 0.065 + width(out) * (GAT if offs else 1.0) * CY, tag=tag)
+
+
+def mm(p, out, lhsT, rhs, start, stop):
+    i = add(p, "p", lambda g, T: g.tensor.matmul(ap(T, out), ap(T, lhsT), ap(T, rhs), start, stop), [lhsT, rhs], [out], max(min(64, width(lhsT)), width(out)) * PEC)
+    if out[0] in p["bank"]:
+        p["ops"][i]["deps"].setdefault(p["bank"][out[0]], False)
+    p["bank"][out[0]] = i
+    return i
+
+
+def iota(p, out, pattern, base, chan):
+    return add(p, "g", lambda g, T: g.iota(ap(T, out), pattern, base, chan), [], [out], 0.13 + width(out) * 2 * CY)
+
+
+def dma(p, out, in0, k, lo=None, hi=None):
+    def fn(g, T):
+        o = ap(T, out) if isinstance(out, tuple) else T[out][:] if lo is None else T[out][:, lo:hi]
+        i = ap(T, in0) if isinstance(in0, tuple) else T[in0][:] if lo is None else T[in0][:, lo:hi]
+        return g.sync.dma_start(o, i)
+    return add(p, "sync", fn, [a for a in (in0,) if isinstance(a, tuple)], [a for a in (out,) if isinstance(a, tuple)], 2.5, dsem="d%d" % k)
+
+
+P_, PM, PG, W0, P16, M0, M1, M2C, M0X2, NM1, C20, DC, MB0, MB1, TG, PP, PI, TMP, PZ = range(19)
+
+
+def constants(p):
+    iota(p, c("pI", 0, 1), [[1, 1]], 0, 1)
+    iota(p, c("ioI", 0, 320), [[1, 320]], 0, 0)
+    ts(p, c("qI", 0, 1), c("pI", 0, 1), 15, OP.bitwise_and)
+    ts(p, c("qI", 1, 2), c("pI", 0, 1), 4, OP.logical_shift_right)
+    ts(p, c("qI", 2, 3), c("qI", 1, 2), 1, OP.bitwise_and)
+    cp(p, col(P_), c("pI", 0, 1))
+    cp(p, col(PM), c("qI", 0, 1))
+    cp(p, col(PG), c("qI", 1, 2))
+    cp(p, col(MB1), c("qI", 2, 3))
+    ts(p, col(MB0), col(MB1), -1.0, OP.mult, 1.0, OP.add)
+    ts(p, col(W0), col(PG), 16.0, OP.mult, 15.0, OP.add)
+    ts(p, col(P16), col(P_), 16.0, OP.add)
+    for k, dst in ((0, M0), (1, M1), (2, M2C)):
+        ts(p, col(dst), col(PM), float(k), OP.is_equal)
+    ts(p, col(M0X2), col(M0), 2.0, OP.mult)
+    ts(p, col(NM1), col(M1), -1.0, OP.mult)
+    ts(p, col(C20), col(PG), 20.0, OP.mult)
+    ts(p, col(DC), col(PM), float(NC), OP.add)
+    ts(p, col(PZ), col(P_), 16.0, OP.mult, 15.0, OP.add)
+    cp(p, c("ioF", 0, 320), c("ioI", 0, 320))
+    io, io144 = c("ioF", 0, 128), c("ioF", 0, 144)
+    ts(p, col(TMP), col(PM), 13.0, OP.is_ge, -16.0, OP.mult)
+    ts(p, col(PP), col(P_), col(TMP), OP.add, 3.0, OP.add)
+    ts(p, col(TMP), col(PM), 3.0, OP.is_lt, 16.0, OP.mult)
+    ts(p, col(PI), col(P_), col(TMP), OP.add, -3.0, OP.add)
+    ts(p, c("PS", 0, 128), io, col(PP), OP.is_equal)
+    ts(p, c("PS", 128, 256), io, col(PI), OP.is_equal)
+    for s in (0, 1):
+        for d in (0, 1):
+            ts(p, col(TG), col(P_), 16.0 * (d - s) + 1.0, OP.add, col(MB1 if s else MB0), OP.mult)
+            ts(p, col(TMP), col(TG), -1.0, OP.add)
+            k = 128 * (2 * s + d)
+            ts(p, c("X", k, k + 128), io, col(TMP), OP.is_equal)
+    ts(p, c("Xs", 0, 512), c("X", 0, 512), -1.0 / 4096.0, OP.mult)
+    ts(p, c("ZW", 0, 144), io144, col(PZ), OP.is_equal)
+    ts(p, c("Ih", 0, 128), io, col(P_), OP.is_equal)
+    ts(p, c("Imh", 0, 128), io, col(P_), OP.is_equal, -1.0, OP.mult)
+    ts(p, c("W", 0, 144), io144, col(W0), OP.is_equal)
+    ts(p, c("Ib", 0, 128), io, col(P_), OP.is_equal)
+    act(p, c("Ihalf", 0, 128), c("Ib", 0, 128), AF.Copy, scale=0.5)
+    act(p, c("Ineg", 0, 128), c("Ib", 0, 128), AF.Copy, scale=-BIG)
+    act(p, c("Im1", 0, 128), c("Ib", 0, 128), AF.Copy, scale=-1.0)
+    ts(p, c("Y", 0, 144), io144, col(P16), OP.is_equal)
+    ts(p, c("tI", 0, 320), c("ioI", 0, 320), 4, OP.logical_shift_right)
+    ts(p, c("tI2", 0, 320), c("ioI", 0, 320), 15, OP.bitwise_and)
+    ts(p, c("BD", 0, 128), c("tI", 0, 128), col(PG), OP.is_equal)
+    ts(p, c("T12", 0, 320), c("tI2", 0, 320), col(PM), OP.is_equal)
+    ts(p, c("tF", 0, 320), c("tI", 0, 320), -10.0, OP.add)
+    tt(p, c("tG", 0, 320), c("tF", 0, 320), c("tF", 0, 320), OP.mult)
+    ts(p, c("tG", 0, 320), c("tG", 0, 320), col(M1), OP.mult, col(M2C), OP.add)
+    ts(p, c("tF", 0, 320), c("tF", 0, 320), col(M0), OP.mult)
+    tt(p, c("T12", 320, 640), c("tF", 0, 320), c("tG", 0, 320), OP.add)
+    iota(p, c("tI", 0, 160), [[0, 8], [1, 20]], -10, 0)
+    iota(p, c("tI2", 0, 160), [[1, 8], [0, 20]], 0, 0)
+    cp(p, c("tH", 0, 160), c("tI", 0, 160))
+    tt(p, c("tG", 0, 160), c("tH", 0, 160), c("tH", 0, 160), OP.mult)
+    ts(p, c("tF", 0, 160), c("tH", 0, 160), col(M0X2), OP.mult, col(NM1), OP.add)
+    ts(p, c("tG", 0, 160), c("tG", 0, 160), -1.0, OP.mult, 1.0, OP.add)
+    ts(p, c("tG", 0, 160), c("tG", 0, 160), col(M2C), OP.mult)
+    tt(p, c("tF", 0, 160), c("tF", 0, 160), c("tG", 0, 160), OP.add)
+    ts(p, c("tG", 0, 160), c("tI2", 0, 160), col(PG), OP.is_equal)
+    tt(p, c("R2", 0, 160), c("tF", 0, 160), c("tG", 0, 160), OP.mult)
+    iota(p, c("tI", 0, 240), [[1, 15], [0, 16]], 1, 0)
+    ts(p, c("TRI", 0, 240), c("tI", 0, 240), col(PM), OP.is_gt, 8192.0, OP.mult)
+    iota(p, c("tI2", 0, 16), [[16, 16]], 0, 0)
+    ts(p, c("iL", 0, 16), c("tI2", 0, 16), col(PM), OP.add)
+    ts(p, c("DUMP", 0, 16), c("iL", 0, 16), float(NC), OP.add)
+    ts(p, c("DUMP", 16, 32), c("iL", 0, 16), float(NU), OP.add)
+    ts(p, c("iL", 0, 16), c("iL", 0, 16), -LN, OP.mult, 128 * LN + math.log(2.5), OP.add)
+    act(p, c("THR", 0, 16), c("iL", 0, 16), AF.Exp)
+    for h in (0, 1):
+        ts(p, c("swa", h, h + 1), col(P_), -0.5 * LN, OP.mult, 0.5 * LN * (128 - 128 * h), OP.add)
+    act(p, c("swt", 0, 2), c("swa", 0, 2), AF.Exp)
+    memset(p, c("one", 0, 128), 1.0)
+    memset(p, c("four", 0, 256), 4.0)
+    memset(p, c("lc", 0, 1), -16.5)
+
+
+def X(s, d, name="X"):
+    return c(name, 128 * (2 * s + d), 128 * (2 * s + d) + 128)
+
+
+def lists_of_w(p, t):
+    pa = t & 1
+    v = 48 * pa
+    src = c("GV", 512 * pa + 16 * t, 512 * pa + 16 * t + 16)
+    ts(p, c("uh", 0, 16), src, 0.125, OP.mult, 1536 + 160 - 0.4375, OP.add)
+    ts(p, c("hh", 0, 16), src, 1.0 / 128, OP.mult, 1536 + 10 - 63.5 / 128, OP.add)
+    ts(p, c("vuL", v + 16, v + 32), c("uh", 0, 16), -1536.0, OP.add)
+    ts(p, c("vuL", v + 32, v + 48), c("uh", 0, 16), NU - 1536.0, OP.add)
+    ts(p, c("hl", 0, 16), c("hh", 0, 16), -1536.0, OP.add, col(C20), OP.add)
+    ts(p, c("wuF", 32 * pa, 32 * pa + 16), src, float(CEN), OP.add)
+    ts(p, c("wuF", 32 * pa + 16, 32 * pa + 32), c("uh", 0, 16), -1536.0, OP.add)
+
+
+def first_lanes(p, t):
+    v = 48 * (t & 1)
+    act(p, c("G12", 0, 512), c("T12", 0, 640), AF.Copy, offs=c("vuL", v + 16, v + 48), tag="G12")
+    for h in (0, 1):
+        mm(p, c("b5", 0, 128), c("G12", 128 * h, 128 * h + 128), c("Ib", 0, 128), True, True)
+        mm(p, c("b5", 128, 288), c("G12", 256 + 128 * h, 256 + 128 * h + 128), c("R2", 0, 160), True, True)
+        act(p, c("LOH", 288 * h, 288 * h + 288), c("b5", 0, 288), AF.Relu, scale=c("swt", h, h + 1))
+    for h in (0, 1):
+        mm(p, c("b5", 288, 448), c("LOH", 288 * h, 288 * h + 128), c("LOH", 288 * h + 128, 288 * h + 288), h == 0, h == 1)
+    act(p, c("Fs", 0, 160), c("b5", 288, 448), AF.Copy)
+    gtt(p, c("Pf", 0, 256), c("Fs", 0, 160), c("hl", 0, 16), c("G12", 0, 256), OP.mult, tag="Pf")
+    for r in range(16):
+        mm(p, c("b5", 448, 464), c("W", 15 - r, 143 - r), c("Pf", r, 256, 16), r == 0, r == 15)
+    tt(p, c("M2", 0, 16), c("b5", 448, 464), c("THR", 0, 16), OP.is_gt, tag="nf")
+
+
+def turn(p, out, lo, k, lo2=0, n=128, start=True, name="X"):
+    for ql in (0, 1):
+        for par in (0, 1):
+            mm(p, c(out, lo + ql, lo + 2 * n, 2), X(ql, par, name), c("TRK", k + 128 * par + lo2, k + 128 * par + lo2 + n), start and par == 0, par == 1 and (ql == 1 or start))
+
+
+def canal_lists(p, t):
+    pa = t & 1
+    gcp(p, c("KN", 0, 512), c("can", 0, NU), c("vuL", 48 * pa, 48 * pa + 32), tag="KN")
+    for ty in (0, 1):
+        for b in range(8):
+            k = 512 * pa + 256 * ty
+            vtr(p, c("TRK", k + b, k + 256, 8), c("KN", 256 * ty + 32 * b, 256 * ty + 32 * b + 32), tag="trk")
+    turn(p, "b3", 0, 512 * pa)
+    ts(p, c("KL", 0, 256), c("b3", 0, 256), float(CEN), OP.add, tag="KL")
+
+
+def to_rows(p, src, lo):
+    for par in (0, 1):
+        for h in (0, 1):
+            for ql in (0, 1):
+                a, o = lo + 256 * h, 256 + 128 * par + 64 * h
+                mm(p, c("b3", o, o + 64), X(par, ql), c(src, a + ql, a + 128, 2), ql == 0, ql == 1)
+    for b in range(8):
+        vtr(p, c("VN", 32 * b, 32 * b + 32), c("b3", 256 + b, 512, 8), tag="trv")
+
+
+def sums(p, bank, o, src, a, stop=True):
+    for r in range(16):
+        mm(p, c(bank, o, o + 64), c("W", 15 - r, 143 - r), c(src, a + r, a + 1024, 16), r == 0, r == 15 and stop)
+
+
+def trail_chunk(p, t, j):
+    pa = t & 1
+    a, e = 1024 * j, 1024 * j + 1024
+    offs = c("GL", 256 * pa + 64 * j, 256 * pa + 64 * j + 64)
+    if j in BY_ACT:
+        act(p, c("R", a, e), c("xs", 0, NC), AF.Copy, offs=offs, tag="R%d" % j)
+        for k in (0, 1):
+            bank = "b6" if k == 0 else "b7"
+            mm(p, c(bank, 0, 512), c("Ib", 0, 128), c("R", a + 512 * k, a + 512 * k + 512), True, False)
+            mm(p, c(bank, 0, 512), c("Im1", 0, 128), c("zr", 1024 * pa, 1024 * pa + 512), False, True)
+            act(p, c("AB", a + 512 * k, a + 512 * k + 512), c(bank, 0, 512), AF.Abs, tag="abs")
+    else:
+        gtt(p, c("D", a, e), c("xs", 0, NC), offs, c("zr", 1024 * pa, 1024 * pa + 1024), OP.subtract, tag="A%d" % j)
+        act(p, c("AB", a, e), c("D", a, e), AF.Abs, tag="abs")
+    act(p, c("SG", a, e), c("AB", a, e), AF.Sign, bias=c("lc", pa, pa + 1), tag="sign")
+    sums(p, "b0" if j < 2 else "b1", 64 * (j & 1), "SG", a)
+
+
+def score_chunk(p, t, j):
+    pa = t & 1
+    gtt(p, c("E", 1024 * j, 1024 * j + 1024), c("xs", 0, NC), c("KL", 64 * j, 64 * j + 64), c("zr", 1024 * pa, 1024 * pa + 1024), OP.max, tag="B%d" % j)
+    sums(p, "b2", 64 * j, "E", 1024 * j, False)
+    turn(p, "b2", 64 * j, 512 * pa, 32 * j, 32, False, "Xs")
+
+
+def blend(p, t, h):
+    pa, nx = t & 1, 1 - (t & 1)
+    bank, s = "b%d" % h, 128 * h
+    act(p, c("SM", s, s + 128), c(bank, 0, 128), AF.Relu, tag="SM")
+    act(p, c("NM", s, s + 128), c(bank, 0, 128), AF.Relu, bias=2.0, scale=-1.0)
+    g0, g1 = 512 * pa + 256 * h, 512 * nx + 256 * h
+    for ty in (0, 1):
+        o = 128 * ty
+        mm(p, c("b4", o, o + 128), c("Ih", 0, 128), c("GV", g0, g0 + 128), True, False)
+        mm(p, c("b4", o, o + 128), c("Ineg", 0, 128), c("SM", s, s + 128), False, True)
+        mm(p, c("b4", o + 256, o + 384), c("Ineg", 0, 128), c("NM", s, s + 128), True, False)
+        turn(p, "b4", o + 256, 512 * pa + 256 * ty, 64 * h, 64, False)
+    act(p, c("BS", 256 * h, 256 * h + 256), c("b4", 256, 512), AF.Copy)
+    tt(p, c("GV", g1, g1 + 256), c("b4", 0, 256), c("BS", 256 * h, 256 * h + 256), OP.max, tag="blend")
+    ts(p, c("GL", 256 * nx + s, 256 * nx + s + 128), c("GV", g1, g1 + 128), float(CEN), OP.add, tag="GL")
+
+
+def replay_value(p, t):
+    pa = t & 1
+    raw = t // 4 in BY_ACT
+    d = c("R" if raw else "D", 256 * t, 256 * t + 256)
+    z, I = c("zr", 1024 * pa, 1024 * pa + 256), c("Ib", 0, 128)
+    n = c(BK["skip"], 0, 256)
+    mm(p, n, c("BD", 0, 128), c("SG", 256 * t, 256 * t + 256), True, True)
+    act(p, c("SW", 0, 256), n, AF.Relu)
+    act(p, c("NW", 0, 256), n, AF.Relu, bias=2.0, scale=-1.0)
+    lo, hi = c("b7", 0, 256), c("b7", 256, 512)
+    mm(p, lo, c("Ihalf", 0, 128), d, True, False)
+    mm(p, lo, c("Ihalf", 0, 128) if raw else I, z, False, False)
+    mm(p, lo, c("Ineg", 0, 128), c("SW", 0, 256), False, True)
+    mm(p, hi, I, d, True, False)
+    if not raw:
+        mm(p, hi, I, z, False, False)
+    mm(p, hi, I, c("four", 0, 256), False, False)
+    mm(p, hi, c("Ineg", 0, 128), c("NW", 0, 256), False, True)
+    act(p, c("PB", 0, 256), lo, AF.Identity, bias=-0.25)
+    tt(p, c("XM", 0, 256), hi, c("PB", 0, 256), OP.max, tag="xm")
+    ts(p, c("XW", 0, 256), c("XM", 0, 256), 191.0, OP.min)
+
+
+def write_lists(p, t):
+    pa = t & 1
+    ts(p, c("skb", 0, 16), c("SM", 16 * t, 16 * t + 16), 0.5, OP.is_gt)
+    if t < STEPS - 1:
+        mm(p, c("b5", 464, 480), c("one", 0, 128), c("skb", 0, 16), True, True)
+        act(p, c("ssj", 0, 16), c("b5", 464, 480), AF.Copy, accum=c("sc", 0, 1))
+        cp(p, c("scI", 0, 1), c("sc", 0, 1))
+        ts(p, c("sdI", 0, 1), c("scI", 0, 1), 3, OP.bitwise_and)
+        ts(p, c("lc", 1 - pa, 2 - pa), c("sdI", 0, 1), -1.0, OP.mult, -16.5, OP.add)
+    tt(p, c("M2", 16, 32), c("M2", 0, 16), c("skb", 0, 16), OP.max)
+    tt(p, c("M3", 0, 32), c("M2", 0, 32), c("DUMP", 0, 32), OP.mult)
+    tt(p, c("M4", 0, 32), c("M3", 0, 32), c("wuF", 32 * pa, 32 * pa + 32), OP.max)
+    cp(p, c("wcl", 0, 32), c("M4", 0, 32))
+
+
+def cut_choice(p, t):
+    nx = 1 - (t & 1)
+    act(p, c("kS", 0, 128), c("b2", 128, 256), AF.Copy)
+    tt(p, c("k1", 0, 128), c("b2", 0, 128), c("kS", 0, 128), OP.max, tag="k1")
+    tt(p, c("k2", 0, 64), c("k1", 0, 64), c("k1", 64, 128), OP.max)
+    tt(p, c("k3", 0, 32), c("k2", 0, 32), c("k2", 32, 64), OP.max)
+    tt(p, c("km", 0, 16), c("k3", 0, 16), c("k3", 16, 32), OP.max)
+    cp(p, c("kr", 0, 16), c("km", 0, 16))
+    tt(p, c("kd", 0, 16), c("kr", 0, 16), c("km", 0, 16), OP.subtract)
+    ts(p, c("cl", 0, 16), c("kd", 0, 16), 4096.0, OP.mult, float(CEN), OP.add, tag="cl")
+    ts(p, c("c16", 0, 16), c("kd", 0, 16), 4096.0, OP.mult)
+    act(p, c("cF", 0, 16), c("kd", 0, 16), AF.Identity, bias=float(CEN), scale=4096.0)
+    if t < STEPS - 1:
+        ts(p, c("vh", 0, 16), c("kd", 0, 16), 512.0, OP.mult, 1536 + 160 - 0.4375, OP.add)
+        ts(p, c("vuL", 48 * nx, 48 * nx + 16), c("vh", 0, 16), -1536.0, OP.add)
+
+
+def gauge(p, t):
+    pa = t & 1
+    act(p, c("xc", 0, 256), c("xs", 0, NC), AF.Copy, offs=c("cl", 0, 16), tag="xc")
+    if t < STEPS - 1:
+        zt, n = c("zn", 256 * t, 256 * t + 256), c(BK["zn"], 128, 384)
+        mm(p, n, c("Ib", 0, 128), c("xc", 0, 256), True, False)
+        mm(p, n, c("Ib", 0, 128), c("zr", 1024 * pa, 1024 * pa + 256), False, True)
+        act(p, zt, n, AF.Identity, bias=-0.25, scale=0.5, tag="zn")
+        add(p, "g", ("send", t), [zt], [], 0.1)
+        add(p, "net", ("net", t), [zt], [c("zland", 256 * t, 256 * t + 256)], NET)
+        for k in range(4):
+            o = 1024 * (1 - pa) + 256 * k
+            i = cp(p, c("zr", o, o + 256), c("zland", 256 * t, 256 * t + 256), tag="zr")
+            p["ops"][i]["ext"] = t
+    act(p, c("xh", 0, 256), c("xc", 0, 256), AF.Identity, bias=63.75, scale=0.5)
+
+
+def cut_lists(p, t):
+    bk = BK["dup"]
+    mm(p, c(bk, 128, 368), c("Ib", 0, 128), c("TRI", 0, 240), True, False)
+    for s in range(1, 16):
+        o = 128 + 16 * (s - 1)
+        mm(p, c(bk, o, o + 16), c("Y", 16 - s, 144 - s), c("c16", 0, 16), False, False)
+        mm(p, c(bk, o, o + 16), c("Imh", 0, 128), c("c16", 0, 16), False, s == 15)
+    ts(p, c("EQ", 0, 240), c(bk, 128, 368), 0.0, OP.is_equal, tag="EQ")
+    for s in range(15):
+        mm(p, c(bk, 368, 384), c("Ib", 0, 128), c("EQ", 16 * s, 16 * s + 16), s == 0, s == 14)
+    ts(p, c("dd", 0, 16), c(bk, 368, 384), 0.5, OP.is_gt, col(DC), OP.mult)
+    tt(p, c("cdI", 0, 16), c("dd", 0, 16), c("cF", 0, 16), OP.max)
+    cp(p, c("cdl", 0, 32, 2), c("cdI", 0, 16))
+
+
+def step(p, t):
+    pa, nx = t & 1, 1 - (t & 1)
+    na = nb = 0
+    for ch in ORDER:
+        if ch == "A":
+            trail_chunk(p, t, na)
+            na += 1
+            if na == 2:
+                blend(p, t, 0)
+                replay_value(p, t)
+                write_lists(p, t)
+            if na == 4:
+                blend(p, t, 1)
+        else:
+            score_chunk(p, t, nb)
+            nb += 1
+            if nb == 4:
+                cut_choice(p, t)
+                gauge(p, t)
+                cut_lists(p, t)
+    k = t + 3
+    g1 = 512 * nx + 256 * (k // 8) + 16 * (k % 8)
+    cp(p, c("GV", g1, g1 + 16), c("c16", 0, 16))
+    cp(p, c("GL", 256 * nx + 16 * k, 256 * nx + 16 * k + 16), c("cl", 0, 16))
+    scat(p, c("xs", 0, NC + B), c("wcl", 0, 16), c("XW", 0, 256), tag="scw")
+    for q in range(16):
+        scat(p, c("xs", 0, NC + B), c("cdl", 2 * q, 2 * q + 1), c("xh", 16 * q, 16 * q + 16), tag="scc")
+    to_rows(p, "GV", 512 * nx + 128)
+    scat(p, c("can", 0, NU + B), c("wcl", 16, 32), c("VN", 0, 256), tag="sccan")
+    if t < STEPS - 1:
+        lists_of_w(p, t + 1)
+        first_lanes(p, t + 1)
+        canal_lists(p, t + 1)
+
+
+def prologue(p):
+    dma(p, c("trI", 0, 256), "trail", 0)
+    dma(p, c("canI", 0, 320), "canal", 1)
+    dma(p, ("cutI", 0, 256, 1, 8), "cut", 2)
+    dma(p, c("zraw", 0, 256), "z", 3)
+    dma(p, c("xraw", 0, NC), "x", 4)
+    constants(p)
+    ts(p, c("tr16", 0, 256), c("trI", 0, 256), -float(CEN), OP.add)
+    mm(p, c("b7", 0, 256), c("PS", 0, 128), c("tr16", 0, 256), True, True)
+    cp(p, c("KN", 0, 256), c("b7", 0, 256))
+    for b in range(8):
+        vtr(p, c("TRK", 512 + b, 512 + 256, 8), c("KN", 32 * b, 32 * b + 32))
+    turn(p, "b3", 0, 512)
+    ts(p, c("GL", 0, 256), c("b3", 0, 256), float(CEN), OP.add)
+    for h in (0, 1):
+        cp(p, c("GV", 256 * h, 256 * h + 128), c("b3", 128 * h, 128 * h + 128))
+    ts(p, ("cut16", 0, 256, 1, 8), ("cutI", 0, 256, 1, 8), -float(CEN), OP.add)
+    for r in range(16):
+        mm(p, c("b6", 0, 16), ("ZW", 15 - r, 143 - r, 1, 8), ("cut16", r, 256, 16, 8), r == 0, r == 15)
+    ts(p, c("vh", 0, 16), c("b6", 0, 16), 0.125, OP.mult, 1536 + 160 - 0.4375, OP.add)
+    ts(p, c("vuL", 0, 16), c("vh", 0, 16), -1536.0, OP.add)
+    ts(p, c("can16", 0, 320), c("canI", 0, 320), -float(CEN), OP.add)
+    mm(p, c("b4", 0, 320), c("PS", 0, 128), c("can16", 0, 320), True, True)
+    act(p, c("can", 0, 320), c("b4", 0, 320), AF.Copy)
+    lists_of_w(p, 0)
+    first_lanes(p, 0)
+    canal_lists(p, 0)
+    for k in range(4):
+        act(p, c("zr", 256 * k, 256 * k + 256), c("zraw", 0, 256), AF.Identity, bias=128.0)
+    act(p, c("xs", 0, NC), c("xraw", 0, NC), AF.Identity, bias=128.0)
+
+
+def epilogue(p):
+    cp(p, c("can16", 0, 320), c("can", 0, 320))
+    mm(p, c("b4", 0, 320), c("PS", 128, 256), c("can16", 0, 320), True, True)
+    act(p, c("outF", 0, 320), c("b4", 0, 320), AF.Identity, bias=float(CEN))
+    dma(p, "yl", c("outF", 0, 320), 5)
+    to_rows(p, "GV", 0)
+    cp(p, c("trO", 0, 256), c("VN", 0, 256))
+    mm(p, c("b7", 0, 256), c("PS", 128, 256), c("trO", 0, 256), True, True)
+    act(p, c("outG", 0, 256), c("b7", 0, 256), AF.Identity, bias=float(CEN))
+    dma(p, "yg", c("outG", 0, 256), 6)
+    h = NC // 2
+    ts(p, c("xo", 0, h), c("xs", 0, h), -128.0, OP.add)
+    dma(p, "yx", c("xo", 0, h), 7, 0, h)
+    act(p, c("xo", h, NC), c("xs", h, NC), AF.Identity, bias=-128.0)
+    dma(p, "yx", c("xo", h, NC), 8, h, NC)
+
+
+LONG = ("A0", "A1", "A2", "A3", "B0", "B1", "B2", "B3")
+
+
+def schedule(p):
+    ops = p["ops"]
+    n = len(ops)
+    succ = [[] for _ in range(n)]
+    for i in range(n):
+        for j in ops[i]["deps"]:
+            succ[j].append(i)
+    tail = [0.0] * n
+    for i in range(n - 1, -1, -1):
+        tail[i] = ops[i]["cost"] + max([tail[k] + (0.0 if ops[k]["q"] == ops[i]["q"] else 0.06) for k in succ[i]] or [0.0])
+    left = [len(o["deps"]) for o in ops]
+    ready = [0.0] * n
+    pools = {"v": [], "a": [], "p": [], "g": [], "sync": [], "net": []}
+    free = {q: 0.0 for q in pools}
+    order = {q: [] for q in pools}
+    for i in range(n):
+        if left[i] == 0:
+            pools[ops[i]["q"]].append(i)
+    p["span"] = 0.0
+    for _ in range(n):
+        t0, q = min((max(free[q], min(ready[i] for i in pools[q])), q) for q in pools if pools[q])
+        cand = [i for i in pools[q] if ready[i] <= t0 + 1e-9]
+        if q == "v":
+            few = [k for k in cand if ops[k]["tag"] not in LONG]
+            i = max(few, key=lambda k: (tail[k], -k)) if few else min(cand)
+        elif q == "a":
+            few = [k for k in cand if ops[k]["cost"] < SMALL] or cand
+            i = max(few, key=lambda k: (tail[k], -k))
+        else:
+            i = max(cand, key=lambda k: (tail[k], -k))
+        pools[q].remove(i)
+        fin = t0 + ops[i]["cost"]
+        free[q] = t0 if q == "net" else t0 + 0.1 if q == "sync" else fin
+        p["span"] = max(p["span"], fin)
+        order[q].append(i)
+        for k in succ[i]:
+            ready[k] = max(ready[k], fin + (0.06 if ops[k]["q"] != q else 0.0 if q == "p" else 0.03))
+            left[k] -= 1
+            if left[k] == 0:
+                pools[ops[k]["q"]].append(k)
+    p["order"] = order
+    seq, ptr, out = [], {q: 0 for q in order}, set()
+    while len(seq) < n:
+        for q in order:
+            while ptr[q] < len(order[q]) and all(j in out for j in ops[order[q][ptr[q]]]["deps"]):
+                seq.append(order[q][ptr[q]])
+                out.add(order[q][ptr[q]])
+                ptr[q] += 1
+    p["emit"] = seq
+
+
+_CACHE = {}
+
+
+def program():
+    if "p" not in _CACHE:
+        p = {"ops": [], "acc": {}, "bank": {}}
+        prologue(p)
+        for t in range(STEPS):
+            step(p, t)
+        epilogue(p)
+        schedule(p)
+        _CACHE["p"] = p
+    return _CACHE["p"]
+
+
+SEMOF = {"v": "sv", "a": "sa", "p": "sp", "g": "sg"}
+
+
+def dest(T, r, t):
+    return T.cores[(r + 1 + t % 7) % len(T.cores)]
+
+
+def relay_of(topo, T, src, dst):
+    if topo.may_write(src, dst):
+        return None
+    cand = [k for k in topo.cores_of(src) if T.rank_of(k) is None and topo.may_write(k, dst)]
+    same = [k for k in cand if topo.die(k) == topo.die(src)]
+    return (same or cand)[0]
+
+
+def hand_on(g, core, T, topo):
+    sent = 0
+    for t in range(STEPS - 1):
+        for r in range(len(T.cores)):
+            src, dst = T.cores[r], dest(T, r, t)
+            if core in topo.cores_of(src) and relay_of(topo, T, src, dst) == core:
+                g.wait_ge(T.sem["r%d" % t], len(topo.engines(src, core)))
+                rid, pid = topo.addr(dst, core)
+                g.remote_dma(T.zland[:, 256 * t:256 * t + 256], T.relay[:, 256 * t:256 * t + 256], T.sem["z%d" % t], T.sem.zl, pid, rid, topo.mask(core, dst))
+                sent += len(topo.engines(core, dst))
+    if sent:
+        g.wait_ge(T.sem.zl, sent)
+
+
+def rank_program(g, core, T, topo):
+    rank = T.rank_of(core)
+    if rank is None:
+        hand_on(g, core, T, topo)
+        return
+    p = program()
+    ops = p["ops"]
+    queue = {"v": g.vector, "a": g.scalar, "p": g.tensor, "g": g, "sync": g.sync}
+    known = {q: {} for q in queue}
+    clk, gpos, seen = {}, {}, {}
+    count = {"v": 0, "a": 0, "p": 0, "g": 0}
+    sent = 0
+    for i in p["emit"]:
+        o = ops[i]
+        q = o["q"]
+        if q == "net":
+            continue
+        kn, need = known[q], {}
+        for j, w in o["deps"].items():
+            oj = ops[j]
+            if oj["q"] == "net" or not w or isinstance(oj["fn"], tuple):
+                continue
+            s, v = (oj["dsem"], 16) if oj["dsem"] else (SEMOF[oj["q"]], gpos[j])
+            if kn.get(s, 0) < v and need.get(s, (0, 0))[0] < v:
+                need[s] = (v, j)
+        for s in list(need):
+            if any(s2 != s and clk[need[s2][1]].get(s, 0) >= need[s][0] for s2 in need):
+                del need[s]
+        for s, (v, j) in need.items():
+            queue[q].wait_ge(T.sem[s], v)
+            for s2, v2 in clk[j].items():
+                kn[s2] = max(kn.get(s2, 0), v2)
+        t = o["ext"]
+        if t is not None and (q, t) not in seen:
+            seen[(q, t)] = True
+            for src in T.cores:
+                if dest(T, T.rank_of(src), t) == core:
+                    via = relay_of(topo, T, src, core)
+                    queue[q].wait_ge(T.sem["z%d" % t], len(topo.engines(src if via is None else via, core)))
+        if isinstance(o["fn"], tuple):
+            t = o["fn"][1]
+            dst = dest(T, rank, t)
+            via = relay_of(topo, T, core, dst)
+            to = dst if via is None else via
+            rid, pid = topo.addr(to, core)
+            g.remote_dma((T.zland if via is None else T.relay)[:, 256 * t:256 * t + 256], T.zn[:, 256 * t:256 * t + 256],
+                         T.sem[("z%d" if via is None else "r%d") % t], T.sem.zl, pid, rid, topo.mask(core, to))
+            sent += len(topo.engines(core, to))
+            continue
+        ins = o["fn"](g, T)
+        clk[i] = dict(kn)
+        if o["dsem"]:
+            ins.then_inc(T.sem[o["dsem"]], 16)
+            clk[i][o["dsem"]] = 16
+        else:
+            ins.then_inc(T.sem[SEMOF[q]], 1)
+            count[q] += 1
+            gpos[i] = clk[i][SEMOF[q]] = count[q]
+    for q in count:
+        g.wait_ge(T.sem[SEMOF[q]], count[q])
+    for o in ops:
+        if o["dsem"]:
+            g.wait_ge(T.sem[o["dsem"]], 16)
+    g.wait_ge(T.sem.zl, sent)

@@ -2,32 +2,34 @@ import math
 from concourse.mybir import AluOpType as OP, ActivationFunctionType as AF
 
 NC, NU, B, STEPS, CEN = 2560, 320, 256, 8, 1280
-BIG = 4096.0
+Y = 4096.0
 LN = math.log(1.75)
-BY_ACT = (0, 1, 2)
-ORDER = "AABBBABA"
-NET = 7.0
-PEC = 0.0006
-SMALL = 0.3
-GAT, SCA, CY = 1.5, 3.0, 0.001
-BK = {"zn": "b0", "dup": "b1", "skip": "b6"}
+SA, SB = 0.97, -13.0 / 256
+C0 = SA + 6148 * SB
+RND = 1.5 * 2.0 ** 28
+STEEP = 400.0
+ROUTE = "VVSSVSSV"
+NH = 1
+ND = 3
+NET, PEC, GAT, SCA, CY, HOP, OWN, PASSES = 6.0, 0.0005, 1.5, 3.5, 0.001, 0.15, 0.1, 4
 
 BUFS = {
-    "bfloat16": "xs 2816 xraw 2560 zraw 256 zland 1792 zn 1792 relay 1792 zr 2048 D 4096 AB 4096 SG 4096 E 4096 R 4096 SM 256 NM 256 SW 256 "
-                "NW 256 PB 256 XM 256 XW 256 xc 256 xh 256 EQ 240 G12 512 LOH 576 Fs 160 Pf 256 skb 16 W 144 Ib 128 Ihalf 128 Ineg 128 "
-                "Im1 128 BD 128 one 128 four 256 TRI 240 T12 640 R2 160 xo 2560",
-    "float16": "can16 320 tr16 256 cut16 256 GV 1024 KN 512 TRK 1024 c16 16 Ih 128 Imh 128 Y 144 X 512 Xs 512 PS 256 ZW 144 trO 256 uh 16 hh 16 vh 16",
-    "float32": "can 576 BS 512 VN 256 kS 128 k1 128 k2 64 k3 32 km 16 kd 16 cF 16 dd 16 wuF 64 ssj 16 sc 1 lc 2 M2 32 M3 32 M4 32 ioF 320 "
-               "pc 24 tF 320 tG 320 tH 320 DUMP 32 iL 16 THR 16 swa 2 swt 2 outF 320 outG 256",
-    "int32": "canI 320 trI 256 cutI 256 kr 16 cdI 16 scI 1 sdI 1 ioI 320 pI 1 qI 4 tI 320 tI2 320",
-    "uint16": "GL 512 KL 256 cl 16 vuL 96 cdl 32 hl 16 wcl 32",
+    "bfloat16": "xs 2816 xraw 2560 zraw 256 zz 4096 zn 1792 relay 1792 R 4096 AB 4096 SG 4096 E 4096 n 256 nsk 256 P1 256 P2 256 xc 256 xh 512 "
+                "EQ 128 G12 256 LOH 624 Fs 46 Pf 256 nf 16 sI 512 Ipm 256 W1 144 W4 144 W16 144 Ihalf 256 I256 256 Ic 128 Ik 128 BD 128 "
+                "one 256 T12 322 R2 312 Q 1024 xo 2560 hB 322 lB 322 t1 322 t2 322 t3 322 jB 184 gB 184",
+    "float16": "G16 512 K16 256 TRK 256 c16 32 Xs 512 S 2304 Yc 1024 Ih 128 Imh 128 Iy 128 Iu 128 It 256 ZW 144 cut16 256 uh 32 w16 32 hh 16 vh 16 ioH 144 fh 1",
+    "float32": "can 576 Ac 256 B2 256 k0 64 k1 64 k2 64 k3 64 k4 32 M 32 acc 1 sc 1 Lb 128 vc 1 pc 24 M16 16 M16n 16 DUMP 32 iL 18 sg 18 swt 18 THR 16 "
+               "FH 16 tF 16 outF 320 outG 256",
+    "int32": "canI 320 trI 256 cutI 256 km 16 cI 32 ioI 144 pI 1 qI 4 tI 16 fI 8",
+    "uint16": "GL 256 KL 256 cv 32 cdl 32 ul 32 hl 16 wcl 32",
 }
 SCRATCH = {"b%d" % i: ("psum", [128, 512], "float32") for i in range(8)}
 for _dt, _s in BUFS.items():
     _l = _s.split()
     for _i in range(0, len(_l), 2):
         SCRATCH[_l[_i]] = ("sbuf", [128, int(_l[_i + 1])], _dt)
-SEMAPHORES = ["sv", "sa", "sp", "sg", "zl"] + ["z%d" % t for t in range(7)] + ["r%d" % t for t in range(7)] + ["d%d" % i for i in range(9)]
+SEMAPHORES = ["sv", "sa", "sp", "sg", "zl"] + ["z%d" % t for t in range(7)] + ["r%d" % t for t in range(7)] + ["d%d" % i for i in range(10)]
+SC, CN, BL, XW, MI = "b3", "b4", "b5", "b6", "b7"
 
 
 def col(i):
@@ -40,9 +42,8 @@ def c(name, lo, hi, st=1):
 
 def ap(T, a):
     t = T[a[0]]
-    if len(a) == 5:
-        return t[0:a[4], a[1]:a[2]:a[3]] if a[3] > 1 else t[0:a[4], a[1]:a[2]]
-    return t[:, a[1]:a[2]:a[3]] if a[3] > 1 else t[:, a[1]:a[2]]
+    p0, p1 = a[4] if len(a) == 5 else (0, 128)
+    return t[p0:p1, a[1]:a[2]:a[3]] if a[3] > 1 else t[p0:p1, a[1]:a[2]]
 
 
 def width(a):
@@ -72,33 +73,38 @@ def add(p, q, fn, reads, writes, cost, dsem=None, tag=""):
                     keep.append(e)
             keep.append((i, lo, hi, st, wr))
             p["acc"][name] = keep
-    p["ops"].append({"q": q, "fn": fn, "deps": deps, "cost": cost, "ext": None, "dsem": dsem, "tag": tag})
+    p["ops"].append({"q": q, "fn": fn, "deps": deps, "cost": cost, "dsem": dsem, "tag": tag or (writes[0][0] if writes else "")})
     return i
 
 
-def ts(p, out, in0, s1, op0, s2=None, op1=None, tag=""):
+def vcost(n):
+    return 0.01 + max(64, n) * CY
+
+
+def ts(p, out, in0, s1, op0, s2=None, op1=None, offs=None, tag=""):
     def fn(g, T):
         a1 = ap(T, s1) if isinstance(s1, tuple) else s1
         a2 = ap(T, s2) if isinstance(s2, tuple) else s2
+        src = ap(T, in0) if offs is None else ap(T, in0).indirect(ap(T, offs))
         if op1 is None:
-            return g.vector.tensor_scalar(ap(T, out), ap(T, in0), a1, None, op0)
-        return g.vector.tensor_scalar(ap(T, out), ap(T, in0), a1, a2, op0, op1)
+            return g.vector.tensor_scalar(ap(T, out), src, a1, None, op0)
+        return g.vector.tensor_scalar(ap(T, out), src, a1, a2, op0, op1)
     f = 0.5 if half(out) and half(in0) else 1.0
-    return add(p, "v", fn, [in0] + [s for s in (s1, s2) if isinstance(s, tuple)], [out], 0.01 + max(64, width(out) * f) * CY, tag=tag)
+    return add(p, "v", fn, [in0] + [s for s in (s1, s2, offs) if isinstance(s, tuple)], [out], vcost(width(out) * f), tag=tag)
 
 
 def tt(p, out, in0, in1, op, tag=""):
     f = 1 if SCRATCH[in0[0]][0] == "psum" or SCRATCH[in1[0]][0] == "psum" else 2
-    return add(p, "v", lambda g, T: g.vector.tensor_tensor(ap(T, out), ap(T, in0), ap(T, in1), op), [in0, in1], [out], 0.01 + max(64, width(out) * f) * CY, tag=tag)
+    return add(p, "v", lambda g, T: g.vector.tensor_tensor(ap(T, out), ap(T, in0), ap(T, in1), op), [in0, in1], [out], vcost(width(out) * f), tag=tag)
 
 
 def cp(p, out, in0, tag=""):
     f = 0.5 if half(out) and half(in0) else 1.0
-    return add(p, "v", lambda g, T: g.vector.tensor_copy(ap(T, out), ap(T, in0)), [in0], [out], 0.01 + max(64, width(out) * f) * CY, tag=tag)
+    return add(p, "v", lambda g, T: g.vector.tensor_copy(ap(T, out), ap(T, in0)), [in0], [out], vcost(width(out) * f), tag=tag)
 
 
 def memset(p, out, val):
-    return add(p, "v", lambda g, T: g.vector.memset(ap(T, out), val), [], [out], 0.01 + max(64, width(out)) * CY)
+    return add(p, "v", lambda g, T: g.vector.memset(ap(T, out), val), [], [out], vcost(width(out) * (0.5 if half(out) else 1)))
 
 
 def gtt(p, out, win, offs, in1, op, tag=""):
@@ -113,8 +119,12 @@ def scat(p, win, offs, in0, tag=""):
     return add(p, "v", lambda g, T: g.vector.tensor_copy(ap(T, win).indirect(ap(T, offs)), ap(T, in0)), [offs, in0], [win], 0.05 + width(in0) * SCA * CY, tag=tag)
 
 
+def scat2(p, win, offs, in0, in1, op, tag=""):
+    return add(p, "v", lambda g, T: g.vector.tensor_tensor(ap(T, win).indirect(ap(T, offs)), ap(T, in0), ap(T, in1), op), [offs, in0, in1], [win], 0.05 + width(in0) * SCA * CY, tag=tag)
+
+
 def vtr(p, out, in0, tag=""):
-    return add(p, "v", lambda g, T: g.vector.transpose(ap(T, out), ap(T, in0)), [in0], [out], 0.01 + 64 * CY, tag=tag)
+    return add(p, "v", lambda g, T: g.vector.transpose(ap(T, out), ap(T, in0)), [in0], [out], vcost(32), tag=tag)
 
 
 def act(p, out, in0, func, bias=None, scale=None, accum=None, offs=None, tag=""):
@@ -132,428 +142,413 @@ def act(p, out, in0, func, bias=None, scale=None, accum=None, offs=None, tag="")
 
 
 def mm(p, out, lhsT, rhs, start, stop):
-    i = add(p, "p", lambda g, T: g.tensor.matmul(ap(T, out), ap(T, lhsT), ap(T, rhs), start, stop), [lhsT, rhs], [out], max(min(64, width(lhsT)), width(out)) * PEC)
+    f = 1 if half(rhs) else 4
+    i = add(p, "p", lambda g, T: g.tensor.matmul(ap(T, out), ap(T, lhsT), ap(T, rhs), start, stop), [lhsT, rhs], [out], f * max(min(64, width(lhsT)), width(out)) * PEC)
     if out[0] in p["bank"]:
         p["ops"][i]["deps"].setdefault(p["bank"][out[0]], False)
     p["bank"][out[0]] = i
     return i
 
 
+def group(p, terms):
+    for k, (o, l, r) in enumerate(terms):
+        mm(p, o, l, r, k == 0, k == len(terms) - 1)
+
+
 def iota(p, out, pattern, base, chan):
-    return add(p, "g", lambda g, T: g.iota(ap(T, out), pattern, base, chan), [], [out], 0.13 + width(out) * 2 * CY)
+    if SCRATCH[out[0]][2] == "int32":
+        return add(p, "g", lambda g, T: g.iota(ap(T, out), pattern, base, chan), [], [out], 0.13 + width(out) * 2 * CY)
+    return add(p, "g", lambda g, T: g.iota(ap(T, out), pattern, base, chan, allow_small_or_imprecise_dtypes=True), [], [out], 0.13 + width(out) * 2 * CY)
 
 
-def dma(p, out, in0, k, lo=None, hi=None):
+def dma(p, q, out, in0, k, lo=None, hi=None):
     def fn(g, T):
         o = ap(T, out) if isinstance(out, tuple) else T[out][:] if lo is None else T[out][:, lo:hi]
         i = ap(T, in0) if isinstance(in0, tuple) else T[in0][:] if lo is None else T[in0][:, lo:hi]
-        return g.sync.dma_start(o, i)
-    return add(p, "sync", fn, [a for a in (in0,) if isinstance(a, tuple)], [a for a in (out,) if isinstance(a, tuple)], 2.5, dsem="d%d" % k)
+        return (g.sync if q == "sync" else g.scalar).dma_start(o, i)
+    return add(p, q, fn, [a for a in (in0,) if isinstance(a, tuple)], [a for a in (out,) if isinstance(a, tuple)], 2.5 if lo is None else 3.2, dsem="d%d" % k)
 
 
-P_, PM, PG, W0, P16, M0, M1, M2C, M0X2, NM1, C20, DC, MB0, MB1, TG, PP, PI, TMP, PZ = range(19)
+P_, PM, PG, W0, G16C, PUP, PDN, MB0, MB1, C23, DC, PZ, LOW, F14, F1 = range(15)
+IB, IM1, IH, IMH = c("Ipm", 0, 128), c("Ipm", 128, 256), c("Ih", 0, 128), c("Imh", 0, 128)
+
+
+def W(name, r):
+    return c(name, 15 - r, 143 - r)
+
+
+def Sel(a, b):
+    return c("S", 144 * a + 15 - b, 144 * a + 143 - b)
+
+
+def X(s, d):
+    return c("Xs", 128 * (2 * s + d), 128 * (2 * s + d) + 128)
 
 
 def constants(p):
     iota(p, c("pI", 0, 1), [[1, 1]], 0, 1)
-    iota(p, c("ioI", 0, 320), [[1, 320]], 0, 0)
+    iota(p, c("ioI", 0, 144), [[1, 144]], 0, 0)
+    iota(p, c("tI", 0, 16), [[16, 16]], 0, 0)
+    iota(p, c("hB", 0, 322), [[1, 23], [0, 14]], -11, 0)
+    iota(p, c("lB", 0, 322), [[0, 23], [1, 14]], 0, 0)
+    iota(p, c("jB", 0, 184), [[0, 8], [1, 23]], -11, 0)
+    iota(p, c("gB", 0, 184), [[1, 8], [0, 23]], 0, 0)
+    iota(p, c("fI", 0, 8), [[1, 8]], 1, 1)
     ts(p, c("qI", 0, 1), c("pI", 0, 1), 15, OP.bitwise_and)
     ts(p, c("qI", 1, 2), c("pI", 0, 1), 4, OP.logical_shift_right)
-    ts(p, c("qI", 2, 3), c("qI", 1, 2), 1, OP.bitwise_and)
+    ts(p, c("qI", 2, 3), c("pI", 0, 1), 4, OP.logical_shift_right, 1, OP.bitwise_and)
+    cp(p, c("pc", PM, PG + 1), c("qI", 0, 2))
     cp(p, col(P_), c("pI", 0, 1))
-    cp(p, col(PM), c("qI", 0, 1))
-    cp(p, col(PG), c("qI", 1, 2))
-    cp(p, col(MB1), c("qI", 2, 3))
-    ts(p, col(MB0), col(MB1), -1.0, OP.mult, 1.0, OP.add)
-    ts(p, col(W0), col(PG), 16.0, OP.mult, 15.0, OP.add)
-    ts(p, col(P16), col(P_), 16.0, OP.add)
-    for k, dst in ((0, M0), (1, M1), (2, M2C)):
-        ts(p, col(dst), col(PM), float(k), OP.is_equal)
-    ts(p, col(M0X2), col(M0), 2.0, OP.mult)
-    ts(p, col(NM1), col(M1), -1.0, OP.mult)
-    ts(p, col(C20), col(PG), 20.0, OP.mult)
-    ts(p, col(DC), col(PM), float(NC), OP.add)
-    ts(p, col(PZ), col(P_), 16.0, OP.mult, 15.0, OP.add)
-    cp(p, c("ioF", 0, 320), c("ioI", 0, 320))
-    io, io144 = c("ioF", 0, 128), c("ioF", 0, 144)
-    ts(p, col(TMP), col(PM), 13.0, OP.is_ge, -16.0, OP.mult)
-    ts(p, col(PP), col(P_), col(TMP), OP.add, 3.0, OP.add)
-    ts(p, col(TMP), col(PM), 3.0, OP.is_lt, 16.0, OP.mult)
-    ts(p, col(PI), col(P_), col(TMP), OP.add, -3.0, OP.add)
-    ts(p, c("PS", 0, 128), io, col(PP), OP.is_equal)
-    ts(p, c("PS", 128, 256), io, col(PI), OP.is_equal)
+    cp(p, c("ioH", 0, 144), c("ioI", 0, 144))
+    io, io144 = c("ioH", 0, 128), c("ioH", 0, 144)
+    ts(p, col(W0), c("qI", 1, 2), 16.0, OP.mult, 15.0, OP.add)
+    ts(p, col(PZ), c("pI", 0, 1), 16.0, OP.mult, 15.0, OP.add)
+    ts(p, c("ZW", 0, 144), io144, col(PZ), OP.is_equal)
+    ts(p, col(PUP), c("pI", 0, 1), 16.0, OP.add)
+    ts(p, col(PDN), c("pI", 0, 1), -16.0, OP.add)
+    ts(p, col(MB1), c("qI", 2, 3), Y, OP.mult)
+    ts(p, col(MB0), c("qI", 2, 3), -Y, OP.mult, Y, OP.add)
     for s in (0, 1):
         for d in (0, 1):
-            ts(p, col(TG), col(P_), 16.0 * (d - s) + 1.0, OP.add, col(MB1 if s else MB0), OP.mult)
-            ts(p, col(TMP), col(TG), -1.0, OP.add)
-            k = 128 * (2 * s + d)
-            ts(p, c("X", k, k + 128), io, col(TMP), OP.is_equal)
-    ts(p, c("Xs", 0, 512), c("X", 0, 512), -1.0 / 4096.0, OP.mult)
-    ts(p, c("ZW", 0, 144), io144, col(PZ), OP.is_equal)
-    ts(p, c("Ih", 0, 128), io, col(P_), OP.is_equal)
-    ts(p, c("Imh", 0, 128), io, col(P_), OP.is_equal, -1.0, OP.mult)
-    ts(p, c("W", 0, 144), io144, col(W0), OP.is_equal)
-    ts(p, c("Ib", 0, 128), io, col(P_), OP.is_equal)
-    act(p, c("Ihalf", 0, 128), c("Ib", 0, 128), AF.Copy, scale=0.5)
-    act(p, c("Ineg", 0, 128), c("Ib", 0, 128), AF.Copy, scale=-BIG)
-    act(p, c("Im1", 0, 128), c("Ib", 0, 128), AF.Copy, scale=-1.0)
-    ts(p, c("Y", 0, 144), io144, col(P16), OP.is_equal)
-    ts(p, c("tI", 0, 320), c("ioI", 0, 320), 4, OP.logical_shift_right)
-    ts(p, c("tI2", 0, 320), c("ioI", 0, 320), 15, OP.bitwise_and)
-    ts(p, c("BD", 0, 128), c("tI", 0, 128), col(PG), OP.is_equal)
-    ts(p, c("T12", 0, 320), c("tI2", 0, 320), col(PM), OP.is_equal)
-    ts(p, c("tF", 0, 320), c("tI", 0, 320), -10.0, OP.add)
-    tt(p, c("tG", 0, 320), c("tF", 0, 320), c("tF", 0, 320), OP.mult)
-    ts(p, c("tG", 0, 320), c("tG", 0, 320), col(M1), OP.mult, col(M2C), OP.add)
-    ts(p, c("tF", 0, 320), c("tF", 0, 320), col(M0), OP.mult)
-    tt(p, c("T12", 320, 640), c("tF", 0, 320), c("tG", 0, 320), OP.add)
-    iota(p, c("tI", 0, 160), [[0, 8], [1, 20]], -10, 0)
-    iota(p, c("tI2", 0, 160), [[1, 8], [0, 20]], 0, 0)
-    cp(p, c("tH", 0, 160), c("tI", 0, 160))
-    tt(p, c("tG", 0, 160), c("tH", 0, 160), c("tH", 0, 160), OP.mult)
-    ts(p, c("tF", 0, 160), c("tH", 0, 160), col(M0X2), OP.mult, col(NM1), OP.add)
-    ts(p, c("tG", 0, 160), c("tG", 0, 160), -1.0, OP.mult, 1.0, OP.add)
-    ts(p, c("tG", 0, 160), c("tG", 0, 160), col(M2C), OP.mult)
-    tt(p, c("tF", 0, 160), c("tF", 0, 160), c("tG", 0, 160), OP.add)
-    ts(p, c("tG", 0, 160), c("tI2", 0, 160), col(PG), OP.is_equal)
-    tt(p, c("R2", 0, 160), c("tF", 0, 160), c("tG", 0, 160), OP.mult)
-    iota(p, c("tI", 0, 240), [[1, 15], [0, 16]], 1, 0)
-    ts(p, c("TRI", 0, 240), c("tI", 0, 240), col(PM), OP.is_gt, 8192.0, OP.mult)
-    iota(p, c("tI2", 0, 16), [[16, 16]], 0, 0)
-    ts(p, c("iL", 0, 16), c("tI2", 0, 16), col(PM), OP.add)
-    ts(p, c("DUMP", 0, 16), c("iL", 0, 16), float(NC), OP.add)
-    ts(p, c("DUMP", 16, 32), c("iL", 0, 16), float(NU), OP.add)
-    ts(p, c("iL", 0, 16), c("iL", 0, 16), -LN, OP.mult, 128 * LN + math.log(2.5), OP.add)
-    act(p, c("THR", 0, 16), c("iL", 0, 16), AF.Exp)
-    for h in (0, 1):
-        ts(p, c("swa", h, h + 1), col(P_), -0.5 * LN, OP.mult, 0.5 * LN * (128 - 128 * h), OP.add)
-    act(p, c("swt", 0, 2), c("swa", 0, 2), AF.Exp)
-    memset(p, c("one", 0, 128), 1.0)
-    memset(p, c("four", 0, 256), 4.0)
-    memset(p, c("lc", 0, 1), -16.5)
+            ts(p, X(s, d), io, col((P_, PUP, PDN)[d - s]), OP.is_equal, col(MB1 if s else MB0), OP.mult)
+    ts(p, c("M16", 0, 16), c("ioH", 0, 16), col(PM), OP.is_equal)
+    ts(p, c("M16n", 0, 16), c("ioH", 0, 16), col(PM), OP.not_equal)
+    for a in range(16):
+        ts(p, c("S", 144 * a, 144 * a + 144), io144, col(W0), OP.is_equal, c("M16", a, a + 1), OP.mult)
+    ts(p, IB, io, col(P_), OP.is_equal)
+    ts(p, c("W1", 0, 144), io144, col(W0), OP.is_equal)
+    for name, f in (("Ih", 1.0), ("Imh", -1.0), ("Iy", Y), ("Iu", 1 / Y)):
+        ts(p, c(name, 0, 128), io, col(P_), OP.is_equal, f, OP.mult)
+    for out, f in ((IM1, -1.0), (c("Ihalf", 0, 128), 0.5), (c("I256", 0, 128), 256.0), (c("I256", 128, 256), -164.0), (c("Ihalf", 128, 256), -0.5),
+                   (c("Ic", 0, 128), float(CEN)), (c("Ik", 0, 128), CEN / Y)):
+        act(p, out, IB, AF.Copy, scale=f)
+    act(p, c("W4", 0, 144), c("W1", 0, 144), AF.Copy, scale=-Y)
+    act(p, c("W16", 0, 144), c("W1", 0, 144), AF.Copy, scale=-1.0 / 16)
+    act(p, c("sI", 0, 256), c("Ipm", 0, 256), AF.Copy, scale=SA)
+    memset(p, c("one", 0, 256), 1.0)
+    memset(p, c("Lb", 0, 128), -SB / 16)
+    memset(p, c("vc", 0, 1), C0 / (-8 * SB))
+    group(p, [(c(XW, 0, 128), IB, W("W1", r)) for r in range(16)])
+    act(p, c("BD", 0, 128), c(XW, 0, 128), AF.Copy)
+    ts(p, col(LOW), col(PM), 14.0, OP.is_lt)
+    ts(p, c("t1", 0, 322), c("lB", 0, 322), col(PM), OP.is_equal)
+    act(p, c("t2", 0, 322), c("hB", 0, 322), AF.Copy, scale=c("M16", 14, 15))
+    act(p, c("t3", 0, 322), c("hB", 0, 322), AF.Square, scale=c("M16", 15, 16))
+    group(p, [(c(BL, 0, 322), IB, c(k, 0, 322)) for k in ("t1", "t2", "t3")])
+    act(p, c("T12", 0, 322), c(BL, 0, 322), AF.Copy)
+    act(p, c("R2", 0, 128), IB, AF.Copy, scale=col(LOW))
+    ts(p, col(F14), c("M16", 14, 15), 2.0, OP.mult)
+    ts(p, col(F1), col(LOW), c("M16", 15, 16), OP.subtract)
+    act(p, c("t2", 0, 184), c("jB", 0, 184), AF.Identity, bias=col(F1), scale=col(F14))
+    act(p, c("t3", 0, 184), c("jB", 0, 184), AF.Square, scale=col(LOW))
+    group(p, [(c(BL, 0, 184), IB, c("t2", 0, 184)), (c(BL, 0, 184), IM1, c("t3", 0, 184))])
+    ts(p, c("t1", 0, 184), c("gB", 0, 184), col(PG), OP.is_equal)
+    tt(p, c("R2", 128, 312), c(BL, 0, 184), c("t1", 0, 184), OP.mult)
+    ts(p, col(C23), c("qI", 2, 3), 23.0, OP.mult, -1536.0, OP.add)
+    ts(p, col(DC), c("qI", 0, 1), float(NC), OP.add)
+    ts(p, c("iL", 0, 16), c("tI", 0, 16), col(PM), OP.add)
+    ts(p, c("iL", 16, 18), c("tI", 0, 16, 8), col(P_), OP.add)
+    ts(p, c("DUMP", 0, 16), c("iL", 0, 16), float(NC - CEN), OP.add, 1 / Y, OP.mult)
+    ts(p, c("DUMP", 16, 32), c("iL", 0, 16), float(NU - CEN), OP.add, 1 / Y, OP.mult)
+    act(p, c("sg", 0, 18), c("iL", 0, 18), AF.Sigmoid, bias=-10.0, scale=-0.5 * LN)
+    ts(p, c("swt", 0, 18), c("sg", 0, 18), math.exp(10 + 64 * LN), OP.mult)
+    tt(p, c("tF", 0, 16), c("swt", 0, 16), c("swt", 0, 16), OP.mult)
+    ts(p, c("THR", 0, 16), c("tF", 0, 16), 2.5, OP.mult)
+    ts(p, c("fI", 0, 8), c("fI", 0, 8), 15, OP.bitwise_and)
+    ts(p, c("FH", 0, 8), c("fI", 0, 8), col(W0), OP.add, -15.0, OP.add)
+    ts(p, c("tF", 0, 8), c("ioH", 1, 9), col(PM), OP.is_gt)
+    ts(p, c("tF", 8, 16), c("ioH", 1, 9), -1.0, OP.mult, 16.0, OP.add)
+    tt(p, c("FH", 8, 16), c("tF", 0, 8), c("tF", 8, 16), OP.mult)
+    ts(p, c("FH", 8, 16), c("FH", 8, 16), col(P_), OP.add)
+    for s in range(8):
+        ts(p, c("Yc", 128 * s, 128 * s + 128), io, c("FH", s, s + 1), OP.is_equal)
+        ts(p, c("Q", 128 * s, 128 * s + 128), io, c("FH", 8 + s, 9 + s), OP.is_equal, 2 * Y, OP.mult)
 
 
-def X(s, d, name="X"):
-    return c(name, 128 * (2 * s + d), 128 * (2 * s + d) + 128)
+def slot(t):
+    return (t + 13) % 16
 
 
-def lists_of_w(p, t):
-    pa = t & 1
-    v = 48 * pa
-    src = c("GV", 512 * pa + 16 * t, 512 * pa + 16 * t + 16)
-    ts(p, c("uh", 0, 16), src, 0.125, OP.mult, 1536 + 160 - 0.4375, OP.add)
-    ts(p, c("hh", 0, 16), src, 1.0 / 128, OP.mult, 1536 + 10 - 63.5 / 128, OP.add)
-    ts(p, c("vuL", v + 16, v + 32), c("uh", 0, 16), -1536.0, OP.add)
-    ts(p, c("vuL", v + 32, v + 48), c("uh", 0, 16), NU - 1536.0, OP.add)
-    ts(p, c("hl", 0, 16), c("hh", 0, 16), -1536.0, OP.add, col(C20), OP.add)
-    ts(p, c("wuF", 32 * pa, 32 * pa + 16), src, float(CEN), OP.add)
-    ts(p, c("wuF", 32 * pa + 16, 32 * pa + 32), c("uh", 0, 16), -1536.0, OP.add)
+def w_terms(t, out):
+    g = 256 * (t & 1)
+    return [(out, Sel(slot(t), r), c("G16", g + r, g + 256, 16)) for r in range(16)]
 
 
 def first_lanes(p, t):
-    v = 48 * (t & 1)
-    act(p, c("G12", 0, 512), c("T12", 0, 640), AF.Copy, offs=c("vuL", v + 16, v + 48), tag="G12")
+    v = 16 * (t & 1)
+    wl = c(MI, 374, 390)
+    group(p, w_terms(t, wl))
+    ts(p, c("uh", v, v + 16), wl, Y / 8, OP.mult, 1536 + CEN / 8 - 0.4375, OP.add)
+    ts(p, c("hh", 0, 16), wl, Y / 112, OP.mult, 1536 + (CEN - 55.5) / 112, OP.add)
+    ts(p, c("ul", v, v + 16), c("uh", v, v + 16), -1536.0, OP.add)
+    cp(p, c("w16", v, v + 16), wl)
+    ts(p, c("hl", 0, 16), c("hh", 0, 16), col(C23), OP.add)
+    act(p, c("G12", 0, 256), c("T12", 0, 322), AF.Copy, offs=c("ul", v, v + 16), tag="G12")
     for h in (0, 1):
-        mm(p, c("b5", 0, 128), c("G12", 128 * h, 128 * h + 128), c("Ib", 0, 128), True, True)
-        mm(p, c("b5", 128, 288), c("G12", 256 + 128 * h, 256 + 128 * h + 128), c("R2", 0, 160), True, True)
-        act(p, c("LOH", 288 * h, 288 * h + 288), c("b5", 0, 288), AF.Relu, scale=c("swt", h, h + 1))
-    for h in (0, 1):
-        mm(p, c("b5", 288, 448), c("LOH", 288 * h, 288 * h + 128), c("LOH", 288 * h + 128, 288 * h + 288), h == 0, h == 1)
-    act(p, c("Fs", 0, 160), c("b5", 288, 448), AF.Copy)
-    gtt(p, c("Pf", 0, 256), c("Fs", 0, 160), c("hl", 0, 16), c("G12", 0, 256), OP.mult, tag="Pf")
-    for r in range(16):
-        mm(p, c("b5", 448, 464), c("W", 15 - r, 143 - r), c("Pf", r, 256, 16), r == 0, r == 15)
-    tt(p, c("M2", 0, 16), c("b5", 448, 464), c("THR", 0, 16), OP.is_gt, tag="nf")
+        mm(p, c(MI, 0, 312), c("G12", 128 * h, 128 * h + 128), c("R2", 0, 312), True, True)
+        act(p, c("LOH", 312 * h, 312 * h + 312), c(MI, 0, 312), AF.Relu, scale=c("swt", 16 + h, 17 + h), tag="LOH")
+    for k in range(4):
+        group(p, [((MI, 312, 358, 1, (32 * k, 32 * k + 32)), c("LOH", 312 * h + 32 * k, 312 * h + 32 * k + 32),
+                   c("LOH", 312 * h + 128 + 46 * k, 312 * h + 174 + 46 * k)) for h in (0, 1)])
+    act(p, c("Fs", 0, 46), c(MI, 312, 358), AF.Copy)
+    gtt(p, c("Pf", 0, 256), c("Fs", 0, 46), c("hl", 0, 16), c("G12", 0, 256), OP.mult, tag="Pf")
+    group(p, [(c(MI, 358, 374), W("W1", r), c("Pf", r, 256, 16)) for r in range(16)])
+    tt(p, c("nf", 0, 16), c(MI, 358, 374), c("THR", 0, 16), OP.is_gt, tag="nf")
 
 
-def turn(p, out, lo, k, lo2=0, n=128, start=True, name="X"):
-    for ql in (0, 1):
-        for par in (0, 1):
-            mm(p, c(out, lo + ql, lo + 2 * n, 2), X(ql, par, name), c("TRK", k + 128 * par + lo2, k + 128 * par + lo2 + n), start and par == 0, par == 1 and (ql == 1 or start))
+def turn_terms(lo, k, n):
+    return [[(c(SC, lo + ql, lo + 2 * n, 2), X(ql, par), c("TRK", 128 * par + k, 128 * par + k + n)) for par in (0, 1)] for ql in (0, 1)]
 
 
-def canal_lists(p, t):
-    pa = t & 1
-    gcp(p, c("KN", 0, 512), c("can", 0, NU), c("vuL", 48 * pa, 48 * pa + 32), tag="KN")
-    for ty in (0, 1):
-        for b in range(8):
-            k = 512 * pa + 256 * ty
-            vtr(p, c("TRK", k + b, k + 256, 8), c("KN", 256 * ty + 32 * b, 256 * ty + 32 * b + 32), tag="trk")
-    turn(p, "b3", 0, 512 * pa)
-    ts(p, c("KL", 0, 256), c("b3", 0, 256), float(CEN), OP.add, tag="KL")
-
-
-def to_rows(p, src, lo):
-    for par in (0, 1):
-        for h in (0, 1):
-            for ql in (0, 1):
-                a, o = lo + 256 * h, 256 + 128 * par + 64 * h
-                mm(p, c("b3", o, o + 64), X(par, ql), c(src, a + ql, a + 128, 2), ql == 0, ql == 1)
+def canal_lists(p):
+    gcp(p, c("K16", 0, 256), c("can", 0, NU), c("cv", 16, 32), tag="K")
     for b in range(8):
-        vtr(p, c("VN", 32 * b, 32 * b + 32), c("b3", 256 + b, 512, 8), tag="trv")
+        vtr(p, c("TRK", b, 256, 8), c("K16", 32 * b, 32 * b + 32), tag="trk")
+    for terms in turn_terms(256, 0, 128):
+        group(p, terms)
+    ts(p, c("KL", 0, 256), c(SC, 256, 512), float(CEN), OP.add, tag="KL")
 
 
-def sums(p, bank, o, src, a, stop=True):
-    for r in range(16):
-        mm(p, c(bank, o, o + 64), c("W", 15 - r, 143 - r), c(src, a + r, a + 1024, 16), r == 0, r == 15 and stop)
-
-
-def trail_chunk(p, t, j):
-    pa = t & 1
-    a, e = 1024 * j, 1024 * j + 1024
-    offs = c("GL", 256 * pa + 64 * j, 256 * pa + 64 * j + 64)
-    if j in BY_ACT:
-        act(p, c("R", a, e), c("xs", 0, NC), AF.Copy, offs=offs, tag="R%d" % j)
+def scores(p, t):
+    z = c("zz", 512 * t, 512 * t + 512)
+    for j in range(4):
         for k in (0, 1):
-            bank = "b6" if k == 0 else "b7"
-            mm(p, c(bank, 0, 512), c("Ib", 0, 128), c("R", a + 512 * k, a + 512 * k + 512), True, False)
-            mm(p, c(bank, 0, 512), c("Im1", 0, 128), c("zr", 1024 * pa, 1024 * pa + 512), False, True)
-            act(p, c("AB", a + 512 * k, a + 512 * k + 512), c(bank, 0, 512), AF.Abs, tag="abs")
+            a = 1024 * j + 512 * k
+            i = gtt(p, c("E", a, a + 512), c("xs", 0, NC), c("KL", a // 16, a // 16 + 32), z, OP.max, tag="B")
+        o = c(SC, 64 * j, 64 * j + 64)
+        turn = turn_terms(64 * j, 32 * j, 32)
+        group(p, [(o, c("Ic", 0, 128), c("one", 0, 64))] + turn[0] + turn[1] + [(o, W("W4", r), c("E", 1024 * j + r, 1024 * j + 1024, 16)) for r in range(16)])
+        if j == 0:
+            cp(p, c("k0", 0, 64), o)
+        else:
+            tt(p, c("k%d" % j, 0, 64), o, c("k%d" % (j - 1), 0, 64), OP.min, tag="tree")
+
+
+def choice(p, t):
+    v = 16 * (t & 1)
+    tt(p, c("k4", 0, 32), c("k3", 0, 32), c("k3", 32, 64), OP.min)
+    tt(p, c("km", 0, 16), c("k4", 0, 16), c("k4", 16, 32), OP.min)
+    ts(p, c("cI", 0, 16), c("km", 0, 16), 4095, OP.bitwise_and)
+    if t < STEPS - 1:
+        ts(p, c("cI", 16, 32), c("km", 0, 16), 3, OP.logical_shift_right, 511, OP.bitwise_and)
+        cp(p, c("cv", 0, 32), c("cI", 0, 32), tag="cv")
     else:
-        gtt(p, c("D", a, e), c("xs", 0, NC), offs, c("zr", 1024 * pa, 1024 * pa + 1024), OP.subtract, tag="A%d" % j)
-        act(p, c("AB", a, e), c("D", a, e), AF.Abs, tag="abs")
-    act(p, c("SG", a, e), c("AB", a, e), AF.Sign, bias=c("lc", pa, pa + 1), tag="sign")
-    sums(p, "b0" if j < 2 else "b1", 64 * (j & 1), "SG", a)
-
-
-def score_chunk(p, t, j):
-    pa = t & 1
-    gtt(p, c("E", 1024 * j, 1024 * j + 1024), c("xs", 0, NC), c("KL", 64 * j, 64 * j + 64), c("zr", 1024 * pa, 1024 * pa + 1024), OP.max, tag="B%d" % j)
-    sums(p, "b2", 64 * j, "E", 1024 * j, False)
-    turn(p, "b2", 64 * j, 512 * pa, 32 * j, 32, False, "Xs")
-
-
-def blend(p, t, h):
-    pa, nx = t & 1, 1 - (t & 1)
-    bank, s = "b%d" % h, 128 * h
-    act(p, c("SM", s, s + 128), c(bank, 0, 128), AF.Relu, tag="SM")
-    act(p, c("NM", s, s + 128), c(bank, 0, 128), AF.Relu, bias=2.0, scale=-1.0)
-    g0, g1 = 512 * pa + 256 * h, 512 * nx + 256 * h
-    for ty in (0, 1):
-        o = 128 * ty
-        mm(p, c("b4", o, o + 128), c("Ih", 0, 128), c("GV", g0, g0 + 128), True, False)
-        mm(p, c("b4", o, o + 128), c("Ineg", 0, 128), c("SM", s, s + 128), False, True)
-        mm(p, c("b4", o + 256, o + 384), c("Ineg", 0, 128), c("NM", s, s + 128), True, False)
-        turn(p, "b4", o + 256, 512 * pa + 256 * ty, 64 * h, 64, False)
-    act(p, c("BS", 256 * h, 256 * h + 256), c("b4", 256, 512), AF.Copy)
-    tt(p, c("GV", g1, g1 + 256), c("b4", 0, 256), c("BS", 256 * h, 256 * h + 256), OP.max, tag="blend")
-    ts(p, c("GL", 256 * nx + s, 256 * nx + s + 128), c("GV", g1, g1 + 128), float(CEN), OP.add, tag="GL")
-
-
-def replay_value(p, t):
-    pa = t & 1
-    raw = t // 4 in BY_ACT
-    d = c("R" if raw else "D", 256 * t, 256 * t + 256)
-    z, I = c("zr", 1024 * pa, 1024 * pa + 256), c("Ib", 0, 128)
-    n = c(BK["skip"], 0, 256)
-    mm(p, n, c("BD", 0, 128), c("SG", 256 * t, 256 * t + 256), True, True)
-    act(p, c("SW", 0, 256), n, AF.Relu)
-    act(p, c("NW", 0, 256), n, AF.Relu, bias=2.0, scale=-1.0)
-    lo, hi = c("b7", 0, 256), c("b7", 256, 512)
-    mm(p, lo, c("Ihalf", 0, 128), d, True, False)
-    mm(p, lo, c("Ihalf", 0, 128) if raw else I, z, False, False)
-    mm(p, lo, c("Ineg", 0, 128), c("SW", 0, 256), False, True)
-    mm(p, hi, I, d, True, False)
-    if not raw:
-        mm(p, hi, I, z, False, False)
-    mm(p, hi, I, c("four", 0, 256), False, False)
-    mm(p, hi, c("Ineg", 0, 128), c("NW", 0, 256), False, True)
-    act(p, c("PB", 0, 256), lo, AF.Identity, bias=-0.25)
-    tt(p, c("XM", 0, 256), hi, c("PB", 0, 256), OP.max, tag="xm")
-    ts(p, c("XW", 0, 256), c("XM", 0, 256), 191.0, OP.min)
-
-
-def write_lists(p, t):
-    pa = t & 1
-    ts(p, c("skb", 0, 16), c("SM", 16 * t, 16 * t + 16), 0.5, OP.is_gt)
-    if t < STEPS - 1:
-        mm(p, c("b5", 464, 480), c("one", 0, 128), c("skb", 0, 16), True, True)
-        act(p, c("ssj", 0, 16), c("b5", 464, 480), AF.Copy, accum=c("sc", 0, 1))
-        cp(p, c("scI", 0, 1), c("sc", 0, 1))
-        ts(p, c("sdI", 0, 1), c("scI", 0, 1), 3, OP.bitwise_and)
-        ts(p, c("lc", 1 - pa, 2 - pa), c("sdI", 0, 1), -1.0, OP.mult, -16.5, OP.add)
-    tt(p, c("M2", 16, 32), c("M2", 0, 16), c("skb", 0, 16), OP.max)
-    tt(p, c("M3", 0, 32), c("M2", 0, 32), c("DUMP", 0, 32), OP.mult)
-    tt(p, c("M4", 0, 32), c("M3", 0, 32), c("wuF", 32 * pa, 32 * pa + 32), OP.max)
-    cp(p, c("wcl", 0, 32), c("M4", 0, 32))
-
-
-def cut_choice(p, t):
-    nx = 1 - (t & 1)
-    act(p, c("kS", 0, 128), c("b2", 128, 256), AF.Copy)
-    tt(p, c("k1", 0, 128), c("b2", 0, 128), c("kS", 0, 128), OP.max, tag="k1")
-    tt(p, c("k2", 0, 64), c("k1", 0, 64), c("k1", 64, 128), OP.max)
-    tt(p, c("k3", 0, 32), c("k2", 0, 32), c("k2", 32, 64), OP.max)
-    tt(p, c("km", 0, 16), c("k3", 0, 16), c("k3", 16, 32), OP.max)
-    cp(p, c("kr", 0, 16), c("km", 0, 16))
-    tt(p, c("kd", 0, 16), c("kr", 0, 16), c("km", 0, 16), OP.subtract)
-    ts(p, c("cl", 0, 16), c("kd", 0, 16), 4096.0, OP.mult, float(CEN), OP.add, tag="cl")
-    ts(p, c("c16", 0, 16), c("kd", 0, 16), 4096.0, OP.mult)
-    act(p, c("cF", 0, 16), c("kd", 0, 16), AF.Identity, bias=float(CEN), scale=4096.0)
-    if t < STEPS - 1:
-        ts(p, c("vh", 0, 16), c("kd", 0, 16), 512.0, OP.mult, 1536 + 160 - 0.4375, OP.add)
-        ts(p, c("vuL", 48 * nx, 48 * nx + 16), c("vh", 0, 16), -1536.0, OP.add)
+        cp(p, c("cv", 0, 16), c("cI", 0, 16), tag="cv")
+    ts(p, c("c16", v, v + 16), c("cI", 0, 16), -float(CEN), OP.add, 1 / Y, OP.mult)
 
 
 def gauge(p, t):
-    pa = t & 1
-    act(p, c("xc", 0, 256), c("xs", 0, NC), AF.Copy, offs=c("cl", 0, 16), tag="xc")
+    act(p, c("xc", 0, 256), c("xs", 0, NC), AF.Copy, offs=c("cv", 0, 16), tag="xc")
     if t < STEPS - 1:
-        zt, n = c("zn", 256 * t, 256 * t + 256), c(BK["zn"], 128, 384)
-        mm(p, n, c("Ib", 0, 128), c("xc", 0, 256), True, False)
-        mm(p, n, c("Ib", 0, 128), c("zr", 1024 * pa, 1024 * pa + 256), False, True)
+        zt, n = c("zn", 256 * t, 256 * t + 256), c(SC, 256, 512)
+        group(p, [(n, IB, c("zz", 512 * t, 512 * t + 256)), (n, IB, c("xc", 0, 256))])
         act(p, zt, n, AF.Identity, bias=-0.25, scale=0.5, tag="zn")
         add(p, "g", ("send", t), [zt], [], 0.1)
-        add(p, "net", ("net", t), [zt], [c("zland", 256 * t, 256 * t + 256)], NET)
-        for k in range(4):
-            o = 1024 * (1 - pa) + 256 * k
-            i = cp(p, c("zr", o, o + 256), c("zland", 256 * t, 256 * t + 256), tag="zr")
-            p["ops"][i]["ext"] = t
-    act(p, c("xh", 0, 256), c("xc", 0, 256), AF.Identity, bias=63.75, scale=0.5)
+        land = c("zz", 512 * t + 512, 512 * t + 768)
+        add(p, "net", ("net", t), [zt], [land], NET)
+        cp(p, c("zz", 512 * t + 768, 512 * t + 1024), land, tag="zr")
+    act(p, c("xh", 256 * (t & 1), 256 * (t & 1) + 256), c("xc", 0, 256), AF.Identity, bias=63.75, scale=0.5, tag="xh")
 
 
 def cut_lists(p, t):
-    bk = BK["dup"]
-    mm(p, c(bk, 128, 368), c("Ib", 0, 128), c("TRI", 0, 240), True, False)
-    for s in range(1, 16):
-        o = 128 + 16 * (s - 1)
-        mm(p, c(bk, o, o + 16), c("Y", 16 - s, 144 - s), c("c16", 0, 16), False, False)
-        mm(p, c(bk, o, o + 16), c("Imh", 0, 128), c("c16", 0, 16), False, s == 15)
-    ts(p, c("EQ", 0, 240), c(bk, 128, 368), 0.0, OP.is_equal, tag="EQ")
-    for s in range(15):
-        mm(p, c(bk, 368, 384), c("Ib", 0, 128), c("EQ", 16 * s, 16 * s + 16), s == 0, s == 14)
-    ts(p, c("dd", 0, 16), c(bk, 368, 384), 0.5, OP.is_gt, col(DC), OP.mult)
-    tt(p, c("cdI", 0, 16), c("dd", 0, 16), c("cF", 0, 16), OP.max)
-    cp(p, c("cdl", 0, 32, 2), c("cdI", 0, 16))
+    c16 = c("c16", 16 * (t & 1), 16 * (t & 1) + 16)
+    for s in range(8):
+        o = c(MI, 16 * s, 16 * s + 16)
+        group(p, [(o, c("Yc", 128 * s, 128 * s + 128), c16), (o, IMH, c16)])
+    ts(p, c("EQ", 0, 128), c(MI, 0, 128), 0.0, OP.is_equal, tag="EQ")
+    o = c(MI, 128, 144)
+    group(p, [(o, c("Iy", 0, 128), c16)] + [(o, c("Q", 128 * s, 128 * s + 128), c("EQ", 16 * s, 16 * s + 16)) for s in range(8)])
+    ts(p, c("cdl", 0, 32, 2), o, float(CEN), OP.add, col(DC), OP.min, tag="cdl")
+
+
+def block(p, t, h, qd, k):
+    bank, s, a = "b%d" % (p["nd"][0] % ND), 256 * (t & 1), 2048 * h + 512 * qd
+    p["nd"][0] += 1
+    for kk in range(4):
+        e, o = 4 * qd + kk, c(bank, 128 * kk, 128 * kk + 128)
+        src = c("xh", 256 * (e & 1) + 128 * h, 256 * (e & 1) + 128 * h + 128) if e == t - 1 else c("R", 2048 * h + e, 2048 * h + 2048, 16)
+        group(p, [(o, c("sI", s, s + 128), src), (o, c("sI", s + 128, s + 256), c("zz", 512 * t + 128 * h, 512 * t + 128 * h + 128))])
+    d, sg, ab = c(bank, 0, 512), c("SG", a, a + 512), c("AB", a, a + 512)
+    if ROUTE[k] == "V":
+        ts(p, sg, d, RND, OP.add, RND, OP.not_equal, tag="test")
+    else:
+        act(p, ab, d, AF.Abs, tag="abs")
+        if ROUTE[k] == "M":
+            ts(p, sg, ab, 16.0, OP.is_gt, tag="test")
+        else:
+            act(p, sg, ab, AF.Sigmoid, bias=-16 * STEEP, scale=STEEP, tag="test")
+
+
+def sg_of(h, e):
+    a = 2048 * h + 128 * e
+    return c("SG", a, a + 128)
+
+
+def replay(p, t):
+    e, v, nsk = slot(t), 16 * (t & 1), c("nsk", 0, 256)
+    for h in (0, 1):
+        mm(p, c(XW, 128 * h, 128 * h + 128), c("BD", 0, 128), sg_of(h, e), True, True)
+    act(p, nsk, c(XW, 0, 256), AF.Sigmoid, bias=8.5 * STEEP, scale=-STEEP, accum=c("acc", 0, 1) if t < STEPS - 1 else None, tag="nsk")
+    lo, hi, xw = c(XW, 0, 256), c(XW, 256, 512), c("R", e, 4096, 16)
+    group(p, [(hi, IB, xw), (hi, c("I256", 128, 256), nsk)])
+    ts(p, c("P2", 0, 256), hi, 4.0, OP.add, 191.0, OP.min, tag="P2")
+    group(p, [(lo, c("Ihalf", 128, 256), xw), (lo, c("Ihalf", 0, 128), c("zz", 512 * t, 512 * t + 256)), (lo, c("I256", 0, 128), nsk)])
+    act(p, c("P1", 0, 256), lo, AF.Relu, bias=159.75 - 256, tag="P1")
+    lw, lu, nf = c(MI, 390, 406), c(MI, 406, 422), c("nf", 0, 16)
+    group(p, [(lw, IH, c("w16", v, v + 16)), (lw, IB, nf)])
+    group(p, [(lu, c("Iu", 0, 128), c("uh", v, v + 16)), (lu, IB, nf), (lu, c("Ik", 0, 128), c("one", 0, 16))] + [(lu, W("W16", r), c("nsk", r, 256, 16)) for r in range(16)])
+    tt(p, c("M", 0, 32), c(MI, 390, 422), c("DUMP", 0, 32), OP.min)
+    ts(p, c("wcl", 0, 32), c("M", 0, 32), Y, OP.mult, float(CEN), OP.add, tag="wcl")
+    if t < STEPS - 1:
+        u, s = c(MI, 422, 423), 256 * (1 - (t & 1))
+        group(p, [(u, c("Lb", 0, 128), c("vc", 0, 1)), (u, c("Lb", 0, 128), c("acc", 0, 1))])
+        ts(p, c("fh", 0, 1), u, 1 / (4 * SB), OP.mult, 1537 - 0.375 - C0 / (4 * SB), OP.add)
+        ts(p, c("sc", 0, 1), c("fh", 0, 1), -4 * SB, OP.mult, u, OP.add)
+        ts(p, c("sI", s, s + 256), c("Ipm", 0, 256), c("sc", 0, 1), OP.mult, tag="sI")
+
+
+def old_trails(p, t, bank, lo, n):
+    g = 256 * (t & 1) + lo
+    if t == 0:
+        return [(c(bank, lo, lo + n), IH, c("G16", g, g + n))]
+    v, it = 16 * ((t - 1) & 1) + lo // 16, 128 * (t & 1)
+    return [(c(bank, lo, lo + n), c("It", it, it + 128), c("G16", g, g + n))] + [(c(bank, lo + r, lo + n, 16), Sel(r, t - 1), c("c16", v, v + n // 16)) for r in range(16)]
+
+
+def counts(p, t, h, order):
+    es = [4 * qd + kk for qd in order for kk in range(4)]
+    group(p, [(c(CN, 128 * h, 128 * h + 128), W("W1", e), sg_of(h, e)) for e in es])
+
+
+def blend(p, t, lo, w):
+    n, a, b, g = c("n", lo, lo + w), c(BL, lo, lo + w), c(BL, 256 + lo, 256 + lo + w), 256 * (1 - (t & 1)) + lo
+    act(p, n, c(CN, lo, lo + w), AF.Sigmoid, bias=8.5 * STEEP, scale=-STEEP, tag="n")
+    group(p, old_trails(p, t, BL, lo, w) + [(a, IB, n)])
+    group(p, [(b, IH, c("K16", lo, lo + w)), (b, IM1, n)])
+    act(p, c("Ac", lo, lo + w), a, AF.Identity, bias=-1.0, tag="Ac")
+    tt(p, c("G16", g, g + w), b, c("Ac", lo, lo + w), OP.max, tag="blend")
+    if t < STEPS - 1:
+        ts(p, c("GL", lo, lo + w), c("G16", g, g + w), Y, OP.mult, float(CEN), OP.add, tag="GL")
 
 
 def step(p, t):
-    pa, nx = t & 1, 1 - (t & 1)
-    na = nb = 0
-    for ch in ORDER:
-        if ch == "A":
-            trail_chunk(p, t, na)
-            na += 1
-            if na == 2:
-                blend(p, t, 0)
-                replay_value(p, t)
-                write_lists(p, t)
-            if na == 4:
-                blend(p, t, 1)
-        else:
-            score_chunk(p, t, nb)
-            nb += 1
-            if nb == 4:
-                cut_choice(p, t)
-                gauge(p, t)
-                cut_lists(p, t)
-    k = t + 3
-    g1 = 512 * nx + 256 * (k // 8) + 16 * (k % 8)
-    cp(p, c("GV", g1, g1 + 16), c("c16", 0, 16))
-    cp(p, c("GL", 256 * nx + 16 * k, 256 * nx + 16 * k + 16), c("cl", 0, 16))
-    scat(p, c("xs", 0, NC + B), c("wcl", 0, 16), c("XW", 0, 256), tag="scw")
-    for q in range(16):
-        scat(p, c("xs", 0, NC + B), c("cdl", 2 * q, 2 * q + 1), c("xh", 16 * q, 16 * q + 16), tag="scc")
-    to_rows(p, "GV", 512 * nx + 128)
-    scat(p, c("can", 0, NU + B), c("wcl", 16, 32), c("VN", 0, 256), tag="sccan")
+    v = 16 * (t & 1)
+    for j in range(4):
+        act(p, c("R", 1024 * j, 1024 * j + 1024), c("xs", 0, NC), AF.Copy, offs=c("GL", 64 * j, 64 * j + 64), tag="A")
+    it = 128 * ((t + 1) & 1)
+    ts(p, c("It", it, it + 128), IH, c("M16n", t, t + 1), OP.mult)
+    scores(p, t)
+    q0 = slot(t) // 4
+    order = [q0] + [q for q in range(4) if q != q0]
+    block(p, t, 0, q0, 0)
+    block(p, t, 1, q0, 1)
+    replay(p, t)
+    choice(p, t)
+    gauge(p, t)
+    cut_lists(p, t)
+    for h in (0, 1):
+        for k in (1, 2, 3):
+            block(p, t, h, order[k], 1 + 3 * h + k)
+        counts(p, t, h, order)
+        if NH == 2:
+            blend(p, t, 128 * h, 128)
+    if NH == 1:
+        blend(p, t, 0, 256)
     if t < STEPS - 1:
-        lists_of_w(p, t + 1)
         first_lanes(p, t + 1)
-        canal_lists(p, t + 1)
+    scat2(p, c("xs", 0, NC + B), c("wcl", 0, 16), c("P1", 0, 256), c("P2", 0, 256), OP.add, tag="scw")
+    for q in range(16):
+        scat(p, c("xs", 0, NC + B), c("cdl", 2 * q, 2 * q + 1), c("xh", 256 * (t & 1) + 16 * q, 256 * (t & 1) + 16 * q + 16), tag="scc")
+    gtt(p, c("B2", 0, 256), c("can", 0, NU), c("ul", v, v + 16), c("n", 0, 256), OP.subtract, tag="KW")
+    scat2(p, c("can", 0, NU + B), c("wcl", 16, 32), c("Ac", 0, 256), c("B2", 0, 256), OP.max, tag="sccan")
+    if t < STEPS - 1:
+        canal_lists(p)
+
+
+XV = 1536
 
 
 def prologue(p):
-    dma(p, c("trI", 0, 256), "trail", 0)
-    dma(p, c("canI", 0, 320), "canal", 1)
-    dma(p, ("cutI", 0, 256, 1, 8), "cut", 2)
-    dma(p, c("zraw", 0, 256), "z", 3)
-    dma(p, c("xraw", 0, NC), "x", 4)
+    cut = (0, 8)
+    dma(p, "sync", ("cutI", 0, 256, 1, cut), "cut", 2)
+    dma(p, "a", c("trI", 0, 256), "trail", 0)
+    dma(p, "sync", c("canI", 0, 320), "canal", 1)
+    dma(p, "a", c("xraw", XV, NC), "x", 9, XV, NC)
+    dma(p, "sync", c("xraw", 0, XV), "x", 4, 0, XV)
+    dma(p, "a", c("zraw", 0, 256), "z", 3)
     constants(p)
-    ts(p, c("tr16", 0, 256), c("trI", 0, 256), -float(CEN), OP.add)
-    mm(p, c("b7", 0, 256), c("PS", 0, 128), c("tr16", 0, 256), True, True)
-    cp(p, c("KN", 0, 256), c("b7", 0, 256))
-    for b in range(8):
-        vtr(p, c("TRK", 512 + b, 512 + 256, 8), c("KN", 32 * b, 32 * b + 32))
-    turn(p, "b3", 0, 512)
-    ts(p, c("GL", 0, 256), c("b3", 0, 256), float(CEN), OP.add)
-    for h in (0, 1):
-        cp(p, c("GV", 256 * h, 256 * h + 128), c("b3", 128 * h, 128 * h + 128))
-    ts(p, ("cut16", 0, 256, 1, 8), ("cutI", 0, 256, 1, 8), -float(CEN), OP.add)
-    for r in range(16):
-        mm(p, c("b6", 0, 16), ("ZW", 15 - r, 143 - r, 1, 8), ("cut16", r, 256, 16, 8), r == 0, r == 15)
-    ts(p, c("vh", 0, 16), c("b6", 0, 16), 0.125, OP.mult, 1536 + 160 - 0.4375, OP.add)
-    ts(p, c("vuL", 0, 16), c("vh", 0, 16), -1536.0, OP.add)
-    ts(p, c("can16", 0, 320), c("canI", 0, 320), -float(CEN), OP.add)
-    mm(p, c("b4", 0, 320), c("PS", 0, 128), c("can16", 0, 320), True, True)
-    act(p, c("can", 0, 320), c("b4", 0, 320), AF.Copy)
-    lists_of_w(p, 0)
+    cp(p, c("GL", 0, 256), c("trI", 0, 256))
+    ts(p, c("G16", 0, 256), c("GL", 0, 256), -float(CEN), OP.add, 1 / Y, OP.mult)
+    ts(p, ("cut16", 0, 256, 1, cut), ("cutI", 0, 256, 1, cut), -float(CEN), OP.add)
+    group(p, [(c(CN, 0, 16), ("ZW", 15 - r, 143 - r, 1, cut), ("cut16", r, 256, 16, cut)) for r in range(16)])
+    ts(p, c("vh", 0, 16), c(CN, 0, 16), 0.125, OP.mult, 1536 + CEN / 8 - 0.4375, OP.add)
+    ts(p, c("cv", 16, 32), c("vh", 0, 16), -1536.0, OP.add)
+    ts(p, c("can", 0, 320), c("canI", 0, 320), -float(CEN), OP.add, 1 / Y, OP.mult)
+    canal_lists(p)
     first_lanes(p, 0)
-    canal_lists(p, 0)
-    for k in range(4):
-        act(p, c("zr", 256 * k, 256 * k + 256), c("zraw", 0, 256), AF.Identity, bias=128.0)
-    act(p, c("xs", 0, NC), c("xraw", 0, NC), AF.Identity, bias=128.0)
+    for k in (0, 1):
+        act(p, c("zz", 256 * k, 256 * k + 256), c("zraw", 0, 256), AF.Identity, bias=128.0)
+    ts(p, c("xs", 0, XV), c("xraw", 0, XV), 128.0, OP.add)
+    act(p, c("xs", XV, NC), c("xraw", XV, NC), AF.Identity, bias=128.0)
 
 
 def epilogue(p):
-    cp(p, c("can16", 0, 320), c("can", 0, 320))
-    mm(p, c("b4", 0, 320), c("PS", 128, 256), c("can16", 0, 320), True, True)
-    act(p, c("outF", 0, 320), c("b4", 0, 320), AF.Identity, bias=float(CEN))
-    dma(p, "yl", c("outF", 0, 320), 5)
-    to_rows(p, "GV", 0)
-    cp(p, c("trO", 0, 256), c("VN", 0, 256))
-    mm(p, c("b7", 0, 256), c("PS", 128, 256), c("trO", 0, 256), True, True)
-    act(p, c("outG", 0, 256), c("b7", 0, 256), AF.Identity, bias=float(CEN))
-    dma(p, "yg", c("outG", 0, 256), 6)
-    h = NC // 2
-    ts(p, c("xo", 0, h), c("xs", 0, h), -128.0, OP.add)
-    dma(p, "yx", c("xo", 0, h), 7, 0, h)
-    act(p, c("xo", h, NC), c("xs", h, NC), AF.Identity, bias=-128.0)
-    dma(p, "yx", c("xo", h, NC), 8, h, NC)
+    act(p, c("outF", 0, 320), c("can", 0, 320), AF.Identity, bias=float(CEN), scale=Y)
+    dma(p, "sync", "yl", c("outF", 0, 320), 5)
+    group(p, old_trails(p, STEPS, CN, 0, 256))
+    act(p, c("outG", 0, 256), c(CN, 0, 256), AF.Identity, bias=float(CEN), scale=Y)
+    dma(p, "sync", "yg", c("outG", 0, 256), 6)
+    ts(p, c("xo", 0, XV), c("xs", 0, XV), -128.0, OP.add)
+    dma(p, "sync", "yx", c("xo", 0, XV), 7, 0, XV)
+    act(p, c("xo", XV, NC), c("xs", XV, NC), AF.Identity, bias=-128.0)
+    dma(p, "a", "yx", c("xo", XV, NC), 8, XV, NC)
 
 
-LONG = ("A0", "A1", "A2", "A3", "B0", "B1", "B2", "B3")
+def place(ops, seq, before, lag):
+    start, busy = {}, {}
+    for i in seq:
+        o = ops[i]
+        t = max([start[j] + ops[j]["cost"] + lag(j, i) for j in before[i]] or [0.0])
+        hold = 0.0 if o["q"] == "net" else 0.06 if o["dsem"] else o["cost"]
+        lst = busy.setdefault(o["q"], [])
+        lo, hi = 0, len(lst)
+        while lo < hi:
+            mid = (lo + hi) // 2
+            if lst[mid][1] <= t:
+                lo = mid + 1
+            else:
+                hi = mid
+        while lo < len(lst) and lst[lo][0] < t + hold - 1e-9:
+            t = max(t, lst[lo][1])
+            lo += 1
+        lst.insert(lo, (t, t + hold))
+        start[i] = t
+    return start, max(start[i] + ops[i]["cost"] for i in seq)
 
 
 def schedule(p):
     ops = p["ops"]
     n = len(ops)
+    pred = [list(o["deps"]) for o in ops]
     succ = [[] for _ in range(n)]
     for i in range(n):
-        for j in ops[i]["deps"]:
+        for j in pred[i]:
             succ[j].append(i)
-    tail = [0.0] * n
-    for i in range(n - 1, -1, -1):
-        tail[i] = ops[i]["cost"] + max([tail[k] + (0.0 if ops[k]["q"] == ops[i]["q"] else 0.06) for k in succ[i]] or [0.0])
-    left = [len(o["deps"]) for o in ops]
-    ready = [0.0] * n
-    pools = {"v": [], "a": [], "p": [], "g": [], "sync": [], "net": []}
-    free = {q: 0.0 for q in pools}
-    order = {q: [] for q in pools}
-    for i in range(n):
-        if left[i] == 0:
-            pools[ops[i]["q"]].append(i)
-    p["span"] = 0.0
-    for _ in range(n):
-        t0, q = min((max(free[q], min(ready[i] for i in pools[q])), q) for q in pools if pools[q])
-        cand = [i for i in pools[q] if ready[i] <= t0 + 1e-9]
-        if q == "v":
-            few = [k for k in cand if ops[k]["tag"] not in LONG]
-            i = max(few, key=lambda k: (tail[k], -k)) if few else min(cand)
-        elif q == "a":
-            few = [k for k in cand if ops[k]["cost"] < SMALL] or cand
-            i = max(few, key=lambda k: (tail[k], -k))
-        else:
-            i = max(cand, key=lambda k: (tail[k], -k))
-        pools[q].remove(i)
-        fin = t0 + ops[i]["cost"]
-        free[q] = t0 if q == "net" else t0 + 0.1 if q == "sync" else fin
-        p["span"] = max(p["span"], fin)
-        order[q].append(i)
-        for k in succ[i]:
-            ready[k] = max(ready[k], fin + (0.06 if ops[k]["q"] != q else 0.0 if q == "p" else 0.03))
-            left[k] -= 1
-            if left[k] == 0:
-                pools[ops[k]["q"]].append(k)
+
+    def lag(i, k):
+        return HOP if ops[k]["q"] != ops[i]["q"] else OWN if ops[max(i, k)]["deps"][min(i, k)] else 0.0
+    best, span = place(ops, range(n), pred, lag)
+    cur = best
+    for _ in range(PASSES):
+        back, _s = place(ops, sorted(range(n), key=lambda i: (-cur[i] - ops[i]["cost"], -i)), succ, lag)
+        cur, s = place(ops, sorted(range(n), key=lambda i: (-back[i] - ops[i]["cost"], i)), pred, lag)
+        if s < span:
+            best, span = cur, s
+    p["span"] = span
+    order = {q: [] for q in ("v", "a", "p", "g", "sync", "net")}
+    for i in sorted(range(n), key=lambda i: (best[i], i)):
+        ops[i]["t0"] = best[i]
+        order[ops[i]["q"]].append(i)
     p["order"] = order
     seq, ptr, out = [], {q: 0 for q in order}, set()
     while len(seq) < n:
@@ -570,7 +565,7 @@ _CACHE = {}
 
 def program():
     if "p" not in _CACHE:
-        p = {"ops": [], "acc": {}, "bank": {}}
+        p = {"ops": [], "acc": {}, "bank": {}, "nd": [0]}
         prologue(p)
         for t in range(STEPS):
             step(p, t)
@@ -595,6 +590,10 @@ def relay_of(topo, T, src, dst):
     return (same or cand)[0]
 
 
+def landing(T, t):
+    return T.zz[:, 512 * t + 512:512 * t + 768]
+
+
 def hand_on(g, core, T, topo):
     sent = 0
     for t in range(STEPS - 1):
@@ -603,7 +602,7 @@ def hand_on(g, core, T, topo):
             if core in topo.cores_of(src) and relay_of(topo, T, src, dst) == core:
                 g.wait_ge(T.sem["r%d" % t], len(topo.engines(src, core)))
                 rid, pid = topo.addr(dst, core)
-                g.remote_dma(T.zland[:, 256 * t:256 * t + 256], T.relay[:, 256 * t:256 * t + 256], T.sem["z%d" % t], T.sem.zl, pid, rid, topo.mask(core, dst))
+                g.remote_dma(landing(T, t), T.relay[:, 256 * t:256 * t + 256], T.sem["z%d" % t], T.sem.zl, pid, rid, topo.mask(core, dst))
                 sent += len(topo.engines(core, dst))
     if sent:
         g.wait_ge(T.sem.zl, sent)
@@ -618,20 +617,29 @@ def rank_program(g, core, T, topo):
     ops = p["ops"]
     queue = {"v": g.vector, "a": g.scalar, "p": g.tensor, "g": g, "sync": g.sync}
     known = {q: {} for q in queue}
-    clk, gpos, seen = {}, {}, {}
+    clk, gpos = {}, {}
     count = {"v": 0, "a": 0, "p": 0, "g": 0}
     sent = 0
+    arrive = {}
+    for t in range(STEPS - 1):
+        src = [k for k in T.cores if dest(T, T.rank_of(k), t) == core][0]
+        via = relay_of(topo, T, src, core)
+        arrive[t] = len(topo.engines(src if via is None else via, core))
     for i in p["emit"]:
         o = ops[i]
         q = o["q"]
         if q == "net":
+            clk[i] = {"z%d" % o["fn"][1]: arrive[o["fn"][1]]}
             continue
         kn, need = known[q], {}
         for j, w in o["deps"].items():
             oj = ops[j]
-            if oj["q"] == "net" or not w or isinstance(oj["fn"], tuple):
+            if not w or (isinstance(oj["fn"], tuple) and oj["q"] != "net"):
                 continue
-            s, v = (oj["dsem"], 16) if oj["dsem"] else (SEMOF[oj["q"]], gpos[j])
+            if oj["q"] == "net":
+                s, v = "z%d" % oj["fn"][1], arrive[oj["fn"][1]]
+            else:
+                s, v = (oj["dsem"], 16) if oj["dsem"] else (SEMOF[oj["q"]], gpos[j])
             if kn.get(s, 0) < v and need.get(s, (0, 0))[0] < v:
                 need[s] = (v, j)
         for s in list(need):
@@ -641,20 +649,13 @@ def rank_program(g, core, T, topo):
             queue[q].wait_ge(T.sem[s], v)
             for s2, v2 in clk[j].items():
                 kn[s2] = max(kn.get(s2, 0), v2)
-        t = o["ext"]
-        if t is not None and (q, t) not in seen:
-            seen[(q, t)] = True
-            for src in T.cores:
-                if dest(T, T.rank_of(src), t) == core:
-                    via = relay_of(topo, T, src, core)
-                    queue[q].wait_ge(T.sem["z%d" % t], len(topo.engines(src if via is None else via, core)))
         if isinstance(o["fn"], tuple):
             t = o["fn"][1]
             dst = dest(T, rank, t)
             via = relay_of(topo, T, core, dst)
             to = dst if via is None else via
             rid, pid = topo.addr(to, core)
-            g.remote_dma((T.zland if via is None else T.relay)[:, 256 * t:256 * t + 256], T.zn[:, 256 * t:256 * t + 256],
+            g.remote_dma(landing(T, t) if via is None else T.relay[:, 256 * t:256 * t + 256], T.zn[:, 256 * t:256 * t + 256],
                          T.sem[("z%d" if via is None else "r%d") % t], T.sem.zl, pid, rid, topo.mask(core, to))
             sent += len(topo.engines(core, to))
             continue

@@ -8,20 +8,34 @@ SA, SB = 0.97, -13.0 / 256
 C0 = SA + 6148 * SB
 RND = 1.5 * 2.0 ** 28
 STEEP = 400.0
-ROUTE = "VVSSVSSV"
-NH = 1
-ND = 3
-NET, PEC, GAT, SCA, CY, HOP, OWN, PASSES = 6.0, 0.0005, 1.5, 3.5, 0.001, 0.15, 0.1, 4
+ROUTE = "SVSSVVSV"
+DBANK = "40612020"
+BLOCKS = (0, 1, 2, 3, 4, 6, 5, 7)
+PERIOD = 18.38
+ZV = False
+OPENS, CLOSES = 0, 6
+DUE = """vB01:0.00 vB02:0.42 vB1:0.83 vB3:1.62 vB2:2.40 vk01:3.19 vB5:3.26 vtest1:4.04 vtree1:4.52 vB4:4.59 vPf1:23.75 vB7:5.80 vtree2:6.58 vB6:6.65 vtest2:7.43 vnf1:26.29
+vtest3:7.98 vtree3:8.46 vMw1:26.91 vk41:8.68 vIt1:8.75 vM1:27.20 vkm1:8.90 vcI2:9.12 vcI1:9.19 vcv1:9.41 vc161:9.48 vP21:10.09 vwcl1:28.71 vEQ1:10.40 vtest4:10.53 vscw1:11.06
+vcdl1:12.01 vscc1:12.23 vscc2:12.48 vscc3:12.74 vscc4:12.99 vscc5:13.25 vMu1:13.50 vscc6:13.57 vKW1:13.67 vscc7:14.09 vucl1:14.20 vfh1:14.27 vscc8:14.35 vblend1:14.45
+vscc9:14.70 vsc1:14.80 vsccan1:14.87 vuh1:15.82 vscc10:15.89 vhh1:15.99 vul1:16.06 vscc11:16.14 vK1:16.25 vscc12:16.67 vtrk2:16.82 vtrk3:16.88 vscc13:16.95 vtrk1:17.06
+vtrk4:17.13 vscc14:17.21 vhl1:17.32 vscc15:17.47 vGL1:17.57 vscc16:17.72 vKL1:17.85 vzr1:18.10 vKH1:18.25
+aA2:1.19 aFs1:21.10 aA3:2.83 aA4:4.36 aabs2:5.90 aabs1:6.43 aabs3:6.97 atest1:7.50 atest2:8.04 atest3:8.58 ansk1:9.13 axc1:9.68 axh1:10.26 aP11:10.56 aabs4:10.86 azn1:11.40
+atest4:11.70 an1:12.89 aAc1:13.85 asI1:15.07 aG121:16.33 aLOH2:17.32 aLOH1:17.67 aA1:-0.35
+psums1:0.20 ptable1:18.64 pblk2:1.39 psums2:1.90 pblk1:2.41 pblk4:2.92 psums3:3.46 psums4:3.52 pblk3:4.03 psums5:4.79 pblk5:4.86 psums6:5.58 pb72:24.47 pblk6:6.60 pxw1:7.11
+psums7:7.50 psums8:7.63 pblk7:8.15 pskip1:8.80 pzn1:8.93 pblk8:9.06 pxw2:9.63 pdd1:9.89 pcnt1:10.14 pcnt5:10.40 pcnt2:10.65 pzn2:10.91 pcnt4:11.04 pdup1:11.29 pcnt7:11.58
+pcnt6:11.84 pcnt3:12.09 pcnt8:12.43 plu1:12.69 pbA1:13.39 pU1:13.77 pb71:15.07 ppre2:16.96 ppre1:17.12 pturn1:17.40 pbE1:-0.72"""
+DUE = {k.split(":")[0]: float(k.split(":")[1]) for k in DUE.split()}
+NET, PEC, GAT, SCA, CY, HOP, OWN, PASSES = 6.0, 0.0005, 1.56, 3.8, 0.00092, 0.2, 0.15, 4
 
 BUFS = {
     "bfloat16": "xs 2816 xraw 2560 zraw 256 zz 4096 zn 1792 relay 1792 R 4096 AB 4096 SG 4096 E 4096 n 256 nsk 256 P1 256 P2 256 xc 256 xh 512 "
-                "EQ 128 G12 256 LOH 624 Fs 46 Pf 256 nf 16 sI 512 Ipm 256 W1 144 W4 144 W16 144 Ihalf 256 I256 256 Ic 128 Ik 128 BD 128 "
+                "EQ 128 G12 256 LOH 624 Fs 46 Pf 256 nf 32 sI 512 Ipm 256 W1 144 W4 144 W16 144 Ihalf 256 I256 256 Ic 128 Ik 128 BD 128 "
                 "one 256 T12 322 R2 312 Q 1024 xo 2560 hB 322 lB 322 t1 322 t2 322 t3 322 jB 184 gB 184",
-    "float16": "G16 512 K16 256 TRK 256 c16 32 Xs 512 S 2304 Yc 1024 Ih 128 Imh 128 Iy 128 Iu 128 It 256 ZW 144 cut16 256 uh 32 w16 32 hh 16 vh 16 ioH 144 fh 1",
-    "float32": "can 576 Ac 256 B2 256 k0 64 k1 64 k2 64 k3 64 k4 32 M 32 acc 1 sc 1 Lb 128 vc 1 pc 24 M16 16 M16n 16 DUMP 32 iL 18 sg 18 swt 18 THR 16 "
+    "float16": "G16 512 K16 256 KH 256 TRK 256 c16 32 Xs 512 S 2304 Yc 1024 Ih 128 Imh 128 Iy 128 Iu 128 It 256 ZW 144 cut16 256 uh 32 hh 16 vh 16 ioH 144 fh 1",
+    "float32": "can 576 zs 256 Ac 256 B2 256 k0 64 k1 64 k2 64 k3 64 k4 32 M 32 Mw 16 acc 1 sc 1 Lb 128 vc 1 pc 24 M16 16 M16n 16 DUMP 32 iL 18 sg 18 swt 18 THR 16 "
                "FH 16 tF 16 outF 320 outG 256",
     "int32": "canI 320 trI 256 cutI 256 km 16 cI 32 ioI 144 pI 1 qI 4 tI 16 fI 8",
-    "uint16": "GL 256 KL 256 cv 32 cdl 32 ul 32 hl 16 wcl 32",
+    "uint16": "GL 256 KL 256 cv 32 cdl 32 ul 32 hl 16 wcl 48",
 }
 SCRATCH = {"b%d" % i: ("psum", [128, 512], "float32") for i in range(8)}
 for _dt, _s in BUFS.items():
@@ -30,6 +44,7 @@ for _dt, _s in BUFS.items():
         SCRATCH[_l[_i]] = ("sbuf", [128, int(_l[_i + 1])], _dt)
 SEMAPHORES = ["sv", "sa", "sp", "sg", "zl"] + ["z%d" % t for t in range(7)] + ["r%d" % t for t in range(7)] + ["d%d" % i for i in range(10)]
 SC, CN, BL, XW, MI = "b3", "b4", "b5", "b6", "b7"
+ZB, DB = "b1", SC
 
 
 def col(i):
@@ -73,7 +88,9 @@ def add(p, q, fn, reads, writes, cost, dsem=None, tag=""):
                     keep.append(e)
             keep.append((i, lo, hi, st, wr))
             p["acc"][name] = keep
-    p["ops"].append({"q": q, "fn": fn, "deps": deps, "cost": cost, "dsem": dsem, "tag": tag or (writes[0][0] if writes else "")})
+    tag = tag or (writes[0][0] if writes else "")
+    p["nth"][q + tag] = p["nth"].get(q + tag, 0) + 1
+    p["ops"].append({"q": q, "fn": fn, "deps": deps, "cost": cost, "dsem": dsem, "tag": tag, "kind": q + tag + str(p["nth"][q + tag]), "step": p["step"]})
     return i
 
 
@@ -141,18 +158,32 @@ def act(p, out, in0, func, bias=None, scale=None, accum=None, offs=None, tag="")
     return add(p, "a", fn, [in0] + [s for s in (bias, scale, offs) if isinstance(s, tuple)], [out] + ([accum] if accum else []), 0.065 + width(out) * (GAT if offs else 1.0) * CY, tag=tag)
 
 
-def mm(p, out, lhsT, rhs, start, stop):
-    f = 1 if half(rhs) else 4
-    i = add(p, "p", lambda g, T: g.tensor.matmul(ap(T, out), ap(T, lhsT), ap(T, rhs), start, stop), [lhsT, rhs], [out], f * max(min(64, width(lhsT)), width(out)) * PEC)
-    if out[0] in p["bank"]:
-        p["ops"][i]["deps"].setdefault(p["bank"][out[0]], False)
-    p["bank"][out[0]] = i
-    return i
+def mms(p, calls, tag=""):
+    def fn(g, T):
+        for o, l, r, start, stop in calls:
+            ins = g.tensor.matmul(ap(T, o), ap(T, l), ap(T, r), start, stop)
+        return ins
+    cost = sum((1 if half(r) else 4) * max(min(64, width(l)), width(o)) * PEC for o, l, r, _a, _b in calls)
+    bank = calls[0][0][0]
+    i = add(p, "p", fn, [k[1] for k in calls] + [k[2] for k in calls], [k[0] for k in calls], cost, tag=tag)
+    if bank in p["bank"]:
+        p["ops"][i]["deps"].setdefault(p["bank"][bank], False)
+    p["bank"][bank] = i
 
 
-def group(p, terms):
-    for k, (o, l, r) in enumerate(terms):
-        mm(p, o, l, r, k == 0, k == len(terms) - 1)
+def flags(terms):
+    return [(o, l, r, k == 0, k == len(terms) - 1) for k, (o, l, r) in enumerate(terms)]
+
+
+def group(p, *runs, tag=""):
+    calls = flags([k for run in runs for k in run])
+    for run in runs:
+        mms(p, calls[:len(run)], tag)
+        calls = calls[len(run):]
+
+
+def groups(p, lst, tag=""):
+    mms(p, [k for terms in lst for k in flags(terms)], tag)
 
 
 def iota(p, out, pattern, base, chan):
@@ -217,7 +248,7 @@ def constants(p):
         ts(p, c("S", 144 * a, 144 * a + 144), io144, col(W0), OP.is_equal, c("M16", a, a + 1), OP.mult)
     ts(p, IB, io, col(P_), OP.is_equal)
     ts(p, c("W1", 0, 144), io144, col(W0), OP.is_equal)
-    for name, f in (("Ih", 1.0), ("Imh", -1.0), ("Iy", Y), ("Iu", 1 / Y)):
+    for name, f in (("Ih", 1.0), ("Iy", Y), ("Iu", 1 / Y)):
         ts(p, c(name, 0, 128), io, col(P_), OP.is_equal, f, OP.mult)
     for out, f in ((IM1, -1.0), (c("Ihalf", 0, 128), 0.5), (c("I256", 0, 128), 256.0), (c("I256", 128, 256), -164.0), (c("Ihalf", 128, 256), -0.5),
                    (c("Ic", 0, 128), float(CEN)), (c("Ik", 0, 128), CEN / Y)):
@@ -263,6 +294,8 @@ def constants(p):
     for s in range(8):
         ts(p, c("Yc", 128 * s, 128 * s + 128), io, c("FH", s, s + 1), OP.is_equal)
         ts(p, c("Q", 128 * s, 128 * s + 128), io, c("FH", 8 + s, 9 + s), OP.is_equal, 2 * Y, OP.mult)
+    yc = c("Yc", 0, 1024)
+    add(p, "g", lambda g, T: g.affine_select(ap(T, yc), ap(T, yc), [[0, 8], [1, 128]], OP.not_equal, -1.0, 0, -1), [yc], [yc], 0.17 + 2048 * CY)
 
 
 def slot(t):
@@ -281,32 +314,30 @@ def first_lanes(p, t):
     ts(p, c("uh", v, v + 16), wl, Y / 8, OP.mult, 1536 + CEN / 8 - 0.4375, OP.add)
     ts(p, c("hh", 0, 16), wl, Y / 112, OP.mult, 1536 + (CEN - 55.5) / 112, OP.add)
     ts(p, c("ul", v, v + 16), c("uh", v, v + 16), -1536.0, OP.add)
-    cp(p, c("w16", v, v + 16), wl)
     ts(p, c("hl", 0, 16), c("hh", 0, 16), col(C23), OP.add)
     act(p, c("G12", 0, 256), c("T12", 0, 322), AF.Copy, offs=c("ul", v, v + 16), tag="G12")
     for h in (0, 1):
-        mm(p, c(MI, 0, 312), c("G12", 128 * h, 128 * h + 128), c("R2", 0, 312), True, True)
-        act(p, c("LOH", 312 * h, 312 * h + 312), c(MI, 0, 312), AF.Relu, scale=c("swt", 16 + h, 17 + h), tag="LOH")
-    for k in range(4):
-        group(p, [((MI, 312, 358, 1, (32 * k, 32 * k + 32)), c("LOH", 312 * h + 32 * k, 312 * h + 32 * k + 32),
-                   c("LOH", 312 * h + 128 + 46 * k, 312 * h + 174 + 46 * k)) for h in (0, 1)])
+        pre = c((MI, XW)[h], 0, 312)
+        group(p, [(pre, c("G12", 128 * h, 128 * h + 128), c("R2", 0, 312))], tag="pre")
+        act(p, c("LOH", 312 * h, 312 * h + 312), pre, AF.Relu, scale=c("swt", 16 + h, 17 + h), tag="LOH")
+    groups(p, [[((MI, 312, 358, 1, (32 * k, 32 * k + 32)), c("LOH", 312 * h + 32 * k, 312 * h + 32 * k + 32),
+                 c("LOH", 312 * h + 128 + 46 * k, 312 * h + 174 + 46 * k)) for h in (0, 1)] for k in range(4)], tag="table")
     act(p, c("Fs", 0, 46), c(MI, 312, 358), AF.Copy)
     gtt(p, c("Pf", 0, 256), c("Fs", 0, 46), c("hl", 0, 16), c("G12", 0, 256), OP.mult, tag="Pf")
     group(p, [(c(MI, 358, 374), W("W1", r), c("Pf", r, 256, 16)) for r in range(16)])
-    tt(p, c("nf", 0, 16), c(MI, 358, 374), c("THR", 0, 16), OP.is_gt, tag="nf")
-
-
-def turn_terms(lo, k, n):
-    return [[(c(SC, lo + ql, lo + 2 * n, 2), X(ql, par), c("TRK", 128 * par + k, 128 * par + k + n)) for par in (0, 1)] for ql in (0, 1)]
+    tt(p, c("nf", v, v + 16), c(MI, 358, 374), c("THR", 0, 16), OP.is_gt, tag="nf")
+    tt(p, c("Mw", 0, 16), wl, c("nf", v, v + 16), OP.add)
+    tt(p, c("M", 0, 16), c("Mw", 0, 16), c("DUMP", 0, 16), OP.min)
+    ts(p, c("wcl", v, v + 16), c("M", 0, 16), Y, OP.mult, float(CEN), OP.add, tag="wcl")
 
 
 def canal_lists(p):
     gcp(p, c("K16", 0, 256), c("can", 0, NU), c("cv", 16, 32), tag="K")
-    for b in range(8):
-        vtr(p, c("TRK", b, 256, 8), c("K16", 32 * b, 32 * b + 32), tag="trk")
-    for terms in turn_terms(256, 0, 128):
-        group(p, terms)
+    for b in range(4):
+        vtr(p, c("TRK", b, 256, 4), c("K16", 64 * b, 64 * b + 64), tag="trk")
+    groups(p, [[(c(SC, 256 + 2 * b + ql, 512, 4), X(ql, par), c("TRK", 128 * b + 64 * par, 128 * b + 64 * par + 64)) for par in (0, 1)] for b in (0, 1) for ql in (0, 1)], tag="turn")
     ts(p, c("KL", 0, 256), c(SC, 256, 512), float(CEN), OP.add, tag="KL")
+    ts(p, c("KH", 0, 256), c("KL", 0, 256), -float(CEN), OP.add, tag="KH")
 
 
 def scores(p, t):
@@ -314,10 +345,13 @@ def scores(p, t):
     for j in range(4):
         for k in (0, 1):
             a = 1024 * j + 512 * k
-            i = gtt(p, c("E", a, a + 512), c("xs", 0, NC), c("KL", a // 16, a // 16 + 32), z, OP.max, tag="B")
+            if a == 0:
+                for b in (0, 256):
+                    gtt(p, c("E", b, b + 256), c("xs", 0, NC), c("KL", b // 16, b // 16 + 16), c("zz", 512 * t, 512 * t + 256), OP.max, tag="B0")
+            else:
+                gtt(p, c("E", a, a + 512), c("xs", 0, NC), c("KL", a // 16, a // 16 + 32), z, OP.max, tag="B")
         o = c(SC, 64 * j, 64 * j + 64)
-        turn = turn_terms(64 * j, 32 * j, 32)
-        group(p, [(o, c("Ic", 0, 128), c("one", 0, 64))] + turn[0] + turn[1] + [(o, W("W4", r), c("E", 1024 * j + r, 1024 * j + 1024, 16)) for r in range(16)])
+        group(p, [(o, c("Ic", 0, 128), c("one", 0, 64)), (o, IH, c("KH", 64 * j, 64 * j + 64))], [(o, W("W4", r), c("E", 1024 * j + r, 1024 * j + 1024, 16)) for r in range(16)], tag="sums")
         if j == 0:
             cp(p, c("k0", 0, 64), o)
         else:
@@ -338,36 +372,44 @@ def choice(p, t):
 
 
 def gauge(p, t):
-    act(p, c("xc", 0, 256), c("xs", 0, NC), AF.Copy, offs=c("cv", 0, 16), tag="xc")
+    xh = c("xh", 256 * (t & 1), 256 * (t & 1) + 256)
+    if t == STEPS - 1 or ZV:
+        act(p, xh, c("xs", 0, NC), AF.Identity, bias=63.75, scale=0.5, offs=c("cv", 0, 16), tag="xh")
+    else:
+        act(p, c("xc", 0, 256), c("xs", 0, NC), AF.Copy, offs=c("cv", 0, 16), tag="xc")
     if t < STEPS - 1:
-        zt, n = c("zn", 256 * t, 256 * t + 256), c(SC, 256, 512)
-        group(p, [(n, IB, c("zz", 512 * t, 512 * t + 256)), (n, IB, c("xc", 0, 256))])
+        zt, n = c("zn", 256 * t, 256 * t + 256), c(ZB, 256, 512)
+        if ZV:
+            n = c("zs", 0, 256)
+            gtt(p, n, c("xs", 0, NC), c("cv", 0, 16), c("zz", 512 * t, 512 * t + 256), OP.add, tag="zs")
+        else:
+            group(p, [(n, IB, c("zz", 512 * t, 512 * t + 256))], [(n, IB, c("xc", 0, 256))], tag="zn")
         act(p, zt, n, AF.Identity, bias=-0.25, scale=0.5, tag="zn")
         add(p, "g", ("send", t), [zt], [], 0.1)
         land = c("zz", 512 * t + 512, 512 * t + 768)
         add(p, "net", ("net", t), [zt], [land], NET)
         cp(p, c("zz", 512 * t + 768, 512 * t + 1024), land, tag="zr")
-    act(p, c("xh", 256 * (t & 1), 256 * (t & 1) + 256), c("xc", 0, 256), AF.Identity, bias=63.75, scale=0.5, tag="xh")
+        if not ZV:
+            act(p, xh, c("xc", 0, 256), AF.Identity, bias=63.75, scale=0.5, tag="xh")
 
 
 def cut_lists(p, t):
     c16 = c("c16", 16 * (t & 1), 16 * (t & 1) + 16)
-    for s in range(8):
-        o = c(MI, 16 * s, 16 * s + 16)
-        group(p, [(o, c("Yc", 128 * s, 128 * s + 128), c16), (o, IMH, c16)])
-    ts(p, c("EQ", 0, 128), c(MI, 0, 128), 0.0, OP.is_equal, tag="EQ")
-    o = c(MI, 128, 144)
-    group(p, [(o, c("Iy", 0, 128), c16)] + [(o, c("Q", 128 * s, 128 * s + 128), c("EQ", 16 * s, 16 * s + 16)) for s in range(8)])
+    groups(p, [[(c(DB, 16 * s, 16 * s + 16), c("Yc", 128 * s, 128 * s + 128), c16)] for s in range(8)], tag="dd")
+    o = c(DB, 128, 144)
+    ts(p, c("EQ", 0, 128), c(DB, 0, 128), 0.0, OP.is_equal, tag="EQ")
+    group(p, [(o, c("Iy", 0, 128), c16)] + [(o, c("Q", 128 * s, 128 * s + 128), c("EQ", 16 * s, 16 * s + 16)) for s in range(8)], tag="dup")
     ts(p, c("cdl", 0, 32, 2), o, float(CEN), OP.add, col(DC), OP.min, tag="cdl")
 
 
-def block(p, t, h, qd, k):
-    bank, s, a = "b%d" % (p["nd"][0] % ND), 256 * (t & 1), 2048 * h + 512 * qd
-    p["nd"][0] += 1
-    for kk in range(4):
-        e, o = 4 * qd + kk, c(bank, 128 * kk, 128 * kk + 128)
-        src = c("xh", 256 * (e & 1) + 128 * h, 256 * (e & 1) + 128 * h + 128) if e == t - 1 else c("R", 2048 * h + e, 2048 * h + 2048, 16)
-        group(p, [(o, c("sI", s, s + 128), src), (o, c("sI", s + 128, s + 256), c("zz", 512 * t + 128 * h, 512 * t + 128 * h + 128))])
+def block(p, t, j, kh, k):
+    bank, s, a = "b" + DBANK[k], 256 * (t & 1), 1024 * j + 512 * kh
+    lst = []
+    for kk in range(8):
+        e, o = 8 * kh + kk, c(bank, 64 * kk, 64 * kk + 64)
+        src = c("xh", 256 * (e & 1) + 64 * j, 256 * (e & 1) + 64 * j + 64) if e == t - 1 else c("R", 1024 * j + e, 1024 * j + 1024, 16)
+        lst.append([(o, c("sI", s, s + 128), src), (o, c("sI", s + 128, s + 256), c("zz", 512 * t + 64 * j, 512 * t + 64 * j + 64))])
+    groups(p, lst, tag="blk")
     d, sg, ab = c(bank, 0, 512), c("SG", a, a + 512), c("AB", a, a + 512)
     if ROUTE[k] == "V":
         ts(p, sg, d, RND, OP.add, RND, OP.not_equal, tag="test")
@@ -379,32 +421,33 @@ def block(p, t, h, qd, k):
             act(p, sg, ab, AF.Sigmoid, bias=-16 * STEEP, scale=STEEP, tag="test")
 
 
-def sg_of(h, e):
-    a = 2048 * h + 128 * e
-    return c("SG", a, a + 128)
+def sg_of(j, e):
+    a = 1024 * j + 64 * e
+    return c("SG", a, a + 64)
 
 
 def replay(p, t):
     e, v, nsk = slot(t), 16 * (t & 1), c("nsk", 0, 256)
-    for h in (0, 1):
-        mm(p, c(XW, 128 * h, 128 * h + 128), c("BD", 0, 128), sg_of(h, e), True, True)
-    act(p, nsk, c(XW, 0, 256), AF.Sigmoid, bias=8.5 * STEEP, scale=-STEEP, accum=c("acc", 0, 1) if t < STEPS - 1 else None, tag="nsk")
+    groups(p, [[(c(MI, 64 * j, 64 * j + 64), c("BD", 0, 128), sg_of(j, e))] for j in range(4)], tag="skip")
+    act(p, nsk, c(MI, 0, 256), AF.Sigmoid, bias=8.5 * STEEP, scale=-STEEP, accum=c("acc", 0, 1) if t < STEPS - 1 else None, tag="nsk")
     lo, hi, xw = c(XW, 0, 256), c(XW, 256, 512), c("R", e, 4096, 16)
-    group(p, [(hi, IB, xw), (hi, c("I256", 128, 256), nsk)])
+    group(p, [(hi, IB, xw), (lo, c("Ihalf", 128, 256), xw), (lo, c("Ihalf", 0, 128), c("zz", 512 * t, 512 * t + 256))],
+          [(hi, c("I256", 128, 256), nsk), (lo, c("I256", 0, 128), nsk)], tag="xw")
     ts(p, c("P2", 0, 256), hi, 4.0, OP.add, 191.0, OP.min, tag="P2")
-    group(p, [(lo, c("Ihalf", 128, 256), xw), (lo, c("Ihalf", 0, 128), c("zz", 512 * t, 512 * t + 256)), (lo, c("I256", 0, 128), nsk)])
     act(p, c("P1", 0, 256), lo, AF.Relu, bias=159.75 - 256, tag="P1")
-    lw, lu, nf = c(MI, 390, 406), c(MI, 406, 422), c("nf", 0, 16)
-    group(p, [(lw, IH, c("w16", v, v + 16)), (lw, IB, nf)])
-    group(p, [(lu, c("Iu", 0, 128), c("uh", v, v + 16)), (lu, IB, nf), (lu, c("Ik", 0, 128), c("one", 0, 16))] + [(lu, W("W16", r), c("nsk", r, 256, 16)) for r in range(16)])
-    tt(p, c("M", 0, 32), c(MI, 390, 422), c("DUMP", 0, 32), OP.min)
-    ts(p, c("wcl", 0, 32), c("M", 0, 32), Y, OP.mult, float(CEN), OP.add, tag="wcl")
-    if t < STEPS - 1:
-        u, s = c(MI, 422, 423), 256 * (1 - (t & 1))
-        group(p, [(u, c("Lb", 0, 128), c("vc", 0, 1)), (u, c("Lb", 0, 128), c("acc", 0, 1))])
-        ts(p, c("fh", 0, 1), u, 1 / (4 * SB), OP.mult, 1537 - 0.375 - C0 / (4 * SB), OP.add)
-        ts(p, c("sc", 0, 1), c("fh", 0, 1), -4 * SB, OP.mult, u, OP.add)
-        ts(p, c("sI", s, s + 256), c("Ipm", 0, 256), c("sc", 0, 1), OP.mult, tag="sI")
+    lu, nf = c(MI, 406, 422), c("nf", v, v + 16)
+    group(p, [(lu, c("Iu", 0, 128), c("uh", v, v + 16)), (lu, IB, nf), (lu, c("Ik", 0, 128), c("one", 0, 16))]
+          + [(lu, W("W16", r), c("nsk", r, 256, 16)) for r in range(16)], tag="lu")
+    tt(p, c("M", 16, 32), lu, c("DUMP", 16, 32), OP.min, tag="Mu")
+    ts(p, c("wcl", 32, 48), c("M", 16, 32), Y, OP.mult, float(CEN), OP.add, tag="ucl")
+
+
+def next_limit(p, t):
+    u, s = c(MI, 422, 423), 256 * (1 - (t & 1))
+    group(p, [(u, c("Lb", 0, 128), c("vc", 0, 1)), (u, c("Lb", 0, 128), c("acc", 0, 1))], tag="U")
+    ts(p, c("fh", 0, 1), u, 1 / (4 * SB), OP.mult, 1537 - 0.375 - C0 / (4 * SB), OP.add)
+    ts(p, c("sc", 0, 1), c("fh", 0, 1), -4 * SB, OP.mult, u, OP.add)
+    act(p, c("sI", s, s + 256), c("Ipm", 0, 256), AF.Copy, scale=c("sc", 0, 1), tag="sI")
 
 
 def old_trails(p, t, bank, lo, n):
@@ -415,16 +458,10 @@ def old_trails(p, t, bank, lo, n):
     return [(c(bank, lo, lo + n), c("It", it, it + 128), c("G16", g, g + n))] + [(c(bank, lo + r, lo + n, 16), Sel(r, t - 1), c("c16", v, v + n // 16)) for r in range(16)]
 
 
-def counts(p, t, h, order):
-    es = [4 * qd + kk for qd in order for kk in range(4)]
-    group(p, [(c(CN, 128 * h, 128 * h + 128), W("W1", e), sg_of(h, e)) for e in es])
-
-
-def blend(p, t, lo, w):
+def blend(p, t, lo, w, late):
     n, a, b, g = c("n", lo, lo + w), c(BL, lo, lo + w), c(BL, 256 + lo, 256 + lo + w), 256 * (1 - (t & 1)) + lo
     act(p, n, c(CN, lo, lo + w), AF.Sigmoid, bias=8.5 * STEEP, scale=-STEEP, tag="n")
-    group(p, old_trails(p, t, BL, lo, w) + [(a, IB, n)])
-    group(p, [(b, IH, c("K16", lo, lo + w)), (b, IM1, n)])
+    mms(p, [(a, IB, n, False, False), (b, IM1, n, False, late)], "bA")
     act(p, c("Ac", lo, lo + w), a, AF.Identity, bias=-1.0, tag="Ac")
     tt(p, c("G16", g, g + w), b, c("Ac", lo, lo + w), OP.max, tag="blend")
     if t < STEPS - 1:
@@ -437,30 +474,39 @@ def step(p, t):
         act(p, c("R", 1024 * j, 1024 * j + 1024), c("xs", 0, NC), AF.Copy, offs=c("GL", 64 * j, 64 * j + 64), tag="A")
     it = 128 * ((t + 1) & 1)
     ts(p, c("It", it, it + 128), IH, c("M16n", t, t + 1), OP.mult)
+    early = old_trails(p, t, BL, 0, 256) + [(c(BL, 256, 512), IH, c("K16", 0, 256))]
     scores(p, t)
-    q0 = slot(t) // 4
-    order = [q0] + [q for q in range(4) if q != q0]
-    block(p, t, 0, q0, 0)
-    block(p, t, 1, q0, 1)
-    replay(p, t)
+    order = (slot(t) // 8, 1 - slot(t) // 8)
+    lo = 0
+    for k in range(8):
+        j, kh = BLOCKS[k] // 2, order[BLOCKS[k] % 2]
+        block(p, t, j, kh, k)
+        if k == max(0, DBANK.rfind(BL[1])):
+            mms(p, [(o, l, r, i == 0, False) for i, (o, l, r) in enumerate(early)], "bE")
+        if BLOCKS[k] == 6:
+            replay(p, t)
+    runs = []
+    for k in (OPENS,) + tuple(k for k in range(8) if k not in (OPENS, CLOSES)) + (CLOSES,):
+        j, kh = BLOCKS[k] // 2, order[BLOCKS[k] % 2]
+        mms(p, [(c(CN, 64 * j, 64 * j + 64), W("W1", e), sg_of(j, e), k == OPENS and e % 8 == 0, k == CLOSES and e % 8 == 7) for e in range(8 * kh, 8 * kh + 8)], "cnt")
+        deps = p["ops"][-1]["deps"]
+        for i in runs[1:]:
+            deps.pop(i, None)
+        for i in runs if k == CLOSES else runs[:1]:
+            deps[i] = False
+        runs.append(len(p["ops"]) - 1)
+    blend(p, t, 0, 256, True)
     choice(p, t)
     gauge(p, t)
     cut_lists(p, t)
-    for h in (0, 1):
-        for k in (1, 2, 3):
-            block(p, t, h, order[k], 1 + 3 * h + k)
-        counts(p, t, h, order)
-        if NH == 2:
-            blend(p, t, 128 * h, 128)
-    if NH == 1:
-        blend(p, t, 0, 256)
     if t < STEPS - 1:
+        next_limit(p, t)
         first_lanes(p, t + 1)
-    scat2(p, c("xs", 0, NC + B), c("wcl", 0, 16), c("P1", 0, 256), c("P2", 0, 256), OP.add, tag="scw")
+    scat2(p, c("xs", 0, NC + B), c("wcl", v, v + 16), c("P1", 0, 256), c("P2", 0, 256), OP.add, tag="scw")
     for q in range(16):
         scat(p, c("xs", 0, NC + B), c("cdl", 2 * q, 2 * q + 1), c("xh", 256 * (t & 1) + 16 * q, 256 * (t & 1) + 16 * q + 16), tag="scc")
     gtt(p, c("B2", 0, 256), c("can", 0, NU), c("ul", v, v + 16), c("n", 0, 256), OP.subtract, tag="KW")
-    scat2(p, c("can", 0, NU + B), c("wcl", 16, 32), c("Ac", 0, 256), c("B2", 0, 256), OP.max, tag="sccan")
+    scat2(p, c("can", 0, NU + B), c("wcl", 32, 48), c("Ac", 0, 256), c("B2", 0, 256), OP.max, tag="sccan")
     if t < STEPS - 1:
         canal_lists(p)
 
@@ -537,14 +583,14 @@ def schedule(p):
 
     def lag(i, k):
         return HOP if ops[k]["q"] != ops[i]["q"] else OWN if ops[max(i, k)]["deps"][min(i, k)] else 0.0
-    best, span = place(ops, range(n), pred, lag)
-    cur = best
-    for _ in range(PASSES):
-        back, _s = place(ops, sorted(range(n), key=lambda i: (-cur[i] - ops[i]["cost"], -i)), succ, lag)
-        cur, s = place(ops, sorted(range(n), key=lambda i: (-back[i] - ops[i]["cost"], i)), pred, lag)
-        if s < span:
-            best, span = cur, s
-    p["span"] = span
+
+    key = [o["step"] * PERIOD + DUE.get(o["kind"], -PERIOD) if o["step"] >= 0 else PERIOD for o in ops]
+    for i in range(n - 1, -1, -1):
+        if ops[i]["step"] < 0:
+            key[i] = min([key[k] - ops[i]["cost"] - lag(i, k) for k in succ[i]] or [key[i]])
+    for i in range(n):
+        key[i] = max([key[i]] + [key[j] for j in pred[i]])
+    best, p["span"] = place(ops, sorted(range(n), key=lambda i: (key[i], i)), pred, lag)
     order = {q: [] for q in ("v", "a", "p", "g", "sync", "net")}
     for i in sorted(range(n), key=lambda i: (best[i], i)):
         ops[i]["t0"] = best[i]
@@ -565,9 +611,10 @@ _CACHE = {}
 
 def program():
     if "p" not in _CACHE:
-        p = {"ops": [], "acc": {}, "bank": {}, "nd": [0]}
+        p = {"ops": [], "acc": {}, "bank": {}, "nth": {}, "step": -1}
         prologue(p)
         for t in range(STEPS):
+            p["nth"], p["step"] = {}, t
             step(p, t)
         epilogue(p)
         schedule(p)

import math
from concourse.mybir import AluOpType as OP, ActivationFunctionType as AF

NC, NU, B, STEPS, CEN = 2560, 320, 256, 8, 1280
Y = 4096.0
LN = math.log(1.75)
SA, SB = 0.97, -13.0 / 256
C0 = SA + 6148 * SB
RND = 1.5 * 2.0 ** 28
STEEP = 400.0
ROUTE = "SVSSVVSV"
DBANK = "40612020"
BLOCKS = (0, 1, 2, 3, 4, 6, 5, 7)
PERIOD = 18.38
ZV = False
OPENS, CLOSES = 0, 6
DUE = """vB01:0.00 vB02:0.42 vB1:0.83 vB3:1.62 vB2:2.40 vk01:3.19 vB5:3.26 vtest1:4.04 vtree1:4.52 vB4:4.59 vPf1:23.75 vB7:5.80 vtree2:6.58 vB6:6.65 vtest2:7.43 vnf1:26.29
vtest3:7.98 vtree3:8.46 vMw1:26.91 vk41:8.68 vIt1:8.75 vM1:27.20 vkm1:8.90 vcI2:9.12 vcI1:9.19 vcv1:9.41 vc161:9.48 vP21:10.09 vwcl1:28.71 vEQ1:10.40 vtest4:10.53 vscw1:11.06
vcdl1:12.01 vscc1:12.23 vscc2:12.48 vscc3:12.74 vscc4:12.99 vscc5:13.25 vMu1:13.50 vscc6:13.57 vKW1:13.67 vscc7:14.09 vucl1:14.20 vfh1:14.27 vscc8:14.35 vblend1:14.45
vscc9:14.70 vsc1:14.80 vsccan1:14.87 vuh1:15.82 vscc10:15.89 vhh1:15.99 vul1:16.06 vscc11:16.14 vK1:16.25 vscc12:16.67 vtrk2:16.82 vtrk3:16.88 vscc13:16.95 vtrk1:17.06
vtrk4:17.13 vscc14:17.21 vhl1:17.32 vscc15:17.47 vGL1:17.57 vscc16:17.72 vKL1:17.85 vzr1:18.10 vKH1:18.25
aA2:1.19 aFs1:21.10 aA3:2.83 aA4:4.36 aabs2:5.90 aabs1:6.43 aabs3:6.97 atest1:7.50 atest2:8.04 atest3:8.58 ansk1:9.13 axc1:9.68 axh1:10.26 aP11:10.56 aabs4:10.86 azn1:11.40
atest4:11.70 an1:12.89 aAc1:13.85 asI1:15.07 aG121:16.33 aLOH2:17.32 aLOH1:17.67 aA1:-0.35
psums1:0.20 ptable1:18.64 pblk2:1.39 psums2:1.90 pblk1:2.41 pblk4:2.92 psums3:3.46 psums4:3.52 pblk3:4.03 psums5:4.79 pblk5:4.86 psums6:5.58 pb72:24.47 pblk6:6.60 pxw1:7.11
psums7:7.50 psums8:7.63 pblk7:8.15 pskip1:8.80 pzn1:8.93 pblk8:9.06 pxw2:9.63 pdd1:9.89 pcnt1:10.14 pcnt5:10.40 pcnt2:10.65 pzn2:10.91 pcnt4:11.04 pdup1:11.29 pcnt7:11.58
pcnt6:11.84 pcnt3:12.09 pcnt8:12.43 plu1:12.69 pbA1:13.39 pU1:13.77 pb71:15.07 ppre2:16.96 ppre1:17.12 pturn1:17.40 pbE1:-0.72"""
DUE = {k.split(":")[0]: float(k.split(":")[1]) for k in DUE.split()}
NET, PEC, GAT, SCA, CY, HOP, OWN, PASSES = 6.0, 0.0005, 1.56, 3.8, 0.00092, 0.2, 0.15, 4

BUFS = {
    "bfloat16": "xs 2816 xraw 2560 zraw 256 zz 4096 zn 1792 relay 1792 R 4096 AB 4096 SG 4096 E 4096 n 256 nsk 256 P1 256 P2 256 xc 256 xh 512 "
                "EQ 128 G12 256 LOH 624 Fs 46 Pf 256 nf 32 sI 512 Ipm 256 W1 144 W4 144 W16 144 Ihalf 256 I256 256 Ic 128 Ik 128 BD 128 "
                "one 256 T12 322 R2 312 Q 1024 xo 2560 hB 322 lB 322 t1 322 t2 322 t3 322 jB 184 gB 184",
    "float16": "G16 512 K16 256 KH 256 TRK 256 c16 32 Xs 512 S 2304 Yc 1024 Ih 128 Imh 128 Iy 128 Iu 128 It 256 ZW 144 cut16 256 uh 32 hh 16 vh 16 ioH 144 fh 1",
    "float32": "can 576 zs 256 Ac 256 B2 256 k0 64 k1 64 k2 64 k3 64 k4 32 M 32 Mw 16 acc 1 sc 1 Lb 128 vc 1 pc 24 M16 16 M16n 16 DUMP 32 iL 18 sg 18 swt 18 THR 16 "
               "FH 16 tF 16 outF 320 outG 256",
    "int32": "canI 320 trI 256 cutI 256 km 16 cI 32 ioI 144 pI 1 qI 4 tI 16 fI 8",
    "uint16": "GL 256 KL 256 cv 32 cdl 32 ul 32 hl 16 wcl 48",
}
SCRATCH = {"b%d" % i: ("psum", [128, 512], "float32") for i in range(8)}
for _dt, _s in BUFS.items():
    _l = _s.split()
    for _i in range(0, len(_l), 2):
        SCRATCH[_l[_i]] = ("sbuf", [128, int(_l[_i + 1])], _dt)
SEMAPHORES = ["sv", "sa", "sp", "sg", "zl"] + ["z%d" % t for t in range(7)] + ["r%d" % t for t in range(7)] + ["d%d" % i for i in range(10)]
SC, CN, BL, XW, MI = "b3", "b4", "b5", "b6", "b7"
ZB, DB = "b1", SC


def col(i):
    return ("pc", i, i + 1, 1)


def c(name, lo, hi, st=1):
    return (name, lo, hi, st)


def ap(T, a):
    t = T[a[0]]
    p0, p1 = a[4] if len(a) == 5 else (0, 128)
    return t[p0:p1, a[1]:a[2]:a[3]] if a[3] > 1 else t[p0:p1, a[1]:a[2]]


def width(a):
    return (a[2] - a[1] + a[3] - 1) // a[3]


def half(a):
    return SCRATCH[a[0]][2] in ("bfloat16", "float16", "uint16")


def add(p, q, fn, reads, writes, cost, dsem=None, tag=""):
    i = len(p["ops"])
    deps = {}
    for lst, wr in ((reads, False), (writes, True)):
        for a in lst:
            name, lo, hi, st = a[:4]
            psum = SCRATCH[name][0] == "psum"
            keep = []
            for e in p["acc"].setdefault(name, []):
                j, l2, h2, s2, w2 = e
                qj = p["ops"][j]["q"] if j < i else q
                apart = h2 <= lo or hi <= l2 or (st == s2 and (lo - l2) % st)
                conf = j < i and ((not apart and (wr or w2)) or (psum and qj != q))
                if conf:
                    deps[j] = deps.get(j, False) or qj != q or q != "p"
                if not (conf and wr and lo <= l2 and h2 <= hi and st in (1, s2) and (not psum or qj == q)):
                    keep.append(e)
            keep.append((i, lo, hi, st, wr))
            p["acc"][name] = keep
    tag = tag or (writes[0][0] if writes else "")
    p["nth"][q + tag] = p["nth"].get(q + tag, 0) + 1
    p["ops"].append({"q": q, "fn": fn, "deps": deps, "cost": cost, "dsem": dsem, "tag": tag, "kind": q + tag + str(p["nth"][q + tag]), "step": p["step"]})
    return i


def vcost(n):
    return 0.01 + max(64, n) * CY


def ts(p, out, in0, s1, op0, s2=None, op1=None, offs=None, tag=""):
    def fn(g, T):
        a1 = ap(T, s1) if isinstance(s1, tuple) else s1
        a2 = ap(T, s2) if isinstance(s2, tuple) else s2
        src = ap(T, in0) if offs is None else ap(T, in0).indirect(ap(T, offs))
        if op1 is None:
            return g.vector.tensor_scalar(ap(T, out), src, a1, None, op0)
        return g.vector.tensor_scalar(ap(T, out), src, a1, a2, op0, op1)
    f = 0.5 if half(out) and half(in0) else 1.0
    return add(p, "v", fn, [in0] + [s for s in (s1, s2, offs) if isinstance(s, tuple)], [out], vcost(width(out) * f), tag=tag)


def tt(p, out, in0, in1, op, tag=""):
    f = 1 if SCRATCH[in0[0]][0] == "psum" or SCRATCH[in1[0]][0] == "psum" else 2
    return add(p, "v", lambda g, T: g.vector.tensor_tensor(ap(T, out), ap(T, in0), ap(T, in1), op), [in0, in1], [out], vcost(width(out) * f), tag=tag)


def cp(p, out, in0, tag=""):
    f = 0.5 if half(out) and half(in0) else 1.0
    return add(p, "v", lambda g, T: g.vector.tensor_copy(ap(T, out), ap(T, in0)), [in0], [out], vcost(width(out) * f), tag=tag)


def memset(p, out, val):
    return add(p, "v", lambda g, T: g.vector.memset(ap(T, out), val), [], [out], vcost(width(out) * (0.5 if half(out) else 1)))


def gtt(p, out, win, offs, in1, op, tag=""):
    return add(p, "v", lambda g, T: g.vector.tensor_tensor(ap(T, out), ap(T, win).indirect(ap(T, offs)), ap(T, in1), op), [win, offs, in1], [out], 0.05 + width(out) * GAT * CY, tag=tag)


def gcp(p, out, win, offs, tag=""):
    return add(p, "v", lambda g, T: g.vector.tensor_copy(ap(T, out), ap(T, win).indirect(ap(T, offs))), [win, offs], [out], 0.05 + width(out) * GAT * CY, tag=tag)


def scat(p, win, offs, in0, tag=""):
    return add(p, "v", lambda g, T: g.vector.tensor_copy(ap(T, win).indirect(ap(T, offs)), ap(T, in0)), [offs, in0], [win], 0.05 + width(in0) * SCA * CY, tag=tag)


def scat2(p, win, offs, in0, in1, op, tag=""):
    return add(p, "v", lambda g, T: g.vector.tensor_tensor(ap(T, win).indirect(ap(T, offs)), ap(T, in0), ap(T, in1), op), [offs, in0, in1], [win], 0.05 + width(in0) * SCA * CY, tag=tag)


def vtr(p, out, in0, tag=""):
    return add(p, "v", lambda g, T: g.vector.transpose(ap(T, out), ap(T, in0)), [in0], [out], vcost(32), tag=tag)


def act(p, out, in0, func, bias=None, scale=None, accum=None, offs=None, tag=""):
    def fn(g, T):
        kw = {}
        if bias is not None:
            kw["bias"] = ap(T, bias) if isinstance(bias, tuple) else bias
        if scale is not None:
            kw["scale"] = ap(T, scale) if isinstance(scale, tuple) else scale
        if accum is not None:
            kw["accum_out"] = ap(T, accum)
        src = ap(T, in0) if offs is None else ap(T, in0).indirect(ap(T, offs))
        return g.scalar.activation(ap(T, out), src, func, **kw)
    return add(p, "a", fn, [in0] + [s for s in (bias, scale, offs) if isinstance(s, tuple)], [out] + ([accum] if accum else []), 0.065 + width(out) * (GAT if offs else 1.0) * CY, tag=tag)


def mms(p, calls, tag=""):
    def fn(g, T):
        for o, l, r, start, stop in calls:
            ins = g.tensor.matmul(ap(T, o), ap(T, l), ap(T, r), start, stop)
        return ins
    cost = sum((1 if half(r) else 4) * max(min(64, width(l)), width(o)) * PEC for o, l, r, _a, _b in calls)
    bank = calls[0][0][0]
    i = add(p, "p", fn, [k[1] for k in calls] + [k[2] for k in calls], [k[0] for k in calls], cost, tag=tag)
    if bank in p["bank"]:
        p["ops"][i]["deps"].setdefault(p["bank"][bank], False)
    p["bank"][bank] = i


def flags(terms):
    return [(o, l, r, k == 0, k == len(terms) - 1) for k, (o, l, r) in enumerate(terms)]


def group(p, *runs, tag=""):
    calls = flags([k for run in runs for k in run])
    for run in runs:
        mms(p, calls[:len(run)], tag)
        calls = calls[len(run):]


def groups(p, lst, tag=""):
    mms(p, [k for terms in lst for k in flags(terms)], tag)


def iota(p, out, pattern, base, chan):
    if SCRATCH[out[0]][2] == "int32":
        return add(p, "g", lambda g, T: g.iota(ap(T, out), pattern, base, chan), [], [out], 0.13 + width(out) * 2 * CY)
    return add(p, "g", lambda g, T: g.iota(ap(T, out), pattern, base, chan, allow_small_or_imprecise_dtypes=True), [], [out], 0.13 + width(out) * 2 * CY)


def dma(p, q, out, in0, k, lo=None, hi=None):
    def fn(g, T):
        o = ap(T, out) if isinstance(out, tuple) else T[out][:] if lo is None else T[out][:, lo:hi]
        i = ap(T, in0) if isinstance(in0, tuple) else T[in0][:] if lo is None else T[in0][:, lo:hi]
        return (g.sync if q == "sync" else g.scalar).dma_start(o, i)
    return add(p, q, fn, [a for a in (in0,) if isinstance(a, tuple)], [a for a in (out,) if isinstance(a, tuple)], 2.5 if lo is None else 3.2, dsem="d%d" % k)


P_, PM, PG, W0, G16C, PUP, PDN, MB0, MB1, C23, DC, PZ, LOW, F14, F1 = range(15)
IB, IM1, IH, IMH = c("Ipm", 0, 128), c("Ipm", 128, 256), c("Ih", 0, 128), c("Imh", 0, 128)


def W(name, r):
    return c(name, 15 - r, 143 - r)


def Sel(a, b):
    return c("S", 144 * a + 15 - b, 144 * a + 143 - b)


def X(s, d):
    return c("Xs", 128 * (2 * s + d), 128 * (2 * s + d) + 128)


def constants(p):
    iota(p, c("pI", 0, 1), [[1, 1]], 0, 1)
    iota(p, c("ioI", 0, 144), [[1, 144]], 0, 0)
    iota(p, c("tI", 0, 16), [[16, 16]], 0, 0)
    iota(p, c("hB", 0, 322), [[1, 23], [0, 14]], -11, 0)
    iota(p, c("lB", 0, 322), [[0, 23], [1, 14]], 0, 0)
    iota(p, c("jB", 0, 184), [[0, 8], [1, 23]], -11, 0)
    iota(p, c("gB", 0, 184), [[1, 8], [0, 23]], 0, 0)
    iota(p, c("fI", 0, 8), [[1, 8]], 1, 1)
    ts(p, c("qI", 0, 1), c("pI", 0, 1), 15, OP.bitwise_and)
    ts(p, c("qI", 1, 2), c("pI", 0, 1), 4, OP.logical_shift_right)
    ts(p, c("qI", 2, 3), c("pI", 0, 1), 4, OP.logical_shift_right, 1, OP.bitwise_and)
    cp(p, c("pc", PM, PG + 1), c("qI", 0, 2))
    cp(p, col(P_), c("pI", 0, 1))
    cp(p, c("ioH", 0, 144), c("ioI", 0, 144))
    io, io144 = c("ioH", 0, 128), c("ioH", 0, 144)
    ts(p, col(W0), c("qI", 1, 2), 16.0, OP.mult, 15.0, OP.add)
    ts(p, col(PZ), c("pI", 0, 1), 16.0, OP.mult, 15.0, OP.add)
    ts(p, c("ZW", 0, 144), io144, col(PZ), OP.is_equal)
    ts(p, col(PUP), c("pI", 0, 1), 16.0, OP.add)
    ts(p, col(PDN), c("pI", 0, 1), -16.0, OP.add)
    ts(p, col(MB1), c("qI", 2, 3), Y, OP.mult)
    ts(p, col(MB0), c("qI", 2, 3), -Y, OP.mult, Y, OP.add)
    for s in (0, 1):
        for d in (0, 1):
            ts(p, X(s, d), io, col((P_, PUP, PDN)[d - s]), OP.is_equal, col(MB1 if s else MB0), OP.mult)
    ts(p, c("M16", 0, 16), c("ioH", 0, 16), col(PM), OP.is_equal)
    ts(p, c("M16n", 0, 16), c("ioH", 0, 16), col(PM), OP.not_equal)
    for a in range(16):
        ts(p, c("S", 144 * a, 144 * a + 144), io144, col(W0), OP.is_equal, c("M16", a, a + 1), OP.mult)
    ts(p, IB, io, col(P_), OP.is_equal)
    ts(p, c("W1", 0, 144), io144, col(W0), OP.is_equal)
    for name, f in (("Ih", 1.0), ("Iy", Y), ("Iu", 1 / Y)):
        ts(p, c(name, 0, 128), io, col(P_), OP.is_equal, f, OP.mult)
    for out, f in ((IM1, -1.0), (c("Ihalf", 0, 128), 0.5), (c("I256", 0, 128), 256.0), (c("I256", 128, 256), -164.0), (c("Ihalf", 128, 256), -0.5),
                   (c("Ic", 0, 128), float(CEN)), (c("Ik", 0, 128), CEN / Y)):
        act(p, out, IB, AF.Copy, scale=f)
    act(p, c("W4", 0, 144), c("W1", 0, 144), AF.Copy, scale=-Y)
    act(p, c("W16", 0, 144), c("W1", 0, 144), AF.Copy, scale=-1.0 / 16)
    act(p, c("sI", 0, 256), c("Ipm", 0, 256), AF.Copy, scale=SA)
    memset(p, c("one", 0, 256), 1.0)
    memset(p, c("Lb", 0, 128), -SB / 16)
    memset(p, c("vc", 0, 1), C0 / (-8 * SB))
    group(p, [(c(XW, 0, 128), IB, W("W1", r)) for r in range(16)])
    act(p, c("BD", 0, 128), c(XW, 0, 128), AF.Copy)
    ts(p, col(LOW), col(PM), 14.0, OP.is_lt)
    ts(p, c("t1", 0, 322), c("lB", 0, 322), col(PM), OP.is_equal)
    act(p, c("t2", 0, 322), c("hB", 0, 322), AF.Copy, scale=c("M16", 14, 15))
    act(p, c("t3", 0, 322), c("hB", 0, 322), AF.Square, scale=c("M16", 15, 16))
    group(p, [(c(BL, 0, 322), IB, c(k, 0, 322)) for k in ("t1", "t2", "t3")])
    act(p, c("T12", 0, 322), c(BL, 0, 322), AF.Copy)
    act(p, c("R2", 0, 128), IB, AF.Copy, scale=col(LOW))
    ts(p, col(F14), c("M16", 14, 15), 2.0, OP.mult)
    ts(p, col(F1), col(LOW), c("M16", 15, 16), OP.subtract)
    act(p, c("t2", 0, 184), c("jB", 0, 184), AF.Identity, bias=col(F1), scale=col(F14))
    act(p, c("t3", 0, 184), c("jB", 0, 184), AF.Square, scale=col(LOW))
    group(p, [(c(BL, 0, 184), IB, c("t2", 0, 184)), (c(BL, 0, 184), IM1, c("t3", 0, 184))])
    ts(p, c("t1", 0, 184), c("gB", 0, 184), col(PG), OP.is_equal)
    tt(p, c("R2", 128, 312), c(BL, 0, 184), c("t1", 0, 184), OP.mult)
    ts(p, col(C23), c("qI", 2, 3), 23.0, OP.mult, -1536.0, OP.add)
    ts(p, col(DC), c("qI", 0, 1), float(NC), OP.add)
    ts(p, c("iL", 0, 16), c("tI", 0, 16), col(PM), OP.add)
    ts(p, c("iL", 16, 18), c("tI", 0, 16, 8), col(P_), OP.add)
    ts(p, c("DUMP", 0, 16), c("iL", 0, 16), float(NC - CEN), OP.add, 1 / Y, OP.mult)
    ts(p, c("DUMP", 16, 32), c("iL", 0, 16), float(NU - CEN), OP.add, 1 / Y, OP.mult)
    act(p, c("sg", 0, 18), c("iL", 0, 18), AF.Sigmoid, bias=-10.0, scale=-0.5 * LN)
    ts(p, c("swt", 0, 18), c("sg", 0, 18), math.exp(10 + 64 * LN), OP.mult)
    tt(p, c("tF", 0, 16), c("swt", 0, 16), c("swt", 0, 16), OP.mult)
    ts(p, c("THR", 0, 16), c("tF", 0, 16), 2.5, OP.mult)
    ts(p, c("fI", 0, 8), c("fI", 0, 8), 15, OP.bitwise_and)
    ts(p, c("FH", 0, 8), c("fI", 0, 8), col(W0), OP.add, -15.0, OP.add)
    ts(p, c("tF", 0, 8), c("ioH", 1, 9), col(PM), OP.is_gt)
    ts(p, c("tF", 8, 16), c("ioH", 1, 9), -1.0, OP.mult, 16.0, OP.add)
    tt(p, c("FH", 8, 16), c("tF", 0, 8), c("tF", 8, 16), OP.mult)
    ts(p, c("FH", 8, 16), c("FH", 8, 16), col(P_), OP.add)
    for s in range(8):
        ts(p, c("Yc", 128 * s, 128 * s + 128), io, c("FH", s, s + 1), OP.is_equal)
        ts(p, c("Q", 128 * s, 128 * s + 128), io, c("FH", 8 + s, 9 + s), OP.is_equal, 2 * Y, OP.mult)
    yc = c("Yc", 0, 1024)
    add(p, "g", lambda g, T: g.affine_select(ap(T, yc), ap(T, yc), [[0, 8], [1, 128]], OP.not_equal, -1.0, 0, -1), [yc], [yc], 0.17 + 2048 * CY)


def slot(t):
    return (t + 13) % 16


def w_terms(t, out):
    g = 256 * (t & 1)
    return [(out, Sel(slot(t), r), c("G16", g + r, g + 256, 16)) for r in range(16)]


def first_lanes(p, t):
    v = 16 * (t & 1)
    wl = c(MI, 374, 390)
    group(p, w_terms(t, wl))
    ts(p, c("uh", v, v + 16), wl, Y / 8, OP.mult, 1536 + CEN / 8 - 0.4375, OP.add)
    ts(p, c("hh", 0, 16), wl, Y / 112, OP.mult, 1536 + (CEN - 55.5) / 112, OP.add)
    ts(p, c("ul", v, v + 16), c("uh", v, v + 16), -1536.0, OP.add)
    ts(p, c("hl", 0, 16), c("hh", 0, 16), col(C23), OP.add)
    act(p, c("G12", 0, 256), c("T12", 0, 322), AF.Copy, offs=c("ul", v, v + 16), tag="G12")
    for h in (0, 1):
        pre = c((MI, XW)[h], 0, 312)
        group(p, [(pre, c("G12", 128 * h, 128 * h + 128), c("R2", 0, 312))], tag="pre")
        act(p, c("LOH", 312 * h, 312 * h + 312), pre, AF.Relu, scale=c("swt", 16 + h, 17 + h), tag="LOH")
    groups(p, [[((MI, 312, 358, 1, (32 * k, 32 * k + 32)), c("LOH", 312 * h + 32 * k, 312 * h + 32 * k + 32),
                 c("LOH", 312 * h + 128 + 46 * k, 312 * h + 174 + 46 * k)) for h in (0, 1)] for k in range(4)], tag="table")
    act(p, c("Fs", 0, 46), c(MI, 312, 358), AF.Copy)
    gtt(p, c("Pf", 0, 256), c("Fs", 0, 46), c("hl", 0, 16), c("G12", 0, 256), OP.mult, tag="Pf")
    group(p, [(c(MI, 358, 374), W("W1", r), c("Pf", r, 256, 16)) for r in range(16)])
    tt(p, c("nf", v, v + 16), c(MI, 358, 374), c("THR", 0, 16), OP.is_gt, tag="nf")
    tt(p, c("Mw", 0, 16), wl, c("nf", v, v + 16), OP.add)
    tt(p, c("M", 0, 16), c("Mw", 0, 16), c("DUMP", 0, 16), OP.min)
    ts(p, c("wcl", v, v + 16), c("M", 0, 16), Y, OP.mult, float(CEN), OP.add, tag="wcl")


def canal_lists(p):
    gcp(p, c("K16", 0, 256), c("can", 0, NU), c("cv", 16, 32), tag="K")
    for b in range(4):
        vtr(p, c("TRK", b, 256, 4), c("K16", 64 * b, 64 * b + 64), tag="trk")
    groups(p, [[(c(SC, 256 + 2 * b + ql, 512, 4), X(ql, par), c("TRK", 128 * b + 64 * par, 128 * b + 64 * par + 64)) for par in (0, 1)] for b in (0, 1) for ql in (0, 1)], tag="turn")
    ts(p, c("KL", 0, 256), c(SC, 256, 512), float(CEN), OP.add, tag="KL")
    ts(p, c("KH", 0, 256), c("KL", 0, 256), -float(CEN), OP.add, tag="KH")


def scores(p, t):
    z = c("zz", 512 * t, 512 * t + 512)
    for j in range(4):
        for k in (0, 1):
            a = 1024 * j + 512 * k
            if a == 0:
                for b in (0, 256):
                    gtt(p, c("E", b, b + 256), c("xs", 0, NC), c("KL", b // 16, b // 16 + 16), c("zz", 512 * t, 512 * t + 256), OP.max, tag="B0")
            else:
                gtt(p, c("E", a, a + 512), c("xs", 0, NC), c("KL", a // 16, a // 16 + 32), z, OP.max, tag="B")
        o = c(SC, 64 * j, 64 * j + 64)
        group(p, [(o, c("Ic", 0, 128), c("one", 0, 64)), (o, IH, c("KH", 64 * j, 64 * j + 64))], [(o, W("W4", r), c("E", 1024 * j + r, 1024 * j + 1024, 16)) for r in range(16)], tag="sums")
        if j == 0:
            cp(p, c("k0", 0, 64), o)
        else:
            tt(p, c("k%d" % j, 0, 64), o, c("k%d" % (j - 1), 0, 64), OP.min, tag="tree")


def choice(p, t):
    v = 16 * (t & 1)
    tt(p, c("k4", 0, 32), c("k3", 0, 32), c("k3", 32, 64), OP.min)
    tt(p, c("km", 0, 16), c("k4", 0, 16), c("k4", 16, 32), OP.min)
    ts(p, c("cI", 0, 16), c("km", 0, 16), 4095, OP.bitwise_and)
    if t < STEPS - 1:
        ts(p, c("cI", 16, 32), c("km", 0, 16), 3, OP.logical_shift_right, 511, OP.bitwise_and)
        cp(p, c("cv", 0, 32), c("cI", 0, 32), tag="cv")
    else:
        cp(p, c("cv", 0, 16), c("cI", 0, 16), tag="cv")
    ts(p, c("c16", v, v + 16), c("cI", 0, 16), -float(CEN), OP.add, 1 / Y, OP.mult)


def gauge(p, t):
    xh = c("xh", 256 * (t & 1), 256 * (t & 1) + 256)
    if t == STEPS - 1 or ZV:
        act(p, xh, c("xs", 0, NC), AF.Identity, bias=63.75, scale=0.5, offs=c("cv", 0, 16), tag="xh")
    else:
        act(p, c("xc", 0, 256), c("xs", 0, NC), AF.Copy, offs=c("cv", 0, 16), tag="xc")
    if t < STEPS - 1:
        zt, n = c("zn", 256 * t, 256 * t + 256), c(ZB, 256, 512)
        if ZV:
            n = c("zs", 0, 256)
            gtt(p, n, c("xs", 0, NC), c("cv", 0, 16), c("zz", 512 * t, 512 * t + 256), OP.add, tag="zs")
        else:
            group(p, [(n, IB, c("zz", 512 * t, 512 * t + 256))], [(n, IB, c("xc", 0, 256))], tag="zn")
        act(p, zt, n, AF.Identity, bias=-0.25, scale=0.5, tag="zn")
        add(p, "g", ("send", t), [zt], [], 0.1)
        land = c("zz", 512 * t + 512, 512 * t + 768)
        add(p, "net", ("net", t), [zt], [land], NET)
        cp(p, c("zz", 512 * t + 768, 512 * t + 1024), land, tag="zr")
        if not ZV:
            act(p, xh, c("xc", 0, 256), AF.Identity, bias=63.75, scale=0.5, tag="xh")


def cut_lists(p, t):
    c16 = c("c16", 16 * (t & 1), 16 * (t & 1) + 16)
    groups(p, [[(c(DB, 16 * s, 16 * s + 16), c("Yc", 128 * s, 128 * s + 128), c16)] for s in range(8)], tag="dd")
    o = c(DB, 128, 144)
    ts(p, c("EQ", 0, 128), c(DB, 0, 128), 0.0, OP.is_equal, tag="EQ")
    group(p, [(o, c("Iy", 0, 128), c16)] + [(o, c("Q", 128 * s, 128 * s + 128), c("EQ", 16 * s, 16 * s + 16)) for s in range(8)], tag="dup")
    ts(p, c("cdl", 0, 32, 2), o, float(CEN), OP.add, col(DC), OP.min, tag="cdl")


def block(p, t, j, kh, k):
    bank, s, a = "b" + DBANK[k], 256 * (t & 1), 1024 * j + 512 * kh
    lst = []
    for kk in range(8):
        e, o = 8 * kh + kk, c(bank, 64 * kk, 64 * kk + 64)
        src = c("xh", 256 * (e & 1) + 64 * j, 256 * (e & 1) + 64 * j + 64) if e == t - 1 else c("R", 1024 * j + e, 1024 * j + 1024, 16)
        lst.append([(o, c("sI", s, s + 128), src), (o, c("sI", s + 128, s + 256), c("zz", 512 * t + 64 * j, 512 * t + 64 * j + 64))])
    groups(p, lst, tag="blk")
    d, sg, ab = c(bank, 0, 512), c("SG", a, a + 512), c("AB", a, a + 512)
    if ROUTE[k] == "V":
        ts(p, sg, d, RND, OP.add, RND, OP.not_equal, tag="test")
    else:
        act(p, ab, d, AF.Abs, tag="abs")
        if ROUTE[k] == "M":
            ts(p, sg, ab, 16.0, OP.is_gt, tag="test")
        else:
            act(p, sg, ab, AF.Sigmoid, bias=-16 * STEEP, scale=STEEP, tag="test")


def sg_of(j, e):
    a = 1024 * j + 64 * e
    return c("SG", a, a + 64)


def replay(p, t):
    e, v, nsk = slot(t), 16 * (t & 1), c("nsk", 0, 256)
    groups(p, [[(c(MI, 64 * j, 64 * j + 64), c("BD", 0, 128), sg_of(j, e))] for j in range(4)], tag="skip")
    act(p, nsk, c(MI, 0, 256), AF.Sigmoid, bias=8.5 * STEEP, scale=-STEEP, accum=c("acc", 0, 1) if t < STEPS - 1 else None, tag="nsk")
    lo, hi, xw = c(XW, 0, 256), c(XW, 256, 512), c("R", e, 4096, 16)
    group(p, [(hi, IB, xw), (lo, c("Ihalf", 128, 256), xw), (lo, c("Ihalf", 0, 128), c("zz", 512 * t, 512 * t + 256))],
          [(hi, c("I256", 128, 256), nsk), (lo, c("I256", 0, 128), nsk)], tag="xw")
    ts(p, c("P2", 0, 256), hi, 4.0, OP.add, 191.0, OP.min, tag="P2")
    act(p, c("P1", 0, 256), lo, AF.Relu, bias=159.75 - 256, tag="P1")
    lu, nf = c(MI, 406, 422), c("nf", v, v + 16)
    group(p, [(lu, c("Iu", 0, 128), c("uh", v, v + 16)), (lu, IB, nf), (lu, c("Ik", 0, 128), c("one", 0, 16))]
          + [(lu, W("W16", r), c("nsk", r, 256, 16)) for r in range(16)], tag="lu")
    tt(p, c("M", 16, 32), lu, c("DUMP", 16, 32), OP.min, tag="Mu")
    ts(p, c("wcl", 32, 48), c("M", 16, 32), Y, OP.mult, float(CEN), OP.add, tag="ucl")


def next_limit(p, t):
    u, s = c(MI, 422, 423), 256 * (1 - (t & 1))
    group(p, [(u, c("Lb", 0, 128), c("vc", 0, 1)), (u, c("Lb", 0, 128), c("acc", 0, 1))], tag="U")
    ts(p, c("fh", 0, 1), u, 1 / (4 * SB), OP.mult, 1537 - 0.375 - C0 / (4 * SB), OP.add)
    ts(p, c("sc", 0, 1), c("fh", 0, 1), -4 * SB, OP.mult, u, OP.add)
    act(p, c("sI", s, s + 256), c("Ipm", 0, 256), AF.Copy, scale=c("sc", 0, 1), tag="sI")


def old_trails(p, t, bank, lo, n):
    g = 256 * (t & 1) + lo
    if t == 0:
        return [(c(bank, lo, lo + n), IH, c("G16", g, g + n))]
    v, it = 16 * ((t - 1) & 1) + lo // 16, 128 * (t & 1)
    return [(c(bank, lo, lo + n), c("It", it, it + 128), c("G16", g, g + n))] + [(c(bank, lo + r, lo + n, 16), Sel(r, t - 1), c("c16", v, v + n // 16)) for r in range(16)]


def blend(p, t, lo, w, late):
    n, a, b, g = c("n", lo, lo + w), c(BL, lo, lo + w), c(BL, 256 + lo, 256 + lo + w), 256 * (1 - (t & 1)) + lo
    act(p, n, c(CN, lo, lo + w), AF.Sigmoid, bias=8.5 * STEEP, scale=-STEEP, tag="n")
    mms(p, [(a, IB, n, False, False), (b, IM1, n, False, late)], "bA")
    act(p, c("Ac", lo, lo + w), a, AF.Identity, bias=-1.0, tag="Ac")
    tt(p, c("G16", g, g + w), b, c("Ac", lo, lo + w), OP.max, tag="blend")
    if t < STEPS - 1:
        ts(p, c("GL", lo, lo + w), c("G16", g, g + w), Y, OP.mult, float(CEN), OP.add, tag="GL")


def step(p, t):
    v = 16 * (t & 1)
    for j in range(4):
        act(p, c("R", 1024 * j, 1024 * j + 1024), c("xs", 0, NC), AF.Copy, offs=c("GL", 64 * j, 64 * j + 64), tag="A")
    it = 128 * ((t + 1) & 1)
    ts(p, c("It", it, it + 128), IH, c("M16n", t, t + 1), OP.mult)
    early = old_trails(p, t, BL, 0, 256) + [(c(BL, 256, 512), IH, c("K16", 0, 256))]
    scores(p, t)
    order = (slot(t) // 8, 1 - slot(t) // 8)
    lo = 0
    for k in range(8):
        j, kh = BLOCKS[k] // 2, order[BLOCKS[k] % 2]
        block(p, t, j, kh, k)
        if k == max(0, DBANK.rfind(BL[1])):
            mms(p, [(o, l, r, i == 0, False) for i, (o, l, r) in enumerate(early)], "bE")
        if BLOCKS[k] == 6:
            replay(p, t)
    runs = []
    for k in (OPENS,) + tuple(k for k in range(8) if k not in (OPENS, CLOSES)) + (CLOSES,):
        j, kh = BLOCKS[k] // 2, order[BLOCKS[k] % 2]
        mms(p, [(c(CN, 64 * j, 64 * j + 64), W("W1", e), sg_of(j, e), k == OPENS and e % 8 == 0, k == CLOSES and e % 8 == 7) for e in range(8 * kh, 8 * kh + 8)], "cnt")
        deps = p["ops"][-1]["deps"]
        for i in runs[1:]:
            deps.pop(i, None)
        for i in runs if k == CLOSES else runs[:1]:
            deps[i] = False
        runs.append(len(p["ops"]) - 1)
    blend(p, t, 0, 256, True)
    choice(p, t)
    gauge(p, t)
    cut_lists(p, t)
    if t < STEPS - 1:
        next_limit(p, t)
        first_lanes(p, t + 1)
    scat2(p, c("xs", 0, NC + B), c("wcl", v, v + 16), c("P1", 0, 256), c("P2", 0, 256), OP.add, tag="scw")
    for q in range(16):
        scat(p, c("xs", 0, NC + B), c("cdl", 2 * q, 2 * q + 1), c("xh", 256 * (t & 1) + 16 * q, 256 * (t & 1) + 16 * q + 16), tag="scc")
    gtt(p, c("B2", 0, 256), c("can", 0, NU), c("ul", v, v + 16), c("n", 0, 256), OP.subtract, tag="KW")
    scat2(p, c("can", 0, NU + B), c("wcl", 32, 48), c("Ac", 0, 256), c("B2", 0, 256), OP.max, tag="sccan")
    if t < STEPS - 1:
        canal_lists(p)


XV = 1536


def prologue(p):
    cut = (0, 8)
    dma(p, "sync", ("cutI", 0, 256, 1, cut), "cut", 2)
    dma(p, "a", c("trI", 0, 256), "trail", 0)
    dma(p, "sync", c("canI", 0, 320), "canal", 1)
    dma(p, "a", c("xraw", XV, NC), "x", 9, XV, NC)
    dma(p, "sync", c("xraw", 0, XV), "x", 4, 0, XV)
    dma(p, "a", c("zraw", 0, 256), "z", 3)
    constants(p)
    cp(p, c("GL", 0, 256), c("trI", 0, 256))
    ts(p, c("G16", 0, 256), c("GL", 0, 256), -float(CEN), OP.add, 1 / Y, OP.mult)
    ts(p, ("cut16", 0, 256, 1, cut), ("cutI", 0, 256, 1, cut), -float(CEN), OP.add)
    group(p, [(c(CN, 0, 16), ("ZW", 15 - r, 143 - r, 1, cut), ("cut16", r, 256, 16, cut)) for r in range(16)])
    ts(p, c("vh", 0, 16), c(CN, 0, 16), 0.125, OP.mult, 1536 + CEN / 8 - 0.4375, OP.add)
    ts(p, c("cv", 16, 32), c("vh", 0, 16), -1536.0, OP.add)
    ts(p, c("can", 0, 320), c("canI", 0, 320), -float(CEN), OP.add, 1 / Y, OP.mult)
    canal_lists(p)
    first_lanes(p, 0)
    for k in (0, 1):
        act(p, c("zz", 256 * k, 256 * k + 256), c("zraw", 0, 256), AF.Identity, bias=128.0)
    ts(p, c("xs", 0, XV), c("xraw", 0, XV), 128.0, OP.add)
    act(p, c("xs", XV, NC), c("xraw", XV, NC), AF.Identity, bias=128.0)


def epilogue(p):
    act(p, c("outF", 0, 320), c("can", 0, 320), AF.Identity, bias=float(CEN), scale=Y)
    dma(p, "sync", "yl", c("outF", 0, 320), 5)
    group(p, old_trails(p, STEPS, CN, 0, 256))
    act(p, c("outG", 0, 256), c(CN, 0, 256), AF.Identity, bias=float(CEN), scale=Y)
    dma(p, "sync", "yg", c("outG", 0, 256), 6)
    ts(p, c("xo", 0, XV), c("xs", 0, XV), -128.0, OP.add)
    dma(p, "sync", "yx", c("xo", 0, XV), 7, 0, XV)
    act(p, c("xo", XV, NC), c("xs", XV, NC), AF.Identity, bias=-128.0)
    dma(p, "a", "yx", c("xo", XV, NC), 8, XV, NC)


def place(ops, seq, before, lag):
    start, busy = {}, {}
    for i in seq:
        o = ops[i]
        t = max([start[j] + ops[j]["cost"] + lag(j, i) for j in before[i]] or [0.0])
        hold = 0.0 if o["q"] == "net" else 0.06 if o["dsem"] else o["cost"]
        lst = busy.setdefault(o["q"], [])
        lo, hi = 0, len(lst)
        while lo < hi:
            mid = (lo + hi) // 2
            if lst[mid][1] <= t:
                lo = mid + 1
            else:
                hi = mid
        while lo < len(lst) and lst[lo][0] < t + hold - 1e-9:
            t = max(t, lst[lo][1])
            lo += 1
        lst.insert(lo, (t, t + hold))
        start[i] = t
    return start, max(start[i] + ops[i]["cost"] for i in seq)


def schedule(p):
    ops = p["ops"]
    n = len(ops)
    pred = [list(o["deps"]) for o in ops]
    succ = [[] for _ in range(n)]
    for i in range(n):
        for j in pred[i]:
            succ[j].append(i)

    def lag(i, k):
        return HOP if ops[k]["q"] != ops[i]["q"] else OWN if ops[max(i, k)]["deps"][min(i, k)] else 0.0

    key = [o["step"] * PERIOD + DUE.get(o["kind"], -PERIOD) if o["step"] >= 0 else PERIOD for o in ops]
    for i in range(n - 1, -1, -1):
        if ops[i]["step"] < 0:
            key[i] = min([key[k] - ops[i]["cost"] - lag(i, k) for k in succ[i]] or [key[i]])
    for i in range(n):
        key[i] = max([key[i]] + [key[j] for j in pred[i]])
    best, p["span"] = place(ops, sorted(range(n), key=lambda i: (key[i], i)), pred, lag)
    order = {q: [] for q in ("v", "a", "p", "g", "sync", "net")}
    for i in sorted(range(n), key=lambda i: (best[i], i)):
        ops[i]["t0"] = best[i]
        order[ops[i]["q"]].append(i)
    p["order"] = order
    seq, ptr, out = [], {q: 0 for q in order}, set()
    while len(seq) < n:
        for q in order:
            while ptr[q] < len(order[q]) and all(j in out for j in ops[order[q][ptr[q]]]["deps"]):
                seq.append(order[q][ptr[q]])
                out.add(order[q][ptr[q]])
                ptr[q] += 1
    p["emit"] = seq


_CACHE = {}


def program():
    if "p" not in _CACHE:
        p = {"ops": [], "acc": {}, "bank": {}, "nth": {}, "step": -1}
        prologue(p)
        for t in range(STEPS):
            p["nth"], p["step"] = {}, t
            step(p, t)
        epilogue(p)
        schedule(p)
        _CACHE["p"] = p
    return _CACHE["p"]


SEMOF = {"v": "sv", "a": "sa", "p": "sp", "g": "sg"}


def dest(T, r, t):
    return T.cores[(r + 1 + t % 7) % len(T.cores)]


def relay_of(topo, T, src, dst):
    if topo.may_write(src, dst):
        return None
    cand = [k for k in topo.cores_of(src) if T.rank_of(k) is None and topo.may_write(k, dst)]
    same = [k for k in cand if topo.die(k) == topo.die(src)]
    return (same or cand)[0]


def landing(T, t):
    return T.zz[:, 512 * t + 512:512 * t + 768]


def hand_on(g, core, T, topo):
    sent = 0
    for t in range(STEPS - 1):
        for r in range(len(T.cores)):
            src, dst = T.cores[r], dest(T, r, t)
            if core in topo.cores_of(src) and relay_of(topo, T, src, dst) == core:
                g.wait_ge(T.sem["r%d" % t], len(topo.engines(src, core)))
                rid, pid = topo.addr(dst, core)
                g.remote_dma(landing(T, t), T.relay[:, 256 * t:256 * t + 256], T.sem["z%d" % t], T.sem.zl, pid, rid, topo.mask(core, dst))
                sent += len(topo.engines(core, dst))
    if sent:
        g.wait_ge(T.sem.zl, sent)


def rank_program(g, core, T, topo):
    rank = T.rank_of(core)
    if rank is None:
        hand_on(g, core, T, topo)
        return
    p = program()
    ops = p["ops"]
    queue = {"v": g.vector, "a": g.scalar, "p": g.tensor, "g": g, "sync": g.sync}
    known = {q: {} for q in queue}
    clk, gpos = {}, {}
    count = {"v": 0, "a": 0, "p": 0, "g": 0}
    sent = 0
    arrive = {}
    for t in range(STEPS - 1):
        src = [k for k in T.cores if dest(T, T.rank_of(k), t) == core][0]
        via = relay_of(topo, T, src, core)
        arrive[t] = len(topo.engines(src if via is None else via, core))
    for i in p["emit"]:
        o = ops[i]
        q = o["q"]
        if q == "net":
            clk[i] = {"z%d" % o["fn"][1]: arrive[o["fn"][1]]}
            continue
        kn, need = known[q], {}
        for j, w in o["deps"].items():
            oj = ops[j]
            if not w or (isinstance(oj["fn"], tuple) and oj["q"] != "net"):
                continue
            if oj["q"] == "net":
                s, v = "z%d" % oj["fn"][1], arrive[oj["fn"][1]]
            else:
                s, v = (oj["dsem"], 16) if oj["dsem"] else (SEMOF[oj["q"]], gpos[j])
            if kn.get(s, 0) < v and need.get(s, (0, 0))[0] < v:
                need[s] = (v, j)
        for s in list(need):
            if any(s2 != s and clk[need[s2][1]].get(s, 0) >= need[s][0] for s2 in need):
                del need[s]
        for s, (v, j) in need.items():
            queue[q].wait_ge(T.sem[s], v)
            for s2, v2 in clk[j].items():
                kn[s2] = max(kn.get(s2, 0), v2)
        if isinstance(o["fn"], tuple):
            t = o["fn"][1]
            dst = dest(T, rank, t)
            via = relay_of(topo, T, core, dst)
            to = dst if via is None else via
            rid, pid = topo.addr(to, core)
            g.remote_dma(landing(T, t) if via is None else T.relay[:, 256 * t:256 * t + 256], T.zn[:, 256 * t:256 * t + 256],
                         T.sem[("z%d" if via is None else "r%d") % t], T.sem.zl, pid, rid, topo.mask(core, to))
            sent += len(topo.engines(core, to))
            continue
        ins = o["fn"](g, T)
        clk[i] = dict(kn)
        if o["dsem"]:
            ins.then_inc(T.sem[o["dsem"]], 16)
            clk[i][o["dsem"]] = 16
        else:
            ins.then_inc(T.sem[SEMOF[q]], 1)
            count[q] += 1
            gpos[i] = clk[i][SEMOF[q]] = count[q]
    for q in count:
        g.wait_ge(T.sem[SEMOF[q]], count[q])
    for o in ops:
        if o["dsem"]:
            g.wait_ge(T.sem[o["dsem"]], 16)
    g.wait_ge(T.sem.zl, sent)
